import numpy as np, ml_dtypes
CORES = [48,51,52,55]
N = 4
BF = ml_dtypes.bfloat16
def gentries(a):
    return np.ascontiguousarray(a.reshape(8, 16, -1).transpose(0, 2, 1)).reshape(8, -1)
def gtable(e):
    e = np.asarray(e); return np.ascontiguousarray(e.reshape(8, -1, 16).transpose(0, 2, 1)).reshape(128, -1).astype(np.int32)
V, B, T, S, LH = 4096, 512, 256, 8, 2
M = V + T * S
def rows_of(rng, u):
    y = np.sort((u * (V - 15)).astype(np.int64), axis=-1) + np.arange(16)
    return rng.permuted(y, axis=-1)
def homes(rng, sb):
    he = rng.integers(0, B, (N, 8, V))
    for r in range(N):
        for g in range(8):
            o = rng.permutation(16 * B); he[r, g, sb[r, g].reshape(-1)[o]] = o >> 4
    return he
def parts(rng):
    sb = rows_of(rng, rng.random((N, 8, B, 16))); he = homes(rng, sb)
    x = rng.integers(0, 64, (N, 8, 16, V)); z = rng.integers(0, 64, (N, 8, 16, T))
    pe = (B * rng.random((N, 8, V)) ** 2).astype(np.int64); bx = (B * rng.random((N, 8, T)) ** 2).astype(np.int64)
    lim = np.stack([rng.integers(100, 450, (N, 8)), rng.integers(180, 320, (N, 8))], axis=-1)
    return x, sb, pe, he, bx, z, lim
def pack(x, sb, pe, he, bx, z, lim):
    w = lambda a: np.ascontiguousarray(a).astype(np.int32)
    return {"xs": x.reshape(N, 128, V).astype(np.float32).astype(BF), "sb": np.stack([gtable(a.reshape(8, -1)) for a in sb]), "pe": w(pe), "he": w(he),
            "bx": w(bx), "zs": z.reshape(N, 128, T).astype(np.float32).astype(BF), "lim": w(lim)}
def setup_inputs(rng):
    return pack(*parts(rng))
def setup_inputs_spread(rng):
    x, sb, pe, he, bx, z, lim = parts(rng)
    sb = rows_of(rng, rng.random((N, 8, B, 16)) ** rng.choice(np.array([1.0, 2.0, 4.0]), (N, 8, 1, 1))); he = homes(rng, sb)
    x = (64 * rng.random(x.shape) * np.exp2(-rng.integers(0, 6, (N, 8, 1, V)))).astype(np.int64)
    z = (64 * rng.random(z.shape) * np.exp2(-rng.integers(0, 6, (N, 8, 1, T)))).astype(np.int64)
    bx = (B * rng.random((N, 8, T)) ** rng.choice(np.array([1.0, 2.0, 4.0]), (N, 8, 1))).astype(np.int64)
    lim = np.minimum((np.exp2(10 * rng.random((N, 8, 2)))).astype(np.int64), 1023); lim[:, 0, 0] = 0; lim[:, 1, 0] = 1023; lim[:, 2, 1] = 0; lim[:, 3, 1] = 1023
    return pack(x, sb, pe, he, bx, z, lim)
def setup_inputs_ends(rng):
    base = np.concatenate([np.arange(8), np.arange(V - 8, V)])
    sb = rng.permuted(np.broadcast_to(base, (N, 8, B, 16)).copy(), axis=-1)
    pe = (B - 1) * rng.integers(0, 2, (N, 8, V)); he = (B - 1) * rng.integers(0, 2, (N, 8, V)); bx = (B - 1) * rng.integers(0, 2, (N, 8, T))
    m = rng.integers(0, 3, (N, 8, 1, V)); x = 63 * np.where(m == 2, rng.integers(0, 2, (N, 8, 16, V)), m)
    m = rng.integers(0, 3, (N, 8, 1, T)); z = 63 * np.where(m == 2, rng.integers(0, 2, (N, 8, 16, T)), m)
    x[:, 2][:, :, base] = 63; z[:, 2] = 63
    for g in (3, 7):
        x[:, g][:, :, base] = 0; z[:, g] = 63
    for g in (1, 5):
        x[:, g][:, :, base] = 63; x[:, g][:, :, V - 1] = 0; z[:, g] = 0; he[:, g][:, base] = B - 1
    he[:, 7][:, base] = B - 1
    for g in (4, 7):
        bx[:, g] = 0; bx[:, g, T - 1] = B - 1
    h = (np.arange(8)[None, :] + N - 1 - np.arange(N)[:, None]) & 7
    lim = 1023 * np.stack([h & 1, (h >> 1) & 1], axis=-1)
    return pack(x, sb, pe, he, bx, z, lim)
def setup_inputs_corners(rng):
    x, sb, pe, he, bx, z, lim = parts(rng)
    for r in range(N):
        for g in range(8):
            k = g & 3
            if k == 0:
                m = int(rng.integers(100, 400)); extra = (rng.random(V) < 0.85).astype(np.int64)
                x[r, g] = (m >> 4) + (np.argsort(rng.random((16, V)), axis=0) < (m & 15) + extra[None, :])
                z[r, g] = 0; lim[r, g] = (1000, m)
            elif k == 1:
                i, j = rng.permutation(16)[:2]; x[r, g] = 20; x[r, g, i] += rng.integers(0, 16, V); x[r, g, j] += rng.integers(0, 16, V)
                z[r, g] = 20; lim[r, g] = (int(rng.integers(4, 9)), 1023)
            elif k == 2:
                sec = np.concatenate([np.array([0, V - 1]), 1 + rng.permutation(V - 2)[:14]])
                sb[r, g] = rng.permuted(np.tile(sec, (B, 1)), axis=-1)
                for j in range(8):
                    sb[r, g, B - 1 - j] = np.concatenate([sec[2 * j:2 * j + 2], rng.permutation(np.delete(sec, [2 * j, 2 * j + 1]))])
                he[r, g, sec] = B - 1 - (np.arange(16) >> 1)
                if r % 2 == 0: he[r, g, sec[2:]] = np.arange(14)
                x[r, g][:, sec] = 31; bx[r, g] = rng.integers(0, B, T); o = rng.permutation(T)[:32]; bx[r, g, o] = B - 1 - (np.arange(32) & 7)
                lim[r, g] = (1023, 1023)
            else:
                pe[r, g] = np.where(rng.random(V) < 0.5, he[r, g], pe[r, g])
                x[r, g] = 63 * rng.integers(0, 2, (1, V)); z[r, g] = 63 * rng.integers(0, 2, (1, T))
                bx[r, g] = rng.choice(np.array([0, 1, B - 2, B - 1]), T)
                lim[r, g] = (int(rng.choice(np.array([1, 8, 1023]))), int(rng.choice(np.array([0, 1007, 1008, 1023]))))
    return pack(x, sb, pe, he, bx, z, lim)
def setup_inputs_crowd(rng):
    x, sb, pe, he, bx, z, lim = parts(rng)
    at = (0, B - 1, B >> 1, B - 1, 5, B - 2, 1, B - 1)
    for r in range(N):
        for g in range(8):
            a = at[g]; bx[r, g] = a
            if g != 6: z[r, g] = z[r, g, :, :1]
            if g == 2: bx[r, g, 0] = 0
            if g == 3: bx[r, g, T - 1] = 3
            if g in (4, 5):
                sb[r, g, a - 1] = rng.permutation(sb[r, g, a])
                if g == 4: bx[r, g, rng.permutation(T)[:T >> 1]] = a - 1
                else: bx[r, g, int(rng.integers(0, T))] = a - 1
            if g == 6: bx[r, g] = rng.integers(0, 4, T)
            if g == 7:
                x[r, g][:, sb[r, g, a]] = x[r, g][:, sb[r, g, a, :1]] & 3; z[r, g] = z[r, g] & 3
                far = rng.permutation(sb[r, g, a])[2 * S - 2:]; x[r, g][:, far] = rng.integers(40, 64, (16, far.size))
                pe[r, g, sb[r, g, a]] = a
            he[r, g, sb[r, g, a]] = a; lim[r, g, 0] = (300, 500, 700, 1000)[g & 3]
            if g != 0: lim[r, g, 1] = int(rng.integers(250, 500))
    return pack(x, sb, pe, he, bx, z, lim)
def setup_inputs_busy(rng):
    x, sb, pe, he, bx, z, lim = parts(rng); K = V >> 4; z = 0 * z + 8
    for g in range(8):
        H = rng.permutation(B)[:K]
        for r in range(N):
            o = rng.permutation(V); own = o.reshape(K, 16); he[r, g, o] = np.repeat(H, 16)
            nx = np.arange(K); nx[0:8:2] += 1; nx[1:8:2] -= 1
            if g & 1:
                src = np.concatenate([np.arange(1, 8, 2), np.arange(8, K)]); nx[src] = rng.permutation(nx[src])
            pe[r, g, o] = np.repeat(H[nx], 16)
            sb[r, g, H] = own; sb[r, g, H[1:8:2], 0] = own[0:8:2, 1]
            far = (np.arange(K) >= 16) & (rng.random(K) < 0.25)
            w = np.where(far, rng.integers(14, 51, K), 0); c = np.where(far, 3, rng.integers(0, 7, K)); c[:16] = 0
            x[r, g][:, o] = 8 + np.repeat(w, 16) * rng.integers(0, 2, (16, V)) + (rng.random((16, V)) * (np.repeat(c, 16) + 1)).astype(np.int64)
            first = np.arange(1, K)
            if S & 1: first = np.delete(first, 7)
            mid = np.concatenate([first, np.arange(16, K)])[:T - 2]
            bx[r, g] = H[np.concatenate([np.array([0]), rng.permutation(mid), np.array([8 if S & 1 else 0])])]
            lim[r, g] = (int(rng.integers(97, 130)), 300 if g == 5 else 1023)
    H = rng.permutation(B)[:K]
    for r in range(N):
        o = rng.permutation(V); own = o.reshape(K, 16); sb[r, 6, H] = own
        ex = np.concatenate([31 + rng.permutation(31), rng.permutation(31), np.arange(62, K)])
        ho = np.concatenate([np.arange(62), np.roll(np.arange(62, K), 1)])
        pe[r, 6, o] = np.repeat(H[ex], 16); he[r, 6, o] = np.repeat(H[ho], 16)
        x[r, 6] = rng.integers(0, 64, (16, V))
        x[r, 6][:, own[:31].reshape(-1)] = rng.integers(8, 10, (16, 31 * 16))
        x[r, 6][:, own[31:62].reshape(-1)] = rng.integers(40, 64, (16, 31 * 16))
        two = np.argsort(rng.random((31, 16)), axis=1)[:, :2]; b = 31 + np.arange(31)
        m = int(lim[r, 6, 0]) + 240 + rng.permutation(31) - 8
        x[r, 6][:, own[b, two[:, 0]]] = 8
        x[r, 6][:, own[b, two[:, 1]]] = 8 + (m >> 4) + (np.argsort(rng.random((16, 31)), axis=0) < (m & 15))
        i = rng.permutation(T); bx[r, 6, i[:31]] = H[:31]; bx[r, 6, i[31:]] = H[rng.integers(62, K, T - 31)]
        z[r, 6] = rng.integers(0, 64, (16, T)); z[r, 6][:, i[:31]] = 8
    return pack(x, sb, pe, he, bx, z, lim)
def check_inputs(d):
    bad = []
    for k, lo, hi in (("xs", 0, 63), ("sb", 0, V - 1), ("pe", 0, B - 1), ("he", 0, B - 1), ("bx", 0, B - 1), ("zs", 0, 63), ("lim", 0, 1023)):
        v = np.asarray(d[k]).astype(np.float64)
        if not (np.min(v) >= lo and np.max(v) <= hi): bad.append("range of " + k)
        elif np.any(v != np.floor(v)): bad.append("whole numbers in " + k)
    w = np.sort(np.stack([gentries(a) for a in np.asarray(d["sb"])]).reshape(N, 8, B, 16), axis=-1)
    if np.any(w[..., 1:] == w[..., :-1]): bad.append("16 different entries of every box in sb")
    return bad
def reference(xs, sb, pe, he, bx, zs, lim):
    X = np.zeros((N, 8, 16, M), np.int64); X[..., :V] = xs.astype(np.float32).astype(np.int64).reshape(N, 8, 16, V)
    rows = np.stack([gentries(a) for a in sb]).astype(np.int64).reshape(N, 8, B, 16)
    P = np.zeros((N, 8, M), np.int64); Q = np.zeros((N, 8, M), np.int64); P[..., :V] = pe; Q[..., :V] = he
    J = np.zeros((N, 8, V), np.int64) + np.arange(V); till = np.full((N, 8, M), -1, np.int64)
    b = bx.astype(np.int64); z = zs.astype(np.float32).astype(np.int64).reshape(N, 8, 16, T); back = np.zeros((N, 8, T), np.int64)
    L = lim.astype(np.int64); A = np.zeros((N, 8), np.int64); BIG = 2 ** 20
    for t in range(S):
        for q in range(N):
            o = (q - t) % N
            for g in range(8):
                act = np.flatnonzero(back[o, g] <= t)
                if act.size == 0: continue
                x = X[q, g]; a = b[o, g, act]; zz = z[o, g][:, act]
                s = rows[q, g][a]; c = J[q, g][s]
                void = (c >= V) & (Q[q, g][s] == a[:, None]); held = till[q, g][c] >= t; free = ~void & ~held
                D = np.add.reduce(np.abs(x[:, c] - zz[:, :, None]), axis=0)
                key = np.where(free, D * 16 + np.arange(16), BIG); two = np.argsort(key, axis=1, kind="stable")[:, :2]
                kk = np.take_along_axis(key, two, 1); ef = np.take_along_axis(c, two, 1); e = ef[:, 0]; f = ef[:, 1]
                some = kk[:, 0] < BIG; pair = kk[:, 1] < BIG; xe = x[:, e]; xf = x[:, f]
                claim = np.flatnonzero(some); tk = claim[np.unique(e[claim], return_index=True)[1]]
                wait = some.copy(); wait[tk] = False
                ms = np.unique(a, return_index=True)[1]
                split = ~some | ((kk[:, 0] >> 4) > L[q, g, 1])
                apart = np.add.reduce(np.abs(xe - xf), axis=0)
                join = pair & ~split & (e < V) & (f < V) & (Q[q, g][e] == a) & (Q[q, g][f] == a) & (apart < L[q, g, 0] + 8 * (A[q, g] & 31))
                sp = ms[split[ms]]; jo = ms[join[ms]]; et = e[tk]; i = act[tk]
                b[o, g, i] = np.where(a[tk] == P[q, g][et], Q[q, g][et], P[q, g][et])
                stay = np.where(et >= V, LH, 1); till[q, g, et] = t + stay; back[o, g, i] = t + stay + 1
                back_s = s[sp][void[sp] & ~held[sp]]; J[q, g, back_s] = back_s
                n = V + T * t + act[jo]; J[q, g, e[jo]] = n; J[q, g, f[jo]] = n
                P[q, g, n] = P[q, g][e[jo]]; Q[q, g, n] = P[q, g][f[jo]]; A[q, g] += jo.size
                x[:, n] = np.maximum(xe, xf)[:, jo]; x[:, et] = zz[:, tk]
                z[o, g][:, i] = (zz[:, tk] + xe[:, tk]) >> 1
                z[o, g][:, act[wait]] = np.abs(zz - xe)[:, wait]
    return {"yj": J.astype(np.float32), "yx": X.reshape(N, 128, M).astype(np.float32).astype(BF), "yb": b.astype(np.float32), "yz": z.reshape(N, 128, T).astype(np.float32).astype(BF)}

@@ -1,0 +1,675 @@
+import numpy as np
+from concourse.mybir import AluOpType as A, ActivationFunctionType as F
+
+S = 8
+MW = 304
+NA = 2
+f32, bf, i32, u16 = "float32", "bfloat16", "int32", "uint16"
+SCRATCH = {
+    "X": ("sbuf", [128, 8464], bf), "PQ": ("sbuf", [128, 8464], bf),
+    "BITS": ("sbuf", [128, 8704], bf), "GB": ("sbuf", [128, 8208], bf), "DD": ("sbuf", [128, 4096], bf),
+    "AD": ("sbuf", [128, 4096], bf), "G1": ("sbuf", [128, 4096], bf), "IOS": ("sbuf", [128, 2560], f32),
+    "TS": ("sbuf", [128, 2560], f32), "TT": ("sbuf", [128, 4096], f32), "SBI": ("sbuf", [128, 1024], i32), "SBU": ("sbuf", [128, 512], u16),
+    "BD": ("sbuf", [128, 2048], bf), "BB": ("sbuf", [128, 256], bf), "BE": ("sbuf", [128, 2048], bf), "BC": ("sbuf", [128, 256], bf),
+    "VR": ("sbuf", [128, 768], f32), "V2": ("sbuf", [128, 1536], bf),
+    "MSG": ("sbuf", [128, MW * (S + 1)], bf), "OUT": ("sbuf", [128, MW * S], bf),
+    "RR": ("sbuf", [128, 1280], f32), "TR": ("sbuf", [128, 512], f32),
+    "W": ("sbuf", [128, 272 * 14], f32), "WI": ("sbuf", [128, 1024], i32), "WB": ("sbuf", [128, 256 * 12], bf),
+    "ZZ": ("sbuf", [128, 1024], bf), "SM": ("sbuf", [128, 16 * 72], f32), "SI": ("sbuf", [128, 16 * 8], i32),
+    "SH": ("sbuf", [128, 16], bf), "L": ("sbuf", [128, 16 * 64], u16), "LB": ("sbuf", [128, 256 * 4], u16),
+    "MAT": ("sbuf", [128, 144 * 7 + 128 * 9 + 288], bf), "T5": ("sbuf", [128, 512 * 4], f32), "IF": ("sbuf", [128, 256], f32),
+    "NI": ("sbuf", [128, 512], i32), "NF": ("sbuf", [128, 256 * 5], f32), "NB": ("sbuf", [128, 256 * 7], bf),
+    "BXI": ("sbuf", [128, 32], i32), "BXF": ("sbuf", [128, 64], f32), "LI": ("sbuf", [128, 4], i32), "LF": ("sbuf", [128, 4], f32),
+    "E8": ("sbuf", [128, 256], f32), "LUT": ("sbuf", [128, 272], f32), "JK": ("sbuf", [128, 2192], bf), "RB": ("sbuf", [128, 1024], bf),
+    "RST": ("sbuf", [128, 256], f32), "QR": ("sbuf", [128, 512], f32),
+}
+for _b in range(8):
+    SCRATCH["P%d" % _b] = ("psum", [128, 512], f32)
+NDMA = 48
+SEMAPHORES = ["ev", "ea", "ep", "eg", "sent"] + [nm + str(t) for t in range(1, S + 1) for nm in ("arr", "box")] + ["d%d" % k for k in range(NDMA)]
+GRAM = ((15, 14), (13, 12, 3, 0), (11, 10, 8), (9, 7, 6, 5), (4, 2, 1))
+SIZE = {f32: 4, bf: 2, i32: 4, u16: 2}
+GATHER, SCATTER, TENSOR, SYNC, WIRE = 1.56, 3.8, 0.5, 60, 2460
+ALL = (1 << 128) - 1
+EARLY = 9000
+PEEK, SEED, TRIES, MOVES = 130, 1, 3000, (150, 400, 1000, 2500, 6000)
+SETTINGS = ((0, 0, 1, 60, 0.4), (-0.46, -1.6, 1, 40, 0.24), (0.44, 1.7, 1, 80, 0.17), (0, 0, 2, 140, 0.16))
+PLAN = {}
+
+
+def rank_program(g, core, T, topo):
+    rank = T.rank_of(core)
+    if rank is None:
+        return
+    nxt = T.cores[(rank + 1) % len(T.cores)]
+    rid, pid, _ = topo.addr(nxt)
+    emask = topo.mask(core, nxt)
+    nen = len(topo.engines(core, nxt))
+    ops = []
+    ndma = [0]
+
+    def a(name, lo, hi, step=1, ps=None):
+        return (name, lo, hi, step, ps)
+
+    def ind(win, off):
+        return ("ind", win, off)
+
+    def ap(x):
+        if not isinstance(x, tuple):
+            return x
+        if x[0] == "ind":
+            return ap(x[1]).indirect(ap(x[2]))
+        ps = slice(None) if x[4] is None else slice(*x[4])
+        return T[x[0]][ps, x[1]:x[2]:x[3]] if x[3] != 1 else T[x[0]][ps, x[1]:x[2]]
+
+    def regs(xs):
+        r = []
+        for x in xs:
+            if isinstance(x, tuple):
+                r += regs([x[1], x[2]]) if x[0] == "ind" else [(x[0], x[1], x[2], ALL if x[4] is None else sum(1 << p for p in range(*x[4])))]
+        return r
+
+    def wid(x):
+        return 16 * wid(x[2]) if x[0] == "ind" else len(range(x[1], x[2], x[3]))
+
+    def op(eng, fn, out, ins, cost):
+        if isinstance(out, tuple) and out[0] == "ind":
+            w_, r_ = regs([out[1]]), regs(list(ins) + [out[2]])
+        else:
+            w_, r_ = regs([out]), regs(ins)
+        ops.append({"e": eng, "f": [fn], "w": w_, "r": r_, "dma": None, "c": cost, "lat": SYNC})
+        if isinstance(out, tuple) and out[0] == "ind": ops[-1]["s"] = wid(out)
+        elif ins and isinstance(ins[0], tuple) and ins[0][0] == "ind": ops[-1]["g"] = wid(out)
+
+    def vc(o, i, k=1.0):
+        if o[0] == "ind": return 60 + wid(o) * SCATTER
+        if i[0] == "ind": return 60 + wid(o) * GATHER
+        if SIZE[SCRATCH[o[0]][2]] == 2 and SIZE[SCRATCH[i[0]][2]] == 2: k *= 0.5
+        return max(64, wid(o) * k)
+
+    def ps(x): return x[0] != "ind" and SCRATCH[x[0]][0] == "psum"
+    def cp(o, i): op("v", lambda: g.vector.tensor_copy(ap(o), ap(i)), o, [i], vc(o, i))
+    def tt(o, x, y, f): op("v", lambda: g.vector.tensor_tensor(ap(o), ap(x), ap(y), f), o, [x, y], vc(o, x, 1.0 if ps(x) or ps(y) else 2.0))
+    def ts(o, x, s1, f0, s2=None, f1=None):
+        if f1 is None: op("v", lambda: g.vector.tensor_scalar(ap(o), ap(x), ap(s1), None, f0), o, [x, s1], vc(o, x))
+        else: op("v", lambda: g.vector.tensor_scalar(ap(o), ap(x), ap(s1), ap(s2), f0, f1), o, [x, s1, s2], vc(o, x))
+    def scan(o, d0, d1, f0, f1): op("v", lambda: g.vector.tensor_tensor_scan(ap(o), ap(d0), ap(d1), 0.0, f0, f1), o, [d0, d1], vc(o, d1))
+    def tp(o, i): op("v", lambda: g.vector.transpose(ap(o), ap(i)), o, [i], vc(o, i))
+    def ms(o, c): op("v", lambda: g.vector.memset(ap(o), c), o, [], vc(o, o))
+    def act(o, i, fn=F.Identity, bias=0.0, scale=1.0, acc=None):
+        c = 78 + wid(o) * GATHER if i[0] == "ind" else max(64, wid(o))
+        if acc is None: op("a", lambda: g.scalar.activation(ap(o), ap(i), fn, bias=ap(bias), scale=ap(scale)), o, [i, bias, scale], c)
+        else: op("a", lambda: g.scalar.activation(ap(o), ap(i), fn, bias=ap(bias), scale=ap(scale), accum_out=ap(acc)), acc, [i, bias, scale], c + 24)
+        if acc is not None: ops[-1]["w"] += regs([o])
+    def mms(items):
+        fs = [(lambda o, l, r, st, sp: lambda: g.tensor.matmul(ap(o), ap(l), ap(r), st, sp))(*x) for x in items]
+        ops.append({"e": "p", "f": fs, "w": regs([x[0] for x in items]), "r": list(set(regs([x[1] for x in items] + [x[2] for x in items]))), "dma": None,
+                    "c": sum(TENSOR * max(64, wid(x[2])) * (4 if SCRATCH[x[1][0]][2] == f32 else 1) for x in items), "lat": SYNC})
+    def acc(o, pairs): return [(o, l, r, k == 0, k == len(pairs) - 1) for k, (l, r) in enumerate(pairs)]
+    def iota(o, pat, base, cm):
+        if SCRATCH[o[0]][2] != i32: op("g", lambda: g.iota(ap(o), pat, base, cm, allow_small_or_imprecise_dtypes=True), o, [], 160 + 2 * wid(o))
+        else: op("g", lambda: g.iota(ap(o), pat, base, cm), o, [], 160 + 2 * wid(o))
+    def dma(q, o, i, kb):
+        eng = {"s": g.sync, "a": g.scalar}[q]
+        op(q, lambda: eng.dma_start(ap(o), ap(i)), o, [i], 60)
+        ops[-1]["dma"] = "d%d" % ndma[0]; ops[-1]["lat"] = 2400 + 5 * kb
+        ndma[0] += 1
+    def arrival(t, after):
+        for nm, lo, hi, j in (("arr", 0, 272, after[1]), ("box", 272, MW, after[0])):
+            ops.append({"e": "x", "f": [], "w": [("MSG", MW * t + lo, MW * t + hi, ALL)], "r": [], "dma": nm + str(t), "c": 0, "lat": 0, "after": j})
+    def send(t, nm, lo, hi):
+        src, dst, sem = a("OUT", MW * t + lo, MW * t + hi), a("MSG", MW * (t + 1) + lo, MW * (t + 1) + hi), T.sem[nm + str(t + 1)]
+        op("g", lambda: g.remote_dma(ap(dst), ap(src), sem, T.sem.sent, pid, rid, emask), None, [src], 600)
+        ops[-1]["dma"] = "remote"; ops[-1]["lat"] = WIRE
+        return len(ops) - 1
+
+    at = {"SM": 0, "L": 0}
+    def slot(buf, name, n):
+        if (buf, name) not in at:
+            at[(buf, name)] = at[buf]; at[buf] += n
+        return a(buf, at[(buf, name)], at[(buf, name)] + n)
+    def sm(name, n=16): return slot("SM", name, n)
+    def col(name): return slot("SM", name, 1)
+    def li(name, n=16): return slot("L", name, n)
+    def sub(x, lo, hi, step=1): return a(x[0], x[1] + lo, x[1] + hi, step)
+    def w(k, n=256): return a("W", 272 * k, 272 * k + n)
+    def wb(k): return a("WB", 256 * k, 256 * k + 256)
+    def si(k, n=16): return a("SI", 16 * k, 16 * k + n)
+    def YM(k): return a("MAT", 144 * k, 144 * k + 144)
+    def Y(k, r): return a("MAT", 144 * k + 15 - r, 144 * k + 143 - r)
+    def MT(k): return a("MAT", 1008 + 128 * k, 1136 + 128 * k)
+    KC = a("MAT", 2160, 2416); TRI = a("MAT", 2416, 2432); CK = a("MAT", 2432, 2448)
+    I128, BLK, NEG, ME, MF = MT(4), MT(5), MT(6), MT(7), MT(8)
+    def io5(lo, hi): return a("TS", 512 + lo, 512 + hi)
+    def nf(k): return a("NF", 256 * k, 256 * k + 256)
+    def nb(k): return a("NB", 256 * k, 256 * k + 256)
+    def t5(k): return a("T5", 512 * k, 512 * k + 512)
+    def grp(name, f, n): return a(name, 0, n, 1, (f, 128, 16))
+    def wsel(out, k, src, lo, n, first=()):
+        mms(acc(out, list(first) + [(Y(k, r), a(src, lo + r, lo + n, 16)) for r in range(16)]))
+
+    for h in range(2):
+        dma("a", a("BXI", 16 * h, 16 * h + 16), T.bx[:], 8)
+    dma("s", a("SBI", 0, 512), T.sb[:], 256)
+    for b in range(8):
+        dma("s" if b & 1 else "a", a("SBI", 512, 1024, 1, (16 * b, 16 * b + 16)), T.sb[16 * (b ^ 1):16 * (b ^ 1) + 16, :], 32)
+    dma("s", a("NI", 256, 512), T.he[:], 128)
+    dma("s", a("X", 0, 4096), T.xs[:], 1024)
+    dma("a", a("MSG", 0, 256), T.zs[:], 64)
+    dma("s", a("NI", 0, 256), T.pe[:], 128)
+    dma("a", a("LI", 0, 2, 1, (0, 8)), T.lim[:], 1)
+    iota(si(0, 1), [[0, 1]], 0, 1)
+    iota(io5(0, 512), [[1, 512]], 0, 0)
+    iota(a("QR", 0, 256), [[1, 16], [0, 16]], 0, 0)
+    iota(a("QR", 256, 512), [[0, 16], [1, 16]], 0, 0)
+    iota(a("E8", 0, 128, 1, (0, 8)), [[1, 128]], 0, -16)
+    iota(a("IOS", 0, 1024), [[1, 64], [256, 16]], 0, 0)
+    for c in range(2):
+        iota(a("BE", 1024 * c, 1024 * c + 1024), [[0, 1024]], 0, 0)
+    for nm in ("X", "PQ"):
+        for c in range(4):
+            iota(a(nm, 4096 + 1092 * c, 5188 + 1092 * c), [[0, 1092]], 0, 0)
+    iota(io5(512, 1536), [[0, 1024]], 0, 0)
+    iota(a("VR", 0, 768), [[0, 768]], 0, 0)
+    pf, pm, p16, pj, par = col("pf"), col("pm"), col("p16"), col("pj"), col("par")
+    nc = [0]
+    def tmp():
+        nc[0] += 1
+        return col("tmp%d" % nc[0])
+    def bit(m):
+        nc[0] += 1
+        x = a("SI", 16 + nc[0] % 16, 17 + nc[0] % 16)
+        ts(x, si(0, 1), m, A.bitwise_and)
+        return x
+    def c_(x, s1, f0, s2=None, f1=None):
+        o = tmp(); ts(o, x, s1, f0, s2, f1); return o
+    cp(pf, si(0, 1))
+    for o, m in ((pm, 15), (p16, 112), (pj, 7), (par, 16)):
+        cp(o, bit(m))
+    ms(col("m192"), -192.0); ms(col("p128"), 128.0)
+    i16 = io5(0, 16)
+    ts(YM(0), io5(0, 144), c_(p16, 15.0, A.add), A.is_equal)
+    ts(I128, io5(0, 128), pf, A.is_equal)
+    for c in range(2):
+        for h in range(2):
+            ts(MT(2 * c + h), io5(0, 128), c_(pf, 16.0 * (h - c), A.add), A.is_equal, c_(par, 16.0 * c, A.is_equal), A.mult)
+    ts(sub(CK, 0, 16, 2), io5(0, 8), 0.0, A.mult, c_(par, 128.0, A.mult), A.add)
+    ts(sub(CK, 1, 16, 2), sub(CK, 0, 16, 2), -1.0, A.mult, 2048.0, A.add)
+    par1 = c_(par, 1.0 / 16, A.mult)
+    def flip(o):
+        tp(a("BXF", 32, 64), a("BXF", 0, 32))
+        tt(o, a("BXF", 48, 64), a("BXF", 32, 48), A.subtract); ts(o, o, par1, A.mult); tt(o, o, a("BXF", 32, 48), A.add)
+    cp(a("BXF", 0, 32), a("BXI", 0, 32)); flip(sm("b0"))
+    cp(a("MSG", 272, 288), sm("b0")); tt(a("MSG", 288, 304), sm("b0"), a("MSG", 272, 288), A.subtract)
+    ms(a("MSG", 256, 272), 0.0)
+    cp(t5(3), a("SBI", 0, 512)); act(a("TS", 0, 512), t5(3), scale=1.0 / 512)
+    ts(a("TS", 2048, 2560), a("SBI", 512, 1024), 1.0 / 512, A.mult)
+    iW, i256, d512, d8k = sm("iW"), sm("i256"), sm("d512"), sm("d8k")
+    ts(iW, i16, 16.0, A.mult, pm, A.add)
+    ts(li("reo"), i16, c_(pm, 16.0, A.mult), A.add)
+    ts(li("exp"), i16, 16.0, A.mult, 15.0, A.add)
+    ts(li("bd"), i16, 128.0, A.mult, pf, A.add)
+    act(d512, iW, bias=512.0); act(d8k, iW, bias=8208.0); act(i256, iW, bias=256.0); act(sm("d4k"), iW, bias=4096.0)
+    qk, rk = a("QR", 0, 256), a("QR", 256, 512)
+    act(KC, qk, scale=1.0 / 16)
+    act(NEG, I128, scale=-1.0)
+    act(a("IF", 0, 128), I128, scale=512.0); act(a("IF", 128, 256), I128, scale=-512.0)
+    RST = a("RST", 0, 256)
+    act(RST, rk, F.Relu, scale=-65536.0, bias=65536.0)
+    ts(TRI, i16, pm, A.is_ge, -64.0, A.mult)
+    ms(a("BD", 0, 2048), 0.0)
+    for o in (a("PQ", 0, 2048), a("PQ", 2048, 4096)):
+        dma("s", o, a("BD", 0, 2048), 512)
+    ms(sub(w(0, 272), 256, 272), 0.0); ms(sub(w(6, 272), 0, 8), 0.0)
+    pw = None
+    for b in range(4):
+        x = c_(c_(bit(1 << b), 0.0, A.is_gt, 2.0 ** -(1 << b) - 1.0, A.mult), 1.0, A.add)
+        pw = x if pw is None else c_(x, pw, A.mult)
+    lo9 = c_(pm, 9.0, A.is_lt)
+    for (n, mul, dst, msk) in ((512, 1.0, a("WB", 0, 512), lo9), (32, 512.0, sm("hb", 32), c_(pm, 14.0, A.is_lt, lo9, A.subtract))):
+        tm = a("T5", 512, 512 + n); ti = a("WI", 512, 512 + n)
+        act(tm, io5(0, n), scale=mul, bias=0.5)
+        ts(ti, tm, pw, A.mult, -0.5, A.add)
+        ts(ti, ti, 1, A.bitwise_and)
+        ts(dst, ti, c_(msk, 2.0, A.mult), A.mult, msk, A.subtract)
+    for h in range(17):
+        o, bcol = a("BITS", 512 * h, 512 * h + 512), sub(sm("hb", 32), h, h + 1)
+        if h in BITS_ON_SCALAR: act(o, a("WB", 0, 512), bias=bcol)
+        else: ts(o, a("WB", 0, 512), bcol, A.add)
+    cp(a("LB", 512, 768), a("NI", 256, 512))
+    for k in range(2):
+        x = a("P7", 256 * k, 256 * k + 256)
+        cp(x, a("NI", 256 * k, 256 * k + 256)); cp(nb(2 * k), a("NI", 256 * k, 256 * k + 256)); tt(nb(2 * k + 1), x, nb(2 * k), A.subtract)
+    he = a("P7", 256, 512)
+    for f in range(4):
+        dma("s", grp("PQ", f, 4096), nb(f), 64)
+    p8 = None
+    for b in range(3):
+        x = c_(c_(bit(1 << b), 0.0, A.is_gt, 8.0 ** (1 << b) - 1.0, A.mult), 1.0, A.add)
+        p8 = x if p8 is None else c_(x, p8, A.mult)
+    r8 = tmp(); op("v", lambda: g.vector.reciprocal(ap(r8), ap(p8)), r8, [p8], 240)
+    m01 = c_(pm, 2.0, A.is_lt); m23 = c_(pm, 4.0, A.is_lt, m01, A.subtract)
+    w5 = c_(c_(pm, 4.0, A.is_equal, 1.0 / 1024, A.mult), c_(pm, 6.0, A.is_equal), A.add)
+    for k, wt in ((1, c_(pm, 1.0, A.add)), (2, r8), (3, m01), (4, c_(pm, 6.0, A.is_lt, m01, A.subtract)), (5, w5), (6, m23)):
+        act(YM(k), YM(0), scale=wt)
+    act(ME, I128, scale=m01); ts(MF, io5(0, 128), c_(pf, 2.0, A.add), A.is_equal, m01, A.mult)
+    ts(a("T5", 1024, 1152), io5(0, 128), p16, A.subtract, 0.0, A.is_ge)
+    ts(a("T5", 1152, 1280), io5(0, 128), p16, A.subtract, 16.0, A.is_lt)
+    tt(BLK, a("T5", 1024, 1152), a("T5", 1152, 1280), A.mult)
+    e8 = a("E8", 0, 128, 1, (0, 8)); e9 = a("E8", 128, 256, 1, (0, 8))
+    ts(e9, e8, 0.0, A.is_ge); ts(e8, e8, 16.0, A.is_lt); tt(e8, e8, e9, A.mult)
+    cp(a("LF", 0, 2, 1, (0, 8)), a("LI", 0, 2, 1, (0, 8)))
+    mms(acc(a("P3", 128, 130), [(e8, a("LF", 0, 2, 1, (0, 8)))]))
+    thr = sm("thr", 32)
+    cp(col("lim0"), a("P3", 128, 129)); cp(col("jl"), a("P3", 128, 129)); ts(col("sl"), a("P3", 129, 130), 1.0, A.add)
+    ts(sub(thr, 0, 16), i16, 0.0, A.mult, col("sl"), A.add); ms(sub(thr, 16, 32), 1009.0)
+    ms(col("A"), 0.0); act(col("nl0"), col("lim0"), scale=-1.0)
+    j7 = c_(pj, 7.0, A.is_equal)
+    for t in range(S):
+        act(col("cd%d" % t), j7, scale=-8.0 if 4 <= t + 1 < 8 else 0.0, bias=(t + 1 if t < 7 else 0) + (256 * t + 1) * 2.0 ** -21)
+    short = c_(j7, 4.0, A.mult, -3.5, A.add)
+    for h in range(2):
+        ts(col("vs%d" % h), pm, 8.0, A.is_ge if h else A.is_lt, p8, A.mult); tt(col("vb%d" % h), col("vs%d" % h), short, A.mult)
+    act(a("V2", 1024, 1536), io5(0, 512), scale=0.0, bias=col("vb0"))
+    ts(a("P6", 0, 256), qk, pm, A.is_equal); ts(a("T5", 1280, 1536), rk, pm, A.is_equal)
+    tt(a("LUT", 0, 256), a("P6", 0, 256), a("T5", 1280, 1536), A.max)
+    ms(a("LUT", 256, 264), 0.0); ms(a("LUT", 264, 265), 1020.0); ms(a("LUT", 265, 272), -1.0)
+
+    cp(a("SBU", 0, 512), a("SBI", 0, 512))
+    for c in range(4):
+        win = a("IOS", 512 + 512 * c, 1024 + 512 * c) if c else t5(3)
+        if c: act(win, t5(3), bias=-64.0 * c)
+        tt(a("G1", 1024 * c, 1024 * c + 1024), ind(win, a("LB", 512 + 64 * c, 576 + 64 * c)), a("IOS", 0, 1024), A.is_equal)
+        wsel(a("P4", 64 * c, 64 * c + 64), 1, "G1", 1024 * c, 1024)
+        wsel(a("P4", 256 + 64 * c, 320 + 64 * c), 2, "G1", 1024 * c, 1024)
+    kh, sc = a("P4", 0, 256), a("P4", 256, 512)
+    ts(nb(4), kh, 0.0, A.is_equal, 1024.0, A.mult); ts(nb(5), kh, 9.0, A.is_ge, 512.0, A.mult); cp(nb(6), sc)
+    for f in range(4, 7):
+        dma("s", grp("PQ", f, 4096), nb(f), 64)
+    act(nf(0), kh, scale=512.0, bias=-512.0); tt(nf(0), he, nf(0), A.add)
+    act(a("P6", 256, 512), nb(4), scale=8.0); tt(nf(0), a("P6", 256, 512), nf(0), A.max)
+    cp(a("LB", 768, 1024), nf(0))
+    ms(a("GB", 8192, 8208), 0.0)
+
+    def tables():
+        for c in range(8):
+            o, i = a("GB", 1024 * c, 1024 * c + 1024), ind(a("PQ", 0, 4096), a("SBU", 64 * c, 64 * c + 64))
+            if c in GB_ON_VECTOR: cp(o, i)
+            else: act(o, i)
+            wsel(a("P4", 64 * c, 64 * c + 64), 4, "GB", 1024 * c, 1024)
+            wsel(a("P5", 64 * c, 64 * c + 64), 5, "GB", 1024 * c, 1024)
+            wsel(a("P0", 64 * c, 64 * c + 64), 6, "GB", 1024 * c, 1024)
+        cp(a("TT", 0, 512), a("P4", 0, 512))
+        act(a("TT", 512, 1024), a("P5", 0, 512))
+        act(a("P5", 0, 512), a("P0", 0, 512), scale=1.0 / 512, bias=8.0); tt(a("TT", 1024, 1536), a("P5", 0, 512), a("TS", 0, 512), A.subtract)
+        tt(t5(1), a("P0", 0, 512), io5(0, 512), A.is_equal); act(a("TT", 1536, 2048), t5(1), scale=4096.0)
+        for b in range(8):
+            dma("s", a("TT", 2048, 4096, 1, (16 * b, 16 * b + 16)), a("TT", 0, 2048, 1, (16 * (b ^ 1), 16 * (b ^ 1) + 16)), 128)
+
+    tables()
+
+    def gram(bd, bb, cnt):
+        for n_, qs in enumerate(GRAM):
+            P = "P%d" % (6 + (n_ & 1)); at_ = 0; pos = []; items = []
+            for q in qs:
+                lh = a(bd, 128 * q, 128 * q + 128)
+                if q: items += acc(a(P, at_, at_ + 16 * q), [(lh, a(bb, 0, 16 * q))])
+                items += acc(a(P, at_ + 16 * q, at_ + 16 * q + 16), [(I128, TRI), (lh, a(bb, 16 * q, 16 * q + 16))])
+                pos.append((q, at_)); at_ += 16 * q + 16
+            mms(items)
+            for q, at_ in pos:
+                act(a("JK", 8 * q * (q + 1), 8 * (q + 1) * (q + 2)), a(P, at_, at_ + 16 * q + 16), F.Relu, bias=-13.0 * 16384, scale=16384.0, acc=sub(cnt, q, q + 1))
+
+    XW = a("X", 0, 8464)
+    def zof(u): return a("MSG", MW * u, MW * u + 256)
+    def lst(t, k): return sub(li("up%d" % t, 64), 16 * k, 16 * k + 16)
+
+    def updates(t):
+        if t >= 1: cp(ind(XW, lst(t - 1, 1 if t < S - 1 else 0)), zof(t - 1))
+        if t >= 2: cp(ind(XW, lst(t - 2, 2)), zof(t - 2))
+        cp(ind(XW, lst(t, 3)), wb(7))
+        cp(ind(XW, lst(t, 0)), wb(1) if t < S - 1 else zof(t))
+        if t < S - 1: cp(ind(a("PQ", 0, 8464), lst(t, 3)), wb(9))
+
+    sent = None
+    marks = []
+    for t in range(S):
+        marks.append(len(ops))
+        M0 = MW * t
+        z = zof(t); ou = a("MSG", M0 + 256, M0 + 272); ah = a("MSG", M0 + 272, M0 + 288); al = a("MSG", M0 + 288, M0 + 304)
+        XT = XW if t else a("X", 0, 4096)
+        if t: arrival(t, sent)
+        items = []
+        for c in range(2):
+            items += acc(a("P3", c, 16, 2), [(I128, sub(CK, c, 16, 2))] + [(MT(2 * c + h), sub(x, h, 16, 2)) for h in range(2) for x in (ah, al)])
+        mms(items)
+        sw = li("sw")
+        cp(sw, a("P3", 0, 16))
+        def tw(j): return ind(a("TT", 512 * j, 512 * j + 2560), sw)
+        def rr(j): return a("RR", 256 * j, 256 * j + 256)
+        ts0 = ind(a("TS", 0, 2560), sw)
+        cc = w(0)
+        aW = sm("aW", 32); kb, a1 = sub(aW, 0, 16), sub(aW, 16, 32)
+        ac, nac = sm("ac"), sm("nac")
+        if t:
+            if FIRST_ON_SCALAR: act(rr(4), tw(0))
+            else: cp(rr(4), tw(0))
+            tp(a("TR", 0, 256), rr(4)); cp(a("LB", 0, 256), a("TR", 0, 256))
+            act(a("RB", 0, 256), tw(1)); act(rr(0), tw(2)); act(rr(1), ts0); act(a("RB", 256, 512), tw(3))
+        else:
+            cp(rr(0), ts0); tp(cc, rr(0))
+        tt(a1, ah, al, A.add)
+        ts(ac, ou, 0.0, A.is_equal); ts(nac, ou, 0.0, A.is_gt, 4096.0, A.mult)
+        tt(kb, nac, d512, A.min); tt(kb, kb, a1, A.max)
+        kbU = li("kb", 32); cp(kbU, sub(aW, 0, 32)); aU = sub(kbU, 16, 32)
+        act(a("BB", 0, 256), ind(a("BITS", 0, 768), sub(kbU, 0, 16)))
+        for h in range(2): act(a("ZZ", 512 + 256 * h, 768 + 256 * h), z)
+        if t:
+            for Q in range(4):
+                for c in (2 * Q, 2 * Q + 1):
+                    (cp if c in DIGITS_ON_VECTOR else act)(a("G1", 512 * c, 512 * c + 512), ind(a("V2", 0, 1536), a("LB", 32 * c, 32 * c + 32)))
+                wsel(a("P0", 64 * Q, 64 * Q + 64), 0, "G1", 1024 * Q, 1024)
+            updates(t - 1)
+            tp(a("RB", 512, 1024), a("RB", 0, 512)); tp(a("P4", 0, 512), a("RR", 0, 512))
+            wi = a("WI", 512, 768); lgp = a("P5", 256, 512)
+            tt(w(1), a("P0", 0, 256), a("RB", 512, 768), A.mult)
+            ts(wi, w(1), 0.5, A.add); ts(wi, wi, 7, A.bitwise_and)
+            tt(w(1), a("P4", 0, 256), wi, A.add); ts(lgp, wi, 1.0, A.not_equal)
+            tt(w(1), lgp, w(1), A.mult); tt(cc, a("P4", 256, 512), w(1), A.add)
+        cU = a("LB", 256, 512)
+        ts(cU, ind(cc, li("reo")), 512.0, A.mult)
+        cp(ind(a("BD", 0, 2048), li("bd")), a("BB", 0, 256))
+        if t:
+            ops[-1]["early"] = EARLY
+            gram("BD", "BB", sm("cb"))
+        for c in range(8):
+            dd, ad, src = a("DD", 512 * c, 512 * c + 512), a("AD", 512 * c, 512 * c + 512), ind(XT, sub(cU, 32 * c, 32 * c + 32))
+            if c < NA:
+                act(dd, src)
+                mms(acc(a("P2", 0, 512), [(I128, dd), (NEG, a("ZZ", 512, 1024))]))
+                act(ad, a("P2", 0, 512), F.Abs)
+            else:
+                tt(dd, src, a("ZZ", 512, 1024), A.subtract)
+                act(ad, dd, F.Abs)
+            if c & 1:
+                Q = c >> 1
+                wsel(a("P1", 64 * Q, 64 * Q + 64), 0, "AD", 1024 * Q, 1024, [(I128, sub(KC, 64 * Q, 64 * Q + 64))])
+        dl = a("P0" if t else "P2", 256, 512)
+        mms(acc(dl, [(a("IF", 0, 128), cc), (a("IF", 128, 256), sub(w(0, 272), 1, 257))]))
+        act(w(3), a("P1", 0, 256))
+        if t == 0: gram("BD", "BB", sm("cb"))
+        if t:
+            mms(acc(a("P2", 0, 256), [(Y(0, k), a("AD", 256 * k, 256 * k + 256)) for k in range(16)]))
+            tt(w(2), lgp, a("RB", 768, 1024), A.mult)
+        nx = sm("nx"); act(nx, sub(w(0, 272), 16, 272, 16), scale=512.0)
+        key = w(5); mn = sub(w(6, 272), 8, 264)
+        if t: tt(key, ind(w(3), li("reo")), w(2), A.add)
+        else: cp(key, ind(w(3), li("reo")))
+        scan(mn, RST, key, A.add, A.min)
+        tt(w(7), ind(mn, li("exp")), key, A.not_equal)
+        scan(w(8), w(7), dl, A.mult, A.add)
+        ef = sm("ef", 32); m12 = sm("m12", 32)
+        e, f = sub(ef, 0, 16), sub(ef, 16, 32); m1, m2 = sub(m12, 0, 16), sub(m12, 16, 32)
+        efU = li("efU", 32); eU, fU = sub(efU, 0, 16), sub(efU, 16, 32)
+        tt(e, sub(w(8), 15, 256, 16), nx, A.add)
+        cl, kc = sm("cl"), sm("kc")
+        tt(m1, sub(mn, 15, 256, 16), nac, A.add)
+        ts(kc, m1, 1009.0, A.is_ge, 16384.0, A.mult); tt(kc, kc, d8k if t else sm("d4k"), A.min); tt(kc, kc, e, A.max); cp(li("kc"), kc)
+        act(a("BC", 0, 256), ind(a("BITS", 0, 8464 if t else 4352), li("kc")))
+        cp(ind(a("BE", 0, 2048), li("bd")), a("BC", 0, 256))
+        gram("BE", "BC", sm("cc"))
+        ts(cl, m1, 1009.0, A.is_lt)
+        if t: act(w(12), a("P2", 0, 256))
+        if t: act(a("P4", 0, 256), key)
+        tt(w(9), a("P4", 0, 256) if t else key, sub(w(6, 272), 7, 263), A.max)
+        ms(sub(w(9), 0, 256, 16), 65536.0)
+        scan(w(10), RST, w(9), A.add, A.min)
+        tt(w(1), ind(w(10), li("exp")), key, A.not_equal)
+        scan(w(4), w(1), dl, A.mult, A.add)
+        tt(f, sub(w(4), 15, 256, 16), nx, A.add)
+        cp(eU, e); cp(fU, f)
+        PT = a("PQ", 0, 8464 if t else 4096)
+        act(wb(10), ind(PT, eU)); act(wb(11), ind(PT, fU))
+        act(wb(0), z, bias=col("m192"))
+        less = [(NEG, ah), (NEG, al)]
+        wsel(a("P3", 32, 48), 3, "WB", 256 * 10, 256, less); wsel(a("P3", 64, 80), 6, "WB", 256 * 10, 256, less); wsel(a("P3", 80, 96), 6, "WB", 256 * 11, 256, less)
+        d1, xe, xf = wb(2), wb(8), wb(3)
+        (act if XE_ON_SCALAR else cp)(xe, ind(XT, eU)); (act if XF_ON_SCALAR else cp)(xf, ind(XT, fU))
+        tt(d1, xe, z, A.subtract)
+        ts(wb(4), d1, 0.5, A.mult, 191.75, A.add)
+        tt(a("ZZ", 256, 512), wb(4), wb(0), A.add)
+        act(a("ZZ", 0, 256), d1, F.Abs)
+        tt(wb(5), xe, xf, A.subtract)
+        act(wb(6), wb(5), F.Abs)
+        wsel(a("P1", 256, 272), 0, "WB", 256 * 6, 256)
+        if t < S - 1: act(wb(1), z, bias=col("p128"))
+        act(w(11), ind(a("VR", 0, 768), aU))
+        act(w(13), io5(0, 256), scale=2.0 ** -21, bias=col("cd%d" % t))
+        tt(wb(7), xe, xf, A.max)
+        if t: act(a("P5", 0, 256), w(11))
+        act(m2, sub(w(10), 15, 256, 16))
+        lg = sm("lg", 32); ts(lg, ef, 4096.0, A.is_ge); lge = sub(lg, 0, 16)
+        on = sm("on"); act(on, ou, F.Relu, bias=-1.0)
+        ix = sm("ix"); act(ix, cl, scale=-512.0, bias=512.0); tt(ix, ix, iW, A.add)
+        ts(si(2, 32), m12, 16.0, A.mult); ts(si(2, 32), si(2, 32), 15, A.bitwise_and)
+        kk = sm("kk"); ts(kk, si(2), 16.0, A.mult, -256.0, A.add); tt(kk, kk, si(3), A.add)
+        Pa, Qa, dx = a("P3", 32, 48), a("P3", 64, 96), sm("dx")
+        ts(dx, Pa, 0.0, A.is_equal); tt(dx, sub(Qa, 0, 16), dx, A.mult); tt(dx, Pa, dx, A.add)
+        hm = sm("hm", 32); ts(hm, Qa, 0.0, A.is_equal)
+        st = sm("st"); act(st, lge, bias=1.0)
+        tk = sm("tk")
+        tt(tk, cl, sm("cc"), A.is_gt)
+        tt(sm("t3"), tk, i256, A.mult); tt(sm("t3"), sm("t3"), ix, A.max); cp(li("ix"), sm("t3"))
+        O0 = MW * t
+        cp(a("OUT", O0, O0 + 256), ind(a("ZZ", 0, 768), li("ix")))
+        tt(dx, dx, tk, A.mult); tt(dx, dx, a1, A.add)
+        cp(a("OUT", O0 + 272, O0 + 288), dx); tt(a("OUT", O0 + 288, O0 + 304), dx, a("OUT", O0 + 272, O0 + 288), A.subtract)
+        tt(st, st, tk, A.mult); tt(a("OUT", O0 + 256, O0 + 272), st, on, A.add)
+        sent = (send(t, "box", 272, MW), send(t, "arr", 0, 272))
+        sw_, vo, jn = sm("ms"), sm("vo"), a("SH", 0, 16)
+        tt(sw_, ac, sm("cb"), A.is_gt); tt(vo, sm("cb"), d512, A.min); tt(vo, vo, kb, A.max); cp(li("vo"), vo)
+        r12 = sm("r12", 32)
+        tt(r12, m12, thr, A.is_lt)
+        if t: cp(li("sp"), sub(r12, 0, 16))
+        tt(hm, hm, lg, A.is_gt); tt(hm, hm, r12, A.mult)
+        ts(sm("t1"), a("P1", 256, 272), col("jl"), A.is_lt); tt(sm("t1"), sm("t1"), sw_, A.mult)
+        tt(sm("t2"), sub(hm, 0, 16), sub(hm, 16, 32), A.mult); tt(jn, sm("t1"), sm("t2"), A.mult)
+        tt(kk, kk, jn, A.mult); ts(li("kk"), kk, 256.0, A.add)
+        tt(w(7), ind(a("LUT", 0, 264), li("kk")), w(13), A.mult)
+        if t:
+            tt(w(8), ind(a("LUT", 264, 272), li("sp")), w(12), A.is_lt)
+            tt(w(11), a("P5", 0, 256), w(8), A.mult)
+        tt(ind(a("VR", 0, 768), li("vo")), w(11), w(7), A.add)
+        if t < S - 1:
+            for h in range(2):
+                act(a("V2", 512 * h, 512 * h + 512), a("VR", 0, 512), bias=col("vb%d" % h), scale=col("vs%d" % h))
+        up = sm("up", 64); u0, u1, u2, u3 = (sub(up, 16 * k, 16 * k + 16) for k in range(4))
+        if t: tt(u0, sm("cc"), d8k, A.min); tt(u0, u0, kc, A.max)
+        else: tt(u0, cl, sm("cc"), A.is_le); tt(u0, u0, d8k, A.mult); tt(u0, u0, e, A.max); ms(sub(up, 16, 48), 0.0)
+        if t < S - 2:
+            tt(u1, lge, d8k, A.mult); tt(u2, d8k, u1, A.subtract); tt(u1, u1, u0, A.max); tt(u2, u2, u0, A.max)
+        act(sm("t4"), a1, bias=4096.0 + 512 * ((t + 2) & 7))
+        act(u3, jn, scale=-16384.0, bias=16384.0); tt(u3, u3, d8k, A.min); tt(u3, u3, sm("t4"), A.max)
+        cp(li("up%d" % t, 64), up)
+        ts(sub(li("yl", 128), 16 * t, 16 * t + 16), u3, 8192.0, A.min)
+        if t < S - 1:
+            mms(acc(a("P1", 256, 512), [(ME, wb(10)), (MF, wb(11))]))
+            act(wb(9), a("P1", 256, 512))
+            mms(acc(a("P3", 96, 112), [(BLK, jn)]))
+            act(a("JK", 2176, 2192), a("P3", 96, 112), acc=col("nj"))
+            ts(si(6, 1), col("nj"), 8.0, A.mult, col("A"), A.add); ts(si(6, 1), si(6, 1), 255, A.bitwise_and)
+            ts(col("jl"), si(6, 1), col("lim0"), A.add); act(col("A"), col("jl"), bias=col("nl0"))
+
+    ts(a("G1", 0, 512), a("VR", 0, 512), short, A.add, 2.0 ** 21, A.mult)
+    act(a("P4", 0, 512), a("VR", 0, 512), scale=2.0 ** 21, bias=c_(short, 2.0 ** 21, A.mult))
+    tt(t5(0), a("P4", 0, 512), a("G1", 0, 512), A.subtract)
+    act(a("NB", 0, 512), t5(0))
+    act(a("P5", 0, 512), t5(0))
+    tt(a("NB", 512, 1024), a("P5", 0, 512), a("NB", 0, 512), A.subtract)
+    for f in range(2):
+        dma("s", grp("GB", f, 8192), a("NB", 512 * f, 512 * f + 512), 128)
+    updates(S - 1)
+    dma("s", T.yx[:, 0:4096], a("X", 0, 4096), 1024)
+    yl = li("yl", 128)
+    act(a("DD", 0, 1024), ind(XW, sub(yl, 0, 64))); (cp if 4 in LAST_ON_VECTOR else act)(a("DD", 1024, 2048), ind(XW, sub(yl, 64, 128)))
+    dma("s", T.yx[:, 4096:6144], a("DD", 0, 2048), 512)
+    for c in range(4):
+        o, i = a("G1", 1024 * c, 1024 * c + 1024), ind(a("GB", 0, 8208), a("LB", 768 + 64 * c, 832 + 64 * c))
+        if c in LAST_ON_VECTOR: cp(o, i)
+        else: act(o, i)
+        wsel(a("P0", 64 * c, 64 * c + 64), 3, "G1", 1024 * c, 1024)
+    M0 = MW * S
+    arrival(S, sent)
+    dma("a", T.yz[:], a("MSG", M0, M0 + 256), 64)
+    for h in range(2): tt(a("BXF", 16 * h, 16 * h + 16), a("MSG", M0 + 272, M0 + 288), a("MSG", M0 + 288, M0 + 304), A.add)
+    flip(sm("b0"))
+    dma("a", T.yb[:], sm("b0"), 8)
+    ts(nf(0), io5(0, 256), c_(pm, 256.0, A.mult), A.add)
+    ts(nf(1), a("P0", 0, 256), 0.0, A.is_gt, 4095.0, A.mult); tt(nf(1), a("P0", 0, 256), nf(1), A.add)
+    tt(nf(1), nf(1), nf(0), A.max)
+    dma("s", T.yj[:], nf(1), 128)
+
+    n = len(ops)
+    hist = {}; turns = {}
+    deps = PLAN.get("deps", [])
+    for i, o in enumerate(ops if not deps else ()):
+        d = {}
+        for kind, rs in (("r", o["r"]), ("w", o["w"])):
+            for (nm, lo, hi, pt) in rs:
+                for (j, k2, l2, h2, p2) in hist.get(nm, ()):
+                    if lo < h2 and l2 < hi and pt & p2 and (kind == "w" or k2 == "w"):
+                        d[j] = bool(ops[j]["e"] != o["e"] or o["e"] != "p")
+        for kind, rs in (("w", o["w"]), ("r", o["r"])):
+            for (nm, lo, hi, pt) in rs:
+                keep = hist.get(nm, [])
+                if kind == "w": keep = [x for x in keep if not (lo <= x[2] and x[3] <= hi and x[4] & ~pt == 0)]
+                hist[nm] = keep + [(i, kind, lo, hi, pt)]
+        for nm in set(x[0] for x in o["w"] + o["r"] if SCRATCH[x[0]][0] == "psum"):
+            was, now = turns.get(nm, ([], []))
+            if now and ops[now[0]]["e"] != o["e"]: was, now = now, []
+            for j in was: d[j] = True
+            turns[nm] = (was, now + [i])
+        d.pop(i, None)
+        deps.append(d)
+    pred = [dict(d) for d in deps]
+    for i, o in enumerate(ops):
+        if o["e"] == "x": pred[i][o["after"]] = True
+    succ = [[] for _ in range(n)]
+    for i in range(n):
+        for j in pred[i]: succ[j].append(i)
+    prio = [0.0] * n
+    for i in range(n - 1, -1, -1):
+        prio[i] = ops[i]["c"] + ops[i].get("early", 0) + max([prio[k] + (ops[i]["lat"] if pred[k][i] else 0) for k in succ[i]] + [ops[i]["lat"] if ops[i]["dma"] else 0])
+    tail = [ops[i]["lat"] if ops[i]["dma"] else 0 for i in range(n)]
+
+    def run(before, after, gap, first, pr, peek):
+        left = [len(p) for p in before]
+        ready = list(first); fin = [0.0] * n
+        free = {q: 0.0 for q in "vapgsx"}
+        pool = {q: [] for q in "vapgsx"}
+        for i in range(n):
+            if not left[i]: pool[ops[i]["e"]].append(i)
+        seq = []
+        while len(seq) < n:
+            s0, q = min((max(free[q_], min(ready[i] for i in p)), q_) for q_, p in pool.items() if p)
+            i = max((i for i in pool[q] if ready[i] <= s0 + peek), key=lambda k: (pr[k], -k))
+            pool[q].remove(i); seq.append(i)
+            end = max(free[q], ready[i]) + ops[i]["c"]; free[q] = end; fin[i] = end
+            for k in after[i]:
+                ready[k] = max(ready[k], end + gap(i, k)); left[k] -= 1
+                if not left[k]: pool[ops[k]["e"]].append(k)
+        return seq, fin
+
+    if "order" not in PLAN:
+        keys = ["%s%s%d" % (o["e"], o["w"][0][0], o["w"][0][1] % MW if o["w"][0][0] in ("MSG", "OUT") else o["w"][0][1]) if o["w"] else "send" for o in ops]
+        keys = [k + ("." if i < marks[1] else "!" if i >= marks[S - 1] else "") for i, k in enumerate(keys)]
+        pl = [list(p.items()) for p in pred]; eng = [o["e"] for o in ops]
+        sets = [([o["c"] * (kp if o["e"] == "p" else 1) + o.get("g", 0) * kg + o.get("s", 0) * ks for o in ops],
+                 [sy if o["lat"] == SYNC else o["lat"] for o in ops], wt) for kg, ks, kp, sy, wt in SETTINGS]
+
+        def score(seq):
+            r = []
+            for c, lat, wt in sets:
+                fin = [0.0] * n; free = dict.fromkeys("vapgsx", 0.0); mx = 0.0
+                for i in seq:
+                    s_ = free[eng[i]]
+                    for j, wait in pl[i]:
+                        x = fin[j] + lat[j] if wait else fin[j]
+                        if x > s_: s_ = x
+                    s_ += c[i]; fin[i] = s_; free[eng[i]] = s_
+                    if s_ + tail[i] > mx: mx = s_ + tail[i]
+                r.append(mx)
+            return sum(x * y[2] for x, y in zip(r, sets)), r
+        forward = lambda pr: run(pred, succ, lambda i, k: ops[i]["lat"] if pred[k][i] else 0, [0.0] * n, pr, PEEK)
+        seq, fin = forward(prio)
+        base = run(succ, pred, lambda i, k: ops[k]["lat"] if pred[i][k] else 0, tail, fin, PEEK)[1]
+        rng = np.random.default_rng(SEED)
+        more = dict.fromkeys(keys, 0.0)
+        seq = forward(base)[0]; best = score(seq) + (seq,)
+        for _ in range(TRIES):
+            i = int(rng.integers(n)); depth = int(rng.choice((0, 1, 2, 3, 5, 9))); step = float(rng.choice(MOVES)) * (1 if rng.random() < 0.5 else -1)
+            near = {i}; edge = {i}
+            for _d in range(depth):
+                edge = set(j for k in edge for j in (pred[k] if step > 0 else succ[k]) if abs(j - i) < 200) - near
+                near |= edge
+            trial = dict(more)
+            for k in set(keys[j] for j in near): trial[k] += step
+            seq = forward([x + trial[k] for x, k in zip(base, keys)])[0]; got = score(seq)
+            if got[0] <= best[0]: best = got + (seq,); more = trial
+        PLAN["deps"], PLAN["order"], PLAN["span"] = deps, best[2], best[1]
+    order = PLAN["order"]
+    place = {i: k for k, i in enumerate(order)}
+    clock = {}
+    know = {q: ({}, set()) for q in "vapgsx"}
+    need = {}
+    marked = set()
+    for i in order:
+        o = ops[i]; kq, kd = know[o["e"]]; need[i] = []
+        for j in sorted((j for j in deps[i] if deps[i][j]), key=lambda k: -place[k]):
+            oj = ops[j]
+            if oj["dma"]:
+                if j in kd or oj["dma"] == "remote": continue
+            elif kq.get(oj["e"], -1) >= place[j]: continue
+            need[i].append(j); marked.add(j)
+            cq, cd = clock[j]
+            for q, v in cq.items():
+                if kq.get(q, -1) < v: kq[q] = v
+            kd |= cd
+        cq = dict(kq); cd = set(kd)
+        if o["dma"]: cd.add(i)
+        else: cq[o["e"]] = place[i]
+        clock[i] = (cq, cd)
+    semof = {"v": "ev", "a": "ea", "p": "ep", "g": "eg"}
+    queue = {"v": g.vector, "a": g.scalar, "p": g.tensor, "g": g, "s": g.sync}
+    cnt = {q: 0 for q in semof}
+    val = {}
+    for i in order:
+        o = ops[i]
+        if o["e"] == "x": continue
+        for j in need[i]:
+            oj = ops[j]
+            if oj["e"] == "x": queue[o["e"]].wait_ge(T.sem[oj["dma"]], nen)
+            elif oj["dma"]: queue[o["e"]].wait_ge(T.sem[oj["dma"]], 16)
+            else: queue[o["e"]].wait_ge(T.sem[semof[oj["e"]]], val[j])
+        for fn in o["f"]: ins = fn()
+        if o["dma"] == "remote": continue
+        if o["dma"]: ins.then_inc(T.sem[o["dma"]], 16)
+        elif i in marked:
+            cnt[o["e"]] += 1; val[i] = cnt[o["e"]]
+            ins.then_inc(T.sem[semof[o["e"]]], 1)
+    for q, v in cnt.items():
+        if v: g.wait_ge(T.sem[semof[q]], v)
+    for k in range(ndma[0]):
+        g.wait_ge(T.sem["d%d" % k], 16)
+    for t in range(1, S + 1):
+        g.wait_ge(T.sem["arr%d" % t], nen); g.wait_ge(T.sem["box%d" % t], nen)
+    g.wait_ge(T.sem.sent, nen * 2 * S)
+
+
+BITS_ON_SCALAR = tuple(range(17))
+GB_ON_VECTOR = (0, 2, 4)
+FIRST_ON_SCALAR = False
+XE_ON_SCALAR = True
+XF_ON_SCALAR = True
+DIGITS_ON_VECTOR = (1,)
+LAST_ON_VECTOR = (1, 3)

@@ -1,40 +1,53 @@
 import numpy as np
+from concourse.bass import DstId, RemoteDMATransfer
 from concourse.mybir import AluOpType as A, ActivationFunctionType as F
 
 S = 8
-MW = 304
-NA = 2
+MW = 1024
+XC = 8704
+SPARE, ZERO, LONG = 4096, 4352, 4096
 f32, bf, i32, u16 = "float32", "bfloat16", "int32", "uint16"
 SCRATCH = {
-    "X": ("sbuf", [128, 8464], bf), "PQ": ("sbuf", [128, 8464], bf),
-    "BITS": ("sbuf", [128, 8704], bf), "GB": ("sbuf", [128, 8208], bf), "DD": ("sbuf", [128, 4096], bf),
-    "AD": ("sbuf", [128, 4096], bf), "G1": ("sbuf", [128, 4096], bf), "IOS": ("sbuf", [128, 2560], f32),
-    "TS": ("sbuf", [128, 2560], f32), "TT": ("sbuf", [128, 4096], f32), "SBI": ("sbuf", [128, 1024], i32), "SBU": ("sbuf", [128, 512], u16),
-    "BD": ("sbuf", [128, 2048], bf), "BB": ("sbuf", [128, 256], bf), "BE": ("sbuf", [128, 2048], bf), "BC": ("sbuf", [128, 256], bf),
-    "VR": ("sbuf", [128, 768], f32), "V2": ("sbuf", [128, 1536], bf),
-    "MSG": ("sbuf", [128, MW * (S + 1)], bf), "OUT": ("sbuf", [128, MW * S], bf),
-    "RR": ("sbuf", [128, 1280], f32), "TR": ("sbuf", [128, 512], f32),
-    "W": ("sbuf", [128, 272 * 14], f32), "WI": ("sbuf", [128, 1024], i32), "WB": ("sbuf", [128, 256 * 12], bf),
-    "ZZ": ("sbuf", [128, 1024], bf), "SM": ("sbuf", [128, 16 * 72], f32), "SI": ("sbuf", [128, 16 * 8], i32),
-    "SH": ("sbuf", [128, 16], bf), "L": ("sbuf", [128, 16 * 64], u16), "LB": ("sbuf", [128, 256 * 4], u16),
-    "MAT": ("sbuf", [128, 144 * 7 + 128 * 9 + 288], bf), "T5": ("sbuf", [128, 512 * 4], f32), "IF": ("sbuf", [128, 256], f32),
-    "NI": ("sbuf", [128, 512], i32), "NF": ("sbuf", [128, 256 * 5], f32), "NB": ("sbuf", [128, 256 * 7], bf),
+    "X": ("sbuf", [128, XC], bf), "PQ": ("sbuf", [128, 8192], bf), "IOT": ("sbuf", [128, 8192], i32),
+    "GB": ("sbuf", [128, 8208], bf), "DD": ("sbuf", [128, 4096], bf), "G1": ("sbuf", [128, 4096], bf),
+    "E": ("sbuf", [128, 16, 256], bf), "IOS": ("sbuf", [128, 2560], f32), "IO": ("sbuf", [128, 512], f32),
+    "TT": ("sbuf", [128, 1536], f32), "TB": ("sbuf", [128, 1024], bf), "SBI": ("sbuf", [128, 1024], i32), "SBU": ("sbuf", [128, 512], u16),
+    "VR": ("sbuf", [128, 768], f32), "V2": ("sbuf", [128, 1024], bf),
+    "MSG": ("sbuf", [128, MW * S + 256], bf), "OUT": ("sbuf", [128, 256 * S], bf),
+    "BOX": ("sbuf", [128, 32 * (S + 1)], u16), "BOXO": ("sbuf", [128, 32 * S], u16),
+    "XD": ("sbuf", [128, 16, 16], bf), "T2": ("sbuf", [128, 16, 16], f32), "MN": ("sbuf", [128, 512], f32),
+    "W": ("sbuf", [128, 256 * 10], f32), "WI": ("sbuf", [128, 512], i32), "WB": ("sbuf", [128, 256 * 16], bf),
+    "SM": ("sbuf", [128, 16 * 72], f32), "SI": ("sbuf", [128, 16 * 8], i32),
+    "SH": ("sbuf", [128, 16 * 12], bf), "L": ("sbuf", [128, 16 * 64], u16), "LB": ("sbuf", [128, 256 * 5], u16),
+    "MAT": ("sbuf", [128, 144 * 8 + 128 * 12 + 256 * 4], bf), "SEL": ("sbuf", [128, 128 * 32], bf), "IF": ("sbuf", [128, 128 * 8], f32),
+    "T5": ("sbuf", [128, 512 * 3], f32),
+    "NI": ("sbuf", [128, 512], i32), "NF": ("sbuf", [128, 256 * 3], f32), "NB": ("sbuf", [128, 256 * 4], bf),
     "BXI": ("sbuf", [128, 32], i32), "BXF": ("sbuf", [128, 64], f32), "LI": ("sbuf", [128, 4], i32), "LF": ("sbuf", [128, 4], f32),
-    "E8": ("sbuf", [128, 256], f32), "LUT": ("sbuf", [128, 272], f32), "JK": ("sbuf", [128, 2192], bf), "RB": ("sbuf", [128, 1024], bf),
-    "RST": ("sbuf", [128, 256], f32), "QR": ("sbuf", [128, 512], f32),
+    "E8": ("sbuf", [128, 256], f32), "JK": ("sbuf", [128, 16], bf), "RST": ("sbuf", [128, 256], f32), "QR": ("sbuf", [128, 512], f32),
 }
+for _b in range(4):
+    SCRATCH["AD%d" % _b] = ("sbuf", [128, 16, 4, 16], bf)
 for _b in range(8):
-    SCRATCH["P%d" % _b] = ("psum", [128, 512], f32)
-NDMA = 48
+    SCRATCH["P%d" % _b] = ("psum", [128, 32, 16] if _b != 2 else [128, 512], f32)
+ROW = [4 * (k & 3) + (k >> 2) for k in range(16)]
+NDMA = 56
 SEMAPHORES = ["ev", "ea", "ep", "eg", "sent"] + [nm + str(t) for t in range(1, S + 1) for nm in ("arr", "box")] + ["d%d" % k for k in range(NDMA)]
-GRAM = ((15, 14), (13, 12, 3, 0), (11, 10, 8), (9, 7, 6, 5), (4, 2, 1))
 SIZE = {f32: 4, bf: 2, i32: 4, u16: 2}
 GATHER, SCATTER, TENSOR, SYNC, WIRE = 1.56, 3.8, 0.5, 60, 2460
 ALL = (1 << 128) - 1
-EARLY = 9000
-PEEK, SEED, TRIES, MOVES = 130, 1, 3000, (150, 400, 1000, 2500, 6000)
+PEEK, SEED, TRIES, MOVES = 130, 1, 2000, (150, 400, 1000, 2500, 6000)
 SETTINGS = ((0, 0, 1, 60, 0.4), (-0.46, -1.6, 1, 40, 0.24), (0.44, 1.7, 1, 80, 0.17), (0, 0, 2, 140, 0.16))
 PLAN = {}
+MASKS = {}
+
+
+def cover(x):
+    if x[:2] not in MASKS:
+        shape = SCRATCH[x[0]][1][1:]
+        cols = np.arange(int(np.prod(shape))).reshape(shape)[tuple(i if isinstance(i, int) else slice(*i) for i in x[1])].reshape(-1)
+        bits = np.zeros(int(np.prod(shape)), np.uint8); bits[cols] = 1
+        MASKS[x[:2]] = (int.from_bytes(np.packbits(bits, bitorder="little").tobytes(), "little"), int(cols.min()), int(cols.size))
+    return MASKS[x[:2]]
 
 
 def rank_program(g, core, T, topo):
@@ -47,9 +60,16 @@ def rank_program(g, core, T, topo):
     nen = len(topo.engines(core, nxt))
     ops = []
     ndma = [0]
+    expect = {}
 
     def a(name, lo, hi, step=1, ps=None):
-        return (name, lo, hi, step, ps)
+        return (name, ((lo, hi, step),), ps)
+
+    def b(name, *idx):
+        return (name, tuple(i if isinstance(i, int) else tuple(i) + (1,) * (3 - len(i)) for i in idx), None)
+
+    def P(k, lo, hi=None, step=1):
+        return b("P%d" % k, lo, (0, 16)) if hi is None else b("P%d" % k, (lo, hi, step), (0, 16))
 
     def ind(win, off):
         return ("ind", win, off)
@@ -59,18 +79,18 @@ def rank_program(g, core, T, topo):
             return x
         if x[0] == "ind":
             return ap(x[1]).indirect(ap(x[2]))
-        ps = slice(None) if x[4] is None else slice(*x[4])
-        return T[x[0]][ps, x[1]:x[2]:x[3]] if x[3] != 1 else T[x[0]][ps, x[1]:x[2]]
+        ps = slice(None) if x[2] is None else slice(*x[2])
+        return T[x[0]][(ps,) + tuple(i if isinstance(i, int) else slice(i[0], i[1]) if i[2] == 1 else slice(*i) for i in x[1])]
 
     def regs(xs):
         r = []
         for x in xs:
             if isinstance(x, tuple):
-                r += regs([x[1], x[2]]) if x[0] == "ind" else [(x[0], x[1], x[2], ALL if x[4] is None else sum(1 << p for p in range(*x[4])))]
+                r += regs([x[1], x[2]]) if x[0] == "ind" else [(x[0], cover(x)[0], ALL if x[2] is None else sum(1 << p for p in range(*x[2])), cover(x)[1])]
         return r
 
     def wid(x):
-        return 16 * wid(x[2]) if x[0] == "ind" else len(range(x[1], x[2], x[3]))
+        return 16 * wid(x[2]) if x[0] == "ind" else cover(x)[2]
 
     def op(eng, fn, out, ins, cost):
         if isinstance(out, tuple) and out[0] == "ind":
@@ -97,15 +117,19 @@ def rank_program(g, core, T, topo):
     def tp(o, i): op("v", lambda: g.vector.transpose(ap(o), ap(i)), o, [i], vc(o, i))
     def ms(o, c): op("v", lambda: g.vector.memset(ap(o), c), o, [], vc(o, o))
     def act(o, i, fn=F.Identity, bias=0.0, scale=1.0, acc=None):
-        c = 78 + wid(o) * GATHER if i[0] == "ind" else max(64, wid(o))
+        c = 78 + wid(o) * GATHER if i[0] == "ind" else max(64, wid(o)) + ACT
         if acc is None: op("a", lambda: g.scalar.activation(ap(o), ap(i), fn, bias=ap(bias), scale=ap(scale)), o, [i, bias, scale], c)
         else: op("a", lambda: g.scalar.activation(ap(o), ap(i), fn, bias=ap(bias), scale=ap(scale), accum_out=ap(acc)), acc, [i, bias, scale], c + 24)
         if acc is not None: ops[-1]["w"] += regs([o])
+    def mul(on_v, o, i, s):
+        if on_v: ts(o, i, s, A.mult)
+        else: act(o, i, scale=s)
+    def get(on_v, o, i): (cp if on_v else act)(o, i)
     def mms(items):
         fs = [(lambda o, l, r, st, sp: lambda: g.tensor.matmul(ap(o), ap(l), ap(r), st, sp))(*x) for x in items]
-        ops.append({"e": "p", "f": fs, "w": regs([x[0] for x in items]), "r": list(set(regs([x[1] for x in items] + [x[2] for x in items]))), "dma": None,
+        ops.append({"e": "p", "f": fs, "w": list(set(regs([x[0] for x in items]))), "r": list(set(regs([x[1] for x in items] + [x[2] for x in items]))), "dma": None,
                     "c": sum(TENSOR * max(64, wid(x[2])) * (4 if SCRATCH[x[1][0]][2] == f32 else 1) for x in items), "lat": SYNC})
-    def acc(o, pairs): return [(o, l, r, k == 0, k == len(pairs) - 1) for k, (l, r) in enumerate(pairs)]
+    def acc(o, pairs, start=True, stop=True): return [(o, l, r, start and k == 0, stop and k == len(pairs) - 1) for k, (l, r) in enumerate(pairs)]
     def iota(o, pat, base, cm):
         if SCRATCH[o[0]][2] != i32: op("g", lambda: g.iota(ap(o), pat, base, cm, allow_small_or_imprecise_dtypes=True), o, [], 160 + 2 * wid(o))
         else: op("g", lambda: g.iota(ap(o), pat, base, cm), o, [], 160 + 2 * wid(o))
@@ -114,64 +138,84 @@ def rank_program(g, core, T, topo):
         op(q, lambda: eng.dma_start(ap(o), ap(i)), o, [i], 60)
         ops[-1]["dma"] = "d%d" % ndma[0]; ops[-1]["lat"] = 2400 + 5 * kb
         ndma[0] += 1
-    def arrival(t, after):
-        for nm, lo, hi, j in (("arr", 0, 272, after[1]), ("box", 272, MW, after[0])):
-            ops.append({"e": "x", "f": [], "w": [("MSG", MW * t + lo, MW * t + hi, ALL)], "r": [], "dma": nm + str(t), "c": 0, "lat": 0, "after": j})
-    def send(t, nm, lo, hi):
-        src, dst, sem = a("OUT", MW * t + lo, MW * t + hi), a("MSG", MW * (t + 1) + lo, MW * (t + 1) + hi), T.sem[nm + str(t + 1)]
-        op("g", lambda: g.remote_dma(ap(dst), ap(src), sem, T.sem.sent, pid, rid, emask), None, [src], 600)
+    def arrival(nm, t, lands, after):
+        ops.append({"e": "x", "f": [], "w": regs(lands), "r": [], "dma": nm + str(t), "c": 0, "lat": 0, "after": after})
+        expect[nm + str(t)] = nen * len(lands)
+    def send(nm, t, src, lands):
+        sem = T.sem[nm + str(t)]
+        if len(lands) == 1:
+            op("g", lambda: g.remote_dma(ap(lands[0]), ap(src), sem, T.sem.sent, pid, rid, emask), None, [src], 600)
+        else:
+            op("g", lambda: g.remote_dma_fused([RemoteDMATransfer(dst_ids=[DstId(rid=rid, pnc=pid)] * len(lands), dma_engine_mask=emask, remote_sem=sem,
+                                                                  src=ap(src), dsts=[ap(x) for x in lands])], local_sem=T.sem.sent), None, [src], 600)
         ops[-1]["dma"] = "remote"; ops[-1]["lat"] = WIRE
         return len(ops) - 1
+    def zlands(t): return [a("MSG", MW * t + 256 * h, MW * t + 256 * h + 256) for h in range(2 if t < S else 1)]
+    def blands(t): return [a("BOX", 32 * t, 32 * t + 32)]
 
-    at = {"SM": 0, "L": 0}
+    at = {"SM": 0, "L": 0, "SH": 0}
     def slot(buf, name, n):
         if (buf, name) not in at:
             at[(buf, name)] = at[buf]; at[buf] += n
         return a(buf, at[(buf, name)], at[(buf, name)] + n)
     def sm(name, n=16): return slot("SM", name, n)
+    def sh(name, n=16): return slot("SH", name, n)
     def col(name): return slot("SM", name, 1)
     def li(name, n=16): return slot("L", name, n)
-    def sub(x, lo, hi, step=1): return a(x[0], x[1] + lo, x[1] + hi, step)
-    def w(k, n=256): return a("W", 272 * k, 272 * k + n)
-    def wb(k): return a("WB", 256 * k, 256 * k + 256)
+    def sub(x, lo, hi, step=1): return a(x[0], x[1][0][0] + lo, x[1][0][0] + hi, step)
+    def w(k): return a("W", 256 * k, 256 * k + 256)
+    def wb(k, n=1): return a("WB", 256 * k, 256 * (k + n))
     def si(k, n=16): return a("SI", 16 * k, 16 * k + n)
+    def lb(k): return a("LB", 256 * k, 256 * k + 256)
     def YM(k): return a("MAT", 144 * k, 144 * k + 144)
     def Y(k, r): return a("MAT", 144 * k + 15 - r, 144 * k + 143 - r)
-    def MT(k): return a("MAT", 1008 + 128 * k, 1136 + 128 * k)
-    KC = a("MAT", 2160, 2416); TRI = a("MAT", 2416, 2432); CK = a("MAT", 2432, 2448)
-    I128, BLK, NEG, ME, MF = MT(4), MT(5), MT(6), MT(7), MT(8)
-    def io5(lo, hi): return a("TS", 512 + lo, 512 + hi)
+    def MT(k): return a("MAT", 1152 + 128 * k, 1280 + 128 * k)
+    def MF(k): return a("IF", 128 * k, 128 * k + 128)
+    def M2(k): return a("MAT", 2688 + 256 * k, 2944 + 256 * k)
+    KC, LUT, IDT, ONES = M2(0), M2(1), M2(2), M2(3)
+    I128, BLK, NEG, HALF, ME, MG, LIM, NIL = MT(4), MT(5), MT(6), MT(7), MT(8), MT(9), MT(10), MT(11)
+    IF, NF, BIG, NBIG = MF(4), MF(5), MF(6), MF(7)
+    def LOW(r): return a("SEL", 128 * r, 128 * r + 128)
+    def SPREAD(r): return a("SEL", 2048 + 128 * r, 2176 + 128 * r)
+    def io5(lo, hi): return a("IO", lo, hi)
     def nf(k): return a("NF", 256 * k, 256 * k + 256)
     def nb(k): return a("NB", 256 * k, 256 * k + 256)
     def t5(k): return a("T5", 512 * k, 512 * k + 512)
     def grp(name, f, n): return a(name, 0, n, 1, (f, 128, 16))
-    def wsel(out, k, src, lo, n, first=()):
-        mms(acc(out, list(first) + [(Y(k, r), a(src, lo + r, lo + n, 16)) for r in range(16)]))
+    def wsel(out, k, src, lo, n, first=(), start=True, to=range(16)):
+        mms(acc(out, list(first) + [(Y(k, to[r]), a(src, lo + r, lo + n, 16)) for r in range(16)], start))
+    TD, TS, TH = a("TT", 0, 512), a("TT", 512, 1024), a("TT", 1024, 1536)
+    TC, IOB = a("TB", 0, 512), a("TB", 512, 1024)
 
     for h in range(2):
         dma("a", a("BXI", 16 * h, 16 * h + 16), T.bx[:], 8)
-    dma("s", a("SBI", 0, 512), T.sb[:], 256)
-    for b in range(8):
-        dma("s" if b & 1 else "a", a("SBI", 512, 1024, 1, (16 * b, 16 * b + 16)), T.sb[16 * (b ^ 1):16 * (b ^ 1) + 16, :], 32)
-    dma("s", a("NI", 256, 512), T.he[:], 128)
     dma("s", a("X", 0, 4096), T.xs[:], 1024)
-    dma("a", a("MSG", 0, 256), T.zs[:], 64)
-    dma("s", a("NI", 0, 256), T.pe[:], 128)
+    dma("a", a("NI", 256, 512), T.he[:], 128)
+    for k in range(16):
+        dma("sa"[k & 1], a("SBI", 512, 1024, 1, (k, 128, 16)), T.sb[ROW[k]:128:16, :], 16)
+    dma("s", a("SBI", 0, 512), T.sb[:], 256)
+    dma("a", a("NI", 0, 256), T.pe[:], 128)
+    for x in zlands(0): dma("a", x, T.zs[:], 64)
     dma("a", a("LI", 0, 2, 1, (0, 8)), T.lim[:], 1)
     iota(si(0, 1), [[0, 1]], 0, 1)
     iota(io5(0, 512), [[1, 512]], 0, 0)
-    iota(a("QR", 0, 256), [[1, 16], [0, 16]], 0, 0)
+    iota(a("QR", 0, 256), [[1, 4], [4, 4], [0, 16]], 0, 0)
     iota(a("QR", 256, 512), [[0, 16], [1, 16]], 0, 0)
     iota(a("E8", 0, 128, 1, (0, 8)), [[1, 128]], 0, -16)
     iota(a("IOS", 0, 1024), [[1, 64], [256, 16]], 0, 0)
-    for c in range(2):
-        iota(a("BE", 1024 * c, 1024 * c + 1024), [[0, 1024]], 0, 0)
-    for nm in ("X", "PQ"):
-        for c in range(4):
-            iota(a(nm, 4096 + 1092 * c, 5188 + 1092 * c), [[0, 1092]], 0, 0)
-    iota(io5(512, 1536), [[0, 1024]], 0, 0)
+    iota(KC, [[1, 16], [16, 4], [64, 4]], 0, 0)
+    iota(IOB, [[1, 512]], -256, 0)
+    iota(ONES, [[0, 256]], 1, 0)
+    iota(NIL, [[0, 128]], 0, 0)
+    iota(sub(wb(12), 0, 16), [[0, 16]], 0, 0)
+    for c in range(8):
+        iota(a("IOT", 1024 * c, 1024 * c + 1024), [[1, 1024]], 1024 * c, 0)
+    for c in range(4):
+        iota(a("X", 4096 + 1152 * c, 5248 + 1152 * c), [[0, 1152]], 0, 0)
+        iota(a("PQ", 4096 + 1024 * c, 5120 + 1024 * c), [[0, 1024]], 0, 0)
     iota(a("VR", 0, 768), [[0, 768]], 0, 0)
-    pf, pm, p16, pj, par = col("pf"), col("pm"), col("p16"), col("pj"), col("par")
+    iota(a("GB", 8192, 8208), [[0, 16]], 0, 0)
+    pf, pm, p16, par = col("pf"), col("pm"), col("p16"), col("par")
     nc = [0]
     def tmp():
         nc[0] += 1
@@ -184,371 +228,311 @@ def rank_program(g, core, T, topo):
     def c_(x, s1, f0, s2=None, f1=None):
         o = tmp(); ts(o, x, s1, f0, s2, f1); return o
     cp(pf, si(0, 1))
-    for o, m in ((pm, 15), (p16, 112), (pj, 7), (par, 16)):
+    for o, m in ((pm, 15), (par, 16)):
         cp(o, bit(m))
-    ms(col("m192"), -192.0); ms(col("p128"), 128.0)
+    tt(p16, pf, pm, A.subtract)
     i16 = io5(0, 16)
     ts(YM(0), io5(0, 144), c_(p16, 15.0, A.add), A.is_equal)
-    ts(I128, io5(0, 128), pf, A.is_equal)
+    ts(IF, io5(0, 128), pf, A.is_equal)
+    act(I128, IF); act(NEG, IF, scale=-1.0); act(HALF, IF, scale=0.5); act(LIM, IF, scale=-1020.0)
+    act(NF, IF, scale=-1.0); act(BIG, IF, scale=16384.0); act(NBIG, IF, scale=-16384.0)
     for c in range(2):
+        on = c_(par, 16.0 * c, A.is_equal)
         for h in range(2):
-            ts(MT(2 * c + h), io5(0, 128), c_(pf, 16.0 * (h - c), A.add), A.is_equal, c_(par, 16.0 * c, A.is_equal), A.mult)
-    ts(sub(CK, 0, 16, 2), io5(0, 8), 0.0, A.mult, c_(par, 128.0, A.mult), A.add)
-    ts(sub(CK, 1, 16, 2), sub(CK, 0, 16, 2), -1.0, A.mult, 2048.0, A.add)
+            ts(MF(2 * c + h), io5(0, 128), c_(pf, 16.0 * (h - c), A.add), A.is_equal, on, A.mult)
+            act(MT(2 * c + h), MF(2 * c + h), scale=1.0 / 16)
     par1 = c_(par, 1.0 / 16, A.mult)
     def flip(o):
         tp(a("BXF", 32, 64), a("BXF", 0, 32))
         tt(o, a("BXF", 48, 64), a("BXF", 32, 48), A.subtract); ts(o, o, par1, A.mult); tt(o, o, a("BXF", 32, 48), A.add)
     cp(a("BXF", 0, 32), a("BXI", 0, 32)); flip(sm("b0"))
-    cp(a("MSG", 272, 288), sm("b0")); tt(a("MSG", 288, 304), sm("b0"), a("MSG", 272, 288), A.subtract)
-    ms(a("MSG", 256, 272), 0.0)
-    cp(t5(3), a("SBI", 0, 512)); act(a("TS", 0, 512), t5(3), scale=1.0 / 512)
-    ts(a("TS", 2048, 2560), a("SBI", 512, 1024), 1.0 / 512, A.mult)
-    iW, i256, d512, d8k = sm("iW"), sm("i256"), sm("d512"), sm("d8k")
-    ts(iW, i16, 16.0, A.mult, pm, A.add)
-    ts(li("reo"), i16, c_(pm, 16.0, A.mult), A.add)
-    ts(li("exp"), i16, 16.0, A.mult, 15.0, A.add)
-    ts(li("bd"), i16, 128.0, A.mult, pf, A.add)
-    act(d512, iW, bias=512.0); act(d8k, iW, bias=8208.0); act(i256, iW, bias=256.0); act(sm("d4k"), iW, bias=4096.0)
+    for h in range(2): cp(a("BOX", 16 * h, 16 * h + 16), sm("b0"))
+    cp(TS, a("SBI", 512, 1024))
+    d512, dW, q16 = sm("d512"), sm("dW"), sm("q16")
+    ts(d512, i16, 16.0, A.mult, c_(pm, 512.0, A.add), A.add)
+    act(dW, d512, bias=SPARE - 512.0); act(q16, i16, scale=1.0 / 16)
+    iota(sm("row"), [[1, 4], [4, 4]], 0, 0)
+    ts(li("reo"), sm("row"), c_(pm, 16.0, A.mult), A.add)
     qk, rk = a("QR", 0, 256), a("QR", 256, 512)
-    act(KC, qk, scale=1.0 / 16)
-    act(NEG, I128, scale=-1.0)
-    act(a("IF", 0, 128), I128, scale=512.0); act(a("IF", 128, 256), I128, scale=-512.0)
+    act(KC, KC, scale=1.0 / 256)
     RST = a("RST", 0, 256)
     act(RST, rk, F.Relu, scale=-65536.0, bias=65536.0)
-    ts(TRI, i16, pm, A.is_ge, -64.0, A.mult)
-    ms(a("BD", 0, 2048), 0.0)
+    ts(LUT, qk, pm, A.not_equal, -2048.0, A.mult)
+    act(IDT, io5(0, 256), scale=2.0 ** -18)
+    ms(a("DD", 0, 2048), 0.0)
     for o in (a("PQ", 0, 2048), a("PQ", 2048, 4096)):
-        dma("s", o, a("BD", 0, 2048), 512)
-    ms(sub(w(0, 272), 256, 272), 0.0); ms(sub(w(6, 272), 0, 8), 0.0)
-    pw = None
-    for b in range(4):
-        x = c_(c_(bit(1 << b), 0.0, A.is_gt, 2.0 ** -(1 << b) - 1.0, A.mult), 1.0, A.add)
-        pw = x if pw is None else c_(x, pw, A.mult)
-    lo9 = c_(pm, 9.0, A.is_lt)
-    for (n, mul, dst, msk) in ((512, 1.0, a("WB", 0, 512), lo9), (32, 512.0, sm("hb", 32), c_(pm, 14.0, A.is_lt, lo9, A.subtract))):
-        tm = a("T5", 512, 512 + n); ti = a("WI", 512, 512 + n)
-        act(tm, io5(0, n), scale=mul, bias=0.5)
-        ts(ti, tm, pw, A.mult, -0.5, A.add)
-        ts(ti, ti, 1, A.bitwise_and)
-        ts(dst, ti, c_(msk, 2.0, A.mult), A.mult, msk, A.subtract)
-    for h in range(17):
-        o, bcol = a("BITS", 512 * h, 512 * h + 512), sub(sm("hb", 32), h, h + 1)
-        if h in BITS_ON_SCALAR: act(o, a("WB", 0, 512), bias=bcol)
-        else: ts(o, a("WB", 0, 512), bcol, A.add)
-    cp(a("LB", 512, 768), a("NI", 256, 512))
-    for k in range(2):
-        x = a("P7", 256 * k, 256 * k + 256)
-        cp(x, a("NI", 256 * k, 256 * k + 256)); cp(nb(2 * k), a("NI", 256 * k, 256 * k + 256)); tt(nb(2 * k + 1), x, nb(2 * k), A.subtract)
-    he = a("P7", 256, 512)
-    for f in range(4):
+        dma("s", o, a("DD", 0, 2048), 512)
+    ts(a("T5", 0, 128), io5(0, 128), p16, A.subtract, -7.5, A.add)
+    act(a("T5", 128, 256), a("T5", 0, 128), F.Abs)
+    ts(BLK, a("T5", 128, 256), 8.0, A.is_lt)
+    ts(sm("low"), i16, pm, A.is_gt, 2.0, A.mult); ts(sm("one"), i16, pm, A.is_equal, 2048.0, A.mult)
+    for r in range(16):
+        mul(r in LOW_ON_VECTOR, LOW(r), Y(0, r), sub(sm("low"), r, r + 1))
+        mul(r in SPREAD_ON_VECTOR, SPREAD(r), BLK, sub(sm("one"), r, r + 1))
+    cp(lb(2), a("NI", 256, 512))
+    ts(a("NB", 0, 512), a("NI", 0, 512), -256.0, A.add)
+    for f in range(2):
         dma("s", grp("PQ", f, 4096), nb(f), 64)
     p8 = None
-    for b in range(3):
-        x = c_(c_(bit(1 << b), 0.0, A.is_gt, 8.0 ** (1 << b) - 1.0, A.mult), 1.0, A.add)
+    for k in range(3):
+        x = c_(c_(bit(1 << k), 0.0, A.is_gt, 8.0 ** (1 << k) - 1.0, A.mult), 1.0, A.add)
         p8 = x if p8 is None else c_(x, p8, A.mult)
     r8 = tmp(); op("v", lambda: g.vector.reciprocal(ap(r8), ap(p8)), r8, [p8], 240)
-    m01 = c_(pm, 2.0, A.is_lt); m23 = c_(pm, 4.0, A.is_lt, m01, A.subtract)
-    w5 = c_(c_(pm, 4.0, A.is_equal, 1.0 / 1024, A.mult), c_(pm, 6.0, A.is_equal), A.add)
-    for k, wt in ((1, c_(pm, 1.0, A.add)), (2, r8), (3, m01), (4, c_(pm, 6.0, A.is_lt, m01, A.subtract)), (5, w5), (6, m23)):
+    one = [sub(sm("one"), k, k + 1) for k in range(4)]
+    m0 = c_(one[0], 1.0 / 2048, A.mult); m1 = c_(one[1], 1.0 / 2048, A.mult)
+    for k, wt in ((1, c_(pm, 1.0, A.add)), (2, c_(r8, 128.0, A.mult)), (3, m0), (4, m1), (5, c_(one[2], 1.0 / 2048, A.mult, m1, A.add)),
+                  (6, c_(one[3], 1.0 / 2048, A.mult)), (7, c_(c_(one[1], 128.0, A.mult), c_(one[0], 0.125, A.mult), A.add))):
         act(YM(k), YM(0), scale=wt)
-    act(ME, I128, scale=m01); ts(MF, io5(0, 128), c_(pf, 2.0, A.add), A.is_equal, m01, A.mult)
-    ts(a("T5", 1024, 1152), io5(0, 128), p16, A.subtract, 0.0, A.is_ge)
-    ts(a("T5", 1152, 1280), io5(0, 128), p16, A.subtract, 16.0, A.is_lt)
-    tt(BLK, a("T5", 1024, 1152), a("T5", 1152, 1280), A.mult)
+    act(ME, I128, scale=m0); ts(MG, io5(0, 128), c_(pf, 1.0, A.add), A.is_equal, m0, A.mult)
     e8 = a("E8", 0, 128, 1, (0, 8)); e9 = a("E8", 128, 256, 1, (0, 8))
     ts(e9, e8, 0.0, A.is_ge); ts(e8, e8, 16.0, A.is_lt); tt(e8, e8, e9, A.mult)
     cp(a("LF", 0, 2, 1, (0, 8)), a("LI", 0, 2, 1, (0, 8)))
-    mms(acc(a("P3", 128, 130), [(e8, a("LF", 0, 2, 1, (0, 8)))]))
+    mms(acc(b("P5", 8, (0, 2)), [(e8, a("LF", 0, 2, 1, (0, 8)))]))
     thr = sm("thr", 32)
-    cp(col("lim0"), a("P3", 128, 129)); cp(col("jl"), a("P3", 128, 129)); ts(col("sl"), a("P3", 129, 130), 1.0, A.add)
-    ts(sub(thr, 0, 16), i16, 0.0, A.mult, col("sl"), A.add); ms(sub(thr, 16, 32), 1009.0)
-    ms(col("A"), 0.0); act(col("nl0"), col("lim0"), scale=-1.0)
-    j7 = c_(pj, 7.0, A.is_equal)
-    for t in range(S):
-        act(col("cd%d" % t), j7, scale=-8.0 if 4 <= t + 1 < 8 else 0.0, bias=(t + 1 if t < 7 else 0) + (256 * t + 1) * 2.0 ** -21)
-    short = c_(j7, 4.0, A.mult, -3.5, A.add)
+    cp(col("lim0"), b("P5", 8, (0, 1))); ts(col("sl"), b("P5", 8, (1, 2)), 1.0, A.add, 1012.0, A.min)
+    ts(sub(thr, 0, 16), i16, 0.0, A.mult, col("sl"), A.add); ms(sub(thr, 16, 32), 1012.0)
+    ms(si(6, 1), 0)
     for h in range(2):
-        ts(col("vs%d" % h), pm, 8.0, A.is_ge if h else A.is_lt, p8, A.mult); tt(col("vb%d" % h), col("vs%d" % h), short, A.mult)
-    act(a("V2", 1024, 1536), io5(0, 512), scale=0.0, bias=col("vb0"))
-    ts(a("P6", 0, 256), qk, pm, A.is_equal); ts(a("T5", 1280, 1536), rk, pm, A.is_equal)
-    tt(a("LUT", 0, 256), a("P6", 0, 256), a("T5", 1280, 1536), A.max)
-    ms(a("LUT", 256, 264), 0.0); ms(a("LUT", 264, 265), 1020.0); ms(a("LUT", 265, 272), -1.0)
+        ts(col("vs%d" % h), pm, 8.0, A.is_ge if h else A.is_lt, p8, A.mult)
 
     cp(a("SBU", 0, 512), a("SBI", 0, 512))
     for c in range(4):
-        win = a("IOS", 512 + 512 * c, 1024 + 512 * c) if c else t5(3)
-        if c: act(win, t5(3), bias=-64.0 * c)
+        win = a("IOS", 512 + 512 * c, 1024 + 512 * c) if c else TS
+        if c: act(win, TS, bias=-64.0 * c)
         tt(a("G1", 1024 * c, 1024 * c + 1024), ind(win, a("LB", 512 + 64 * c, 576 + 64 * c)), a("IOS", 0, 1024), A.is_equal)
-        wsel(a("P4", 64 * c, 64 * c + 64), 1, "G1", 1024 * c, 1024)
-        wsel(a("P4", 256 + 64 * c, 320 + 64 * c), 2, "G1", 1024 * c, 1024)
-    kh, sc = a("P4", 0, 256), a("P4", 256, 512)
-    ts(nb(4), kh, 0.0, A.is_equal, 1024.0, A.mult); ts(nb(5), kh, 9.0, A.is_ge, 512.0, A.mult); cp(nb(6), sc)
-    for f in range(4, 7):
+        wsel(P(0, 4 * c, 4 * c + 4), 1, "G1", 1024 * c, 1024)
+        wsel(P(0, 16 + 4 * c, 20 + 4 * c), 2, "G1", 1024 * c, 1024)
+    kh, sc = P(0, 0, 16), P(0, 16, 32)
+    ts(nb(2), kh, 9.0, A.is_ge, 512.0, A.mult); cp(nb(3), sc)
+    for f in range(2, 4):
         dma("s", grp("PQ", f, 4096), nb(f), 64)
-    act(nf(0), kh, scale=512.0, bias=-512.0); tt(nf(0), he, nf(0), A.add)
-    act(a("P6", 256, 512), nb(4), scale=8.0); tt(nf(0), a("P6", 256, 512), nf(0), A.max)
-    cp(a("LB", 768, 1024), nf(0))
-    ms(a("GB", 8192, 8208), 0.0)
+    act(nf(0), kh, scale=512.0, bias=-512.0); tt(nf(0), nf(0), a("NI", 256, 512), A.add)
+    ts(nf(1), kh, 0.0, A.is_equal, 8192.0, A.mult); tt(nf(0), nf(0), nf(1), A.max)
+    cp(lb(3), nf(0))
+    for c in range(8):
+        get(c in GB_ON_VECTOR, a("GB", 1024 * c, 1024 * c + 1024), ind(a("PQ", 0, 4096), a("SBU", 64 * c, 64 * c + 64)))
+        for bank, k in ((4, 5), (6, 6), (7, 4)):
+            wsel(P(bank, 4 * c, 4 * c + 4), k, "GB", 1024 * c, 1024, to=ROW)
+    act(TD, P(4, 0, 32), bias=256.0)
+    act(TC, P(6, 0, 32))
+    tt(t5(1), P(7, 0, 32), IOB, A.is_equal); act(t5(2), t5(1), scale=0.25, bias=LONG + 256.0); tt(TH, P(7, 0, 32), t5(2), A.add)
 
-    def tables():
-        for c in range(8):
-            o, i = a("GB", 1024 * c, 1024 * c + 1024), ind(a("PQ", 0, 4096), a("SBU", 64 * c, 64 * c + 64))
-            if c in GB_ON_VECTOR: cp(o, i)
-            else: act(o, i)
-            wsel(a("P4", 64 * c, 64 * c + 64), 4, "GB", 1024 * c, 1024)
-            wsel(a("P5", 64 * c, 64 * c + 64), 5, "GB", 1024 * c, 1024)
-            wsel(a("P0", 64 * c, 64 * c + 64), 6, "GB", 1024 * c, 1024)
-        cp(a("TT", 0, 512), a("P4", 0, 512))
-        act(a("TT", 512, 1024), a("P5", 0, 512))
-        act(a("P5", 0, 512), a("P0", 0, 512), scale=1.0 / 512, bias=8.0); tt(a("TT", 1024, 1536), a("P5", 0, 512), a("TS", 0, 512), A.subtract)
-        tt(t5(1), a("P0", 0, 512), io5(0, 512), A.is_equal); act(a("TT", 1536, 2048), t5(1), scale=4096.0)
-        for b in range(8):
-            dma("s", a("TT", 2048, 4096, 1, (16 * b, 16 * b + 16)), a("TT", 0, 2048, 1, (16 * (b ^ 1), 16 * (b ^ 1) + 16)), 128)
+    def lowest(keys, own, on, out):
+        for q in range(16):
+            ts(b("E", q, (0, 256 - 16 * q)), sub(keys, 16 * q, 256), own(q), A.is_equal, sub(on, q, q + 1), A.mult)
+            if q < 15: mms([(P(3, q + 1, 16), BLK, b("E", q, (16, 256 - 16 * q)), q == 0, q == 14)])
+        mms(acc(out, [(LOW(r), b("E", (0, 16), r)) for r in range(1, 16)], True, False))
+        act(sub(wb(12), 16, 256), P(3, 1, 16))
+        wsel(out, 0, "WB", 256 * 12, 256, start=False)
 
-    tables()
+    def spread(bank, lo, x):
+        return [(b("P%d" % bank, (lo, lo + 16), r), SPREAD(r), x, False, False) for r in range(16)]
 
-    def gram(bd, bb, cnt):
-        for n_, qs in enumerate(GRAM):
-            P = "P%d" % (6 + (n_ & 1)); at_ = 0; pos = []; items = []
-            for q in qs:
-                lh = a(bd, 128 * q, 128 * q + 128)
-                if q: items += acc(a(P, at_, at_ + 16 * q), [(lh, a(bb, 0, 16 * q))])
-                items += acc(a(P, at_ + 16 * q, at_ + 16 * q + 16), [(I128, TRI), (lh, a(bb, 16 * q, 16 * q + 16))])
-                pos.append((q, at_)); at_ += 16 * q + 16
-            mms(items)
-            for q, at_ in pos:
-                act(a("JK", 8 * q * (q + 1), 8 * (q + 1) * (q + 2)), a(P, at_, at_ + 16 * q + 16), F.Relu, bias=-13.0 * 16384, scale=16384.0, acc=sub(cnt, q, q + 1))
-
-    XW = a("X", 0, 8464)
-    def zof(u): return a("MSG", MW * u, MW * u + 256)
+    XW = a("X", 0, XC)
+    def zof(u, h=0): return a("MSG", MW * u + 256 * h, MW * u + 256 * h + 256)
     def lst(t, k): return sub(li("up%d" % t, 64), 16 * k, 16 * k + 16)
 
     def updates(t):
-        if t >= 1: cp(ind(XW, lst(t - 1, 1 if t < S - 1 else 0)), zof(t - 1))
-        if t >= 2: cp(ind(XW, lst(t - 2, 2)), zof(t - 2))
-        cp(ind(XW, lst(t, 3)), wb(7))
-        cp(ind(XW, lst(t, 0)), wb(1) if t < S - 1 else zof(t))
-        if t < S - 1: cp(ind(a("PQ", 0, 8464), lst(t, 3)), wb(9))
+        if t >= 1: cp(ind(XW, lst(t - 1, 2 if 1 < t < S - 1 else 1)), zof(t - 1))
+        if t >= 3: cp(ind(XW, lst(t - 2, 3)), zof(t - 2))
+        cp(ind(XW, lst(t, 0)), wb(7))
+        cp(ind(XW, lst(t, 1)), wb(1) if t < S - 1 else zof(t))
+        if t < S - 1: cp(ind(a("PQ", 0, 8192), lst(t, 0)), wb(9))
 
     sent = None
     marks = []
     for t in range(S):
         marks.append(len(ops))
-        M0 = MW * t
-        z = zof(t); ou = a("MSG", M0 + 256, M0 + 272); ah = a("MSG", M0 + 272, M0 + 288); al = a("MSG", M0 + 288, M0 + 304)
+        z = zof(t); aU = a("BOX", 32 * t, 32 * t + 16); msg = a("BOX", 32 * t + 16, 32 * t + 32)
         XT = XW if t else a("X", 0, 4096)
-        if t: arrival(t, sent)
-        items = []
-        for c in range(2):
-            items += acc(a("P3", c, 16, 2), [(I128, sub(CK, c, 16, 2))] + [(MT(2 * c + h), sub(x, h, 16, 2)) for h in range(2) for x in (ah, al)])
-        mms(items)
-        sw = li("sw")
-        cp(sw, a("P3", 0, 16))
-        def tw(j): return ind(a("TT", 512 * j, 512 * j + 2560), sw)
-        def rr(j): return a("RR", 256 * j, 256 * j + 256)
-        ts0 = ind(a("TS", 0, 2560), sw)
-        cc = w(0)
-        aW = sm("aW", 32); kb, a1 = sub(aW, 0, 16), sub(aW, 16, 32)
-        ac, nac = sm("ac"), sm("nac")
         if t:
-            if FIRST_ON_SCALAR: act(rr(4), tw(0))
-            else: cp(rr(4), tw(0))
-            tp(a("TR", 0, 256), rr(4)); cp(a("LB", 0, 256), a("TR", 0, 256))
-            act(a("RB", 0, 256), tw(1)); act(rr(0), tw(2)); act(rr(1), ts0); act(a("RB", 256, 512), tw(3))
+            arrival("arr", t, zlands(t), sent[1]); arrival("box", t, blands(t), sent[0])
+            cp(lb(0), ind(TD, aU))
+            act(wb(13), ind(TC, aU)); act(w(1), ind(TS, aU)); act(w(2), ind(TH, aU))
         else:
-            cp(rr(0), ts0); tp(cc, rr(0))
-        tt(a1, ah, al, A.add)
-        ts(ac, ou, 0.0, A.is_equal); ts(nac, ou, 0.0, A.is_gt, 4096.0, A.mult)
-        tt(kb, nac, d512, A.min); tt(kb, kb, a1, A.max)
-        kbU = li("kb", 32); cp(kbU, sub(aW, 0, 32)); aU = sub(kbU, 16, 32)
-        act(a("BB", 0, 256), ind(a("BITS", 0, 768), sub(kbU, 0, 16)))
-        for h in range(2): act(a("ZZ", 512 + 256 * h, 768 + 256 * h), z)
+            act(w(1), ind(TS, aU))
+        mf, thA, ab, base, a3 = sm("mf"), sh("thA"), sh("ab"), sm("base"), sm("a3")
+        cp(mf, msg); ts(thA, msg, 512.0, A.is_lt, 1012.0, A.mult); ts(ab, aU, -256.0, A.add)
+        if t:
+            ts(base, msg, 512.0, A.is_ge, -512.0, A.mult); tt(base, base, mf, A.add)
+            if t == S - 1: ts(sm("t0"), base, 512.0, A.is_ge, -512.0, A.mult); tt(base, base, sm("t0"), A.add)
+        else: base = mf
+        ts(a3, aU, 256.0, A.mult); tt(a3, a3, i16, A.subtract)
+        act(wb(14), ind(IOB, aU))
+        T2 = b("T2", (0, 16), (0, 16)); XD = b("XD", (0, 16), (0, 16))
         if t:
             for Q in range(4):
                 for c in (2 * Q, 2 * Q + 1):
-                    (cp if c in DIGITS_ON_VECTOR else act)(a("G1", 512 * c, 512 * c + 512), ind(a("V2", 0, 1536), a("LB", 32 * c, 32 * c + 32)))
-                wsel(a("P0", 64 * Q, 64 * Q + 64), 0, "G1", 1024 * Q, 1024)
+                    get(c in DIGITS_ON_VECTOR, a("G1", 512 * c, 512 * c + 512), ind(a("V2", 0, 1024), a("LB", 32 * c, 32 * c + 32)))
+                wsel(P(0, 4 * Q, 4 * Q + 4), 0, "G1", 1024 * Q, 1024)
             updates(t - 1)
-            tp(a("RB", 512, 1024), a("RB", 0, 512)); tp(a("P4", 0, 512), a("RR", 0, 512))
-            wi = a("WI", 512, 768); lgp = a("P5", 256, 512)
-            tt(w(1), a("P0", 0, 256), a("RB", 512, 768), A.mult)
-            ts(wi, w(1), 0.5, A.add); ts(wi, wi, 7, A.bitwise_and)
-            tt(w(1), a("P4", 0, 256), wi, A.add); ts(lgp, wi, 1.0, A.not_equal)
-            tt(w(1), lgp, w(1), A.mult); tt(cc, a("P4", 256, 512), w(1), A.add)
-        cU = a("LB", 256, 512)
-        ts(cU, ind(cc, li("reo")), 512.0, A.mult)
-        cp(ind(a("BD", 0, 2048), li("bd")), a("BB", 0, 256))
-        if t:
-            ops[-1]["early"] = EARLY
-            gram("BD", "BB", sm("cb"))
-        for c in range(8):
-            dd, ad, src = a("DD", 512 * c, 512 * c + 512), a("AD", 512 * c, 512 * c + 512), ind(XT, sub(cU, 32 * c, 32 * c + 32))
-            if c < NA:
-                act(dd, src)
-                mms(acc(a("P2", 0, 512), [(I128, dd), (NEG, a("ZZ", 512, 1024))]))
-                act(ad, a("P2", 0, 512), F.Abs)
+            wi = a("WI", 0, 256)
+            if t < S - 1:
+                tt(wi, P(0, 0, 16), wb(13), A.mult)
             else:
-                tt(dd, src, a("ZZ", 512, 1024), A.subtract)
-                act(ad, dd, F.Abs)
+                tt(w(3), P(0, 0, 16), wb(13), A.mult); ts(wi, w(3), -0.24, A.add)
+            ts(wi, wi, 7, A.arith_shift_right, 7, A.bitwise_and)
+            ts(XD, wi, 8192.0, A.mult)
+            mms([(P(7, 0, 16), IF, w(1), True, False)])
+            mms([(P(7, 0, 16), I128, XD, False, True)])
+            tt(T2, P(7, 0, 16), w(2), A.min)
+        else:
+            act(T2, w(1))
+        mms([(P(1, 0, 16), NIL, KC, True, False)])
+        if t: mms([(P(1, c, 16, 2), MT(2 * c + h), b("XD", (h, 16, 2), (0, 16)), False, False) for c in range(2) for h in range(2)])
+        mms([(P(1, c, 16, 2), MF(2 * c + h), b("T2", (h, 16, 2), (0, 16)), False, c + h == 2) for c in range(2) for h in range(2)])
+        cc = w(0)
+        tp(cc, P(1, 0, 16))
+        cU = lb(1)
+        cp(cU, ind(cc, li("reo")))
+        RN = w(9)
+        if t: ts(RN, cc, 1.5 * 2 ** 23, A.add, -1.5 * 2 ** 23, A.add)
+        else: act(RN, cc)
+        key, dl = a("P2", 0, 256), a("P2", 256, 512)
+        mms([(dl, IF, RN, True, False), (sub(dl, 0, 255), NF, sub(RN, 1, 256), False, False), (sub(dl, 15, 255, 16), IF, sub(RN, 16, 256, 16), False, True)])
+        mms(acc(key, ([(BIG, cc), (NBIG, RN)] if t else []) + [(I128, KC)], True, False))
+        lowest(wb(14), lambda q: sub(ab, q, q + 1), thA, P(4, 0))
+        for c in range(8):
+            tt(a("DD", 512 * c, 512 * c + 512), ind(XT, sub(cU, 32 * c, 32 * c + 32)), a("MSG", MW * t, MW * t + 512), A.subtract)
+            for k in (2 * c, 2 * c + 1):
+                act(b("AD%d" % (k >> 2), (0, 16), k & 3, (0, 16)), a("DD", 256 * k, 256 * k + 256), F.Abs)
             if c & 1:
                 Q = c >> 1
-                wsel(a("P1", 64 * Q, 64 * Q + 64), 0, "AD", 1024 * Q, 1024, [(I128, sub(KC, 64 * Q, 64 * Q + 64))])
-        dl = a("P0" if t else "P2", 256, 512)
-        mms(acc(dl, [(a("IF", 0, 128), cc), (a("IF", 128, 256), sub(w(0, 272), 1, 257))]))
-        act(w(3), a("P1", 0, 256))
-        if t == 0: gram("BD", "BB", sm("cb"))
-        if t:
-            mms(acc(a("P2", 0, 256), [(Y(0, k), a("AD", 256 * k, 256 * k + 256)) for k in range(16)]))
-            tt(w(2), lgp, a("RB", 768, 1024), A.mult)
-        nx = sm("nx"); act(nx, sub(w(0, 272), 16, 272, 16), scale=512.0)
-        key = w(5); mn = sub(w(6, 272), 8, 264)
-        if t: tt(key, ind(w(3), li("reo")), w(2), A.add)
-        else: cp(key, ind(w(3), li("reo")))
+                mms(acc(sub(key, Q, 256, 4), [(Y(0, r), b("AD%d" % Q, (0, 16), (0, 4), r)) for r in range(16)], False, Q == 3))
+        mn = a("MN", 0, 256); m12 = a("MN", 15, 512, 16)
         scan(mn, RST, key, A.add, A.min)
-        tt(w(7), ind(mn, li("exp")), key, A.not_equal)
+        tt(w(7), mn, key, A.not_equal)
         scan(w(8), w(7), dl, A.mult, A.add)
-        ef = sm("ef", 32); m12 = sm("m12", 32)
-        e, f = sub(ef, 0, 16), sub(ef, 16, 32); m1, m2 = sub(m12, 0, 16), sub(m12, 16, 32)
-        efU = li("efU", 32); eU, fU = sub(efU, 0, 16), sub(efU, 16, 32)
-        tt(e, sub(w(8), 15, 256, 16), nx, A.add)
-        cl, kc = sm("cl"), sm("kc")
-        tt(m1, sub(mn, 15, 256, 16), nac, A.add)
-        ts(kc, m1, 1009.0, A.is_ge, 16384.0, A.mult); tt(kc, kc, d8k if t else sm("d4k"), A.min); tt(kc, kc, e, A.max); cp(li("kc"), kc)
-        act(a("BC", 0, 256), ind(a("BITS", 0, 8464 if t else 4352), li("kc")))
-        cp(ind(a("BE", 0, 2048), li("bd")), a("BC", 0, 256))
-        gram("BE", "BC", sm("cc"))
-        ts(cl, m1, 1009.0, A.is_lt)
-        if t: act(w(12), a("P2", 0, 256))
-        if t: act(a("P4", 0, 256), key)
-        tt(w(9), a("P4", 0, 256) if t else key, sub(w(6, 272), 7, 263), A.max)
-        ms(sub(w(9), 0, 256, 16), 65536.0)
-        scan(w(10), RST, w(9), A.add, A.min)
-        tt(w(1), ind(w(10), li("exp")), key, A.not_equal)
-        scan(w(4), w(1), dl, A.mult, A.add)
-        tt(f, sub(w(4), 15, 256, 16), nx, A.add)
-        cp(eU, e); cp(fU, f)
-        PT = a("PQ", 0, 8464 if t else 4096)
-        act(wb(10), ind(PT, eU)); act(wb(11), ind(PT, fU))
-        act(wb(0), z, bias=col("m192"))
-        less = [(NEG, ah), (NEG, al)]
-        wsel(a("P3", 32, 48), 3, "WB", 256 * 10, 256, less); wsel(a("P3", 64, 80), 6, "WB", 256 * 10, 256, less); wsel(a("P3", 80, 96), 6, "WB", 256 * 11, 256, less)
-        d1, xe, xf = wb(2), wb(8), wb(3)
-        (act if XE_ON_SCALAR else cp)(xe, ind(XT, eU)); (act if XF_ON_SCALAR else cp)(xf, ind(XT, fU))
-        tt(d1, xe, z, A.subtract)
-        ts(wb(4), d1, 0.5, A.mult, 191.75, A.add)
-        tt(a("ZZ", 256, 512), wb(4), wb(0), A.add)
-        act(a("ZZ", 0, 256), d1, F.Abs)
-        tt(wb(5), xe, xf, A.subtract)
-        act(wb(6), wb(5), F.Abs)
-        wsel(a("P1", 256, 272), 0, "WB", 256 * 6, 256)
-        if t < S - 1: act(wb(1), z, bias=col("p128"))
-        act(w(11), ind(a("VR", 0, 768), aU))
-        act(w(13), io5(0, 256), scale=2.0 ** -21, bias=col("cd%d" % t))
-        tt(wb(7), xe, xf, A.max)
-        if t: act(a("P5", 0, 256), w(11))
-        act(m2, sub(w(10), 15, 256, 16))
-        lg = sm("lg", 32); ts(lg, ef, 4096.0, A.is_ge); lge = sub(lg, 0, 16)
-        on = sm("on"); act(on, ou, F.Relu, bias=-1.0)
-        ix = sm("ix"); act(ix, cl, scale=-512.0, bias=512.0); tt(ix, ix, iW, A.add)
-        ts(si(2, 32), m12, 16.0, A.mult); ts(si(2, 32), si(2, 32), 15, A.bitwise_and)
-        kk = sm("kk"); ts(kk, si(2), 16.0, A.mult, -256.0, A.add); tt(kk, kk, si(3), A.add)
-        Pa, Qa, dx = a("P3", 32, 48), a("P3", 64, 96), sm("dx")
-        ts(dx, Pa, 0.0, A.is_equal); tt(dx, sub(Qa, 0, 16), dx, A.mult); tt(dx, Pa, dx, A.add)
-        hm = sm("hm", 32); ts(hm, Qa, 0.0, A.is_equal)
-        st = sm("st"); act(st, lge, bias=1.0)
-        tk = sm("tk")
-        tt(tk, cl, sm("cc"), A.is_gt)
-        tt(sm("t3"), tk, i256, A.mult); tt(sm("t3"), sm("t3"), ix, A.max); cp(li("ix"), sm("t3"))
-        O0 = MW * t
-        cp(a("OUT", O0, O0 + 256), ind(a("ZZ", 0, 768), li("ix")))
-        tt(dx, dx, tk, A.mult); tt(dx, dx, a1, A.add)
-        cp(a("OUT", O0 + 272, O0 + 288), dx); tt(a("OUT", O0 + 288, O0 + 304), dx, a("OUT", O0 + 272, O0 + 288), A.subtract)
-        tt(st, st, tk, A.mult); tt(a("OUT", O0 + 256, O0 + 272), st, on, A.add)
-        sent = (send(t, "box", 272, MW), send(t, "arr", 0, 272))
-        sw_, vo, jn = sm("ms"), sm("vo"), a("SH", 0, 16)
-        tt(sw_, ac, sm("cb"), A.is_gt); tt(vo, sm("cb"), d512, A.min); tt(vo, vo, kb, A.max); cp(li("vo"), vo)
-        r12 = sm("r12", 32)
+        e = sub(w(8), 15, 256, 16)
+        eU, cl = li("eU"), sm("cl")
+        cp(eU, e)
+        tt(cl, sub(mn, 15, 256, 16), thA, A.is_lt)
+        cp(lb(4), ind(a("IOT", 0, 8192 if t else 4096), eU))
+        tt(sub(w(3), 1, 256), sub(key, 1, 256), sub(mn, 0, 255), A.max)
+        scan(a("MN", 257, 512), sub(RST, 0, 255), sub(w(3), 1, 256), A.add, A.min)
+        lowest(lb(4), lambda q: sub(w(8), 16 * q + 15, 16 * q + 16), cl, P(4, 1))
+        kq = si(2, 32)
+        ts(kq, m12, 256.0, A.mult); ts(kq, kq, 255, A.bitwise_and)
+        ts(li("dU", 32), kq, 16.0, A.mult, pm, A.add); cp(li("kU", 32), kq)
+        tt(sm("gb"), si(3), a3, A.add); ts(li("gb"), sm("gb"), 1.0 / 16, A.mult)
+        d1, d2 = wb(2), wb(3)
+        act(wb(10), ind(a("PQ", 0, 8192 if t else 4096), eU))
+        act(d1, ind(a("DD", 0, 4096), sub(li("dU", 32), 0, 16)))
+        act(zof(t, 2), d1, F.Abs)
+        mms(acc(P(7, 0, 16), [(I128, z), (HALF, d1)]))
+        act(wb(4), P(7, 0, 16), bias=191.75)
+        if TAKE_ON_VECTOR: ts(zof(t, 3), wb(4), -192.0, A.add)
+        else: act(zof(t, 3), wb(4), bias=-192.0)
+        less = [(NEG, ab)]
+        wsel(P(5, 0), 3, "WB", 256 * 10, 256, less); wsel(P(5, 1), 4, "WB", 256 * 10, 256, less)
+        lge = sh("lge"); dx = sm("dx")
+        ts(dx, P(5, 0), 0.0, A.is_equal); tt(dx, P(5, 1), dx, A.mult); tt(dx, P(5, 0), dx, A.add)
+        if t: ts(lge, e, 4096.0, A.is_ge)
+        if t == 0: act(dx, dx, bias=512.0)
+        elif t < S - 1: act(sm("st"), lge, scale=512.0, bias=512.0); tt(dx, dx, sm("st"), A.add)
+        clq, ed, tk = sm("clq"), sm("ed"), sm("tk")
+        tt(clq, cl, q16, A.add); tt(ed, e, dW, A.subtract)
+        tt(tk, cl, P(4, 1), A.is_gt)
+        tt(dx, dx, tk, A.mult); tt(dx, dx, base, A.add)
+        ts(a("BOXO", 32 * t, 32 * t + 16), dx, 511.0, A.min); cp(a("BOXO", 32 * t + 16, 32 * t + 32), dx)
+        tt(clq, clq, tk, A.add); ts(li("ix"), clq, 256.0, A.mult, pm, A.add)
+        get(OUT_ON_VECTOR, a("OUT", 256 * t, 256 * t + 256), ind(a("MSG", MW * t + 256, MW * t + 1024), li("ix")))
+        sent = (send("box", t + 1, a("BOXO", 32 * t, 32 * t + 32), blands(t + 1)), send("arr", t + 1, a("OUT", 256 * t, 256 * t + 256), zlands(t + 1)))
+        act(d2, ind(a("DD", 0, 4096), sub(li("dU", 32), 16, 32)))
+        act(wb(11), ind(a("GB", 0, 8192), li("gb")))
+        wsel(P(5, 2), 4, "WB", 256 * 11, 256, less)
+        mms(acc(P(0, 0, 16), [(I128, d1), (NEG, d2)]))
+        act(wb(6), P(0, 0, 16), F.Abs)
+        wsel(P(5, 3), 0, "WB", 256 * 6, 256)
+        mms(acc(P(0, 16, 32), [(I128, z), (HALF, d1), (HALF, d2), (HALF, wb(6))]))
+        act(wb(7), P(0, 16, 32))
+        if t < S - 1: act(wb(1), z, bias=128.0)
+        sw, vo, jn = sh("sw"), sm("vo"), sh("jn")
+        tt(sw, thA, P(4, 0), A.is_gt); tt(vo, mf, d512, A.subtract); tt(vo, vo, sw, A.mult); tt(vo, vo, d512, A.add); cp(li("vo"), vo)
+        r12, hm, t1 = sh("r12", 32), sh("hm", 32), sh("t1")
         tt(r12, m12, thr, A.is_lt)
-        if t: cp(li("sp"), sub(r12, 0, 16))
-        tt(hm, hm, lg, A.is_gt); tt(hm, hm, r12, A.mult)
-        ts(sm("t1"), a("P1", 256, 272), col("jl"), A.is_lt); tt(sm("t1"), sm("t1"), sw_, A.mult)
-        tt(sm("t2"), sub(hm, 0, 16), sub(hm, 16, 32), A.mult); tt(jn, sm("t1"), sm("t2"), A.mult)
-        tt(kk, kk, jn, A.mult); ts(li("kk"), kk, 256.0, A.add)
-        tt(w(7), ind(a("LUT", 0, 264), li("kk")), w(13), A.mult)
+        ts(hm, P(5, 1, 3), 0.0, A.is_equal)
+        ts(t1, P(5, 3), col("jl") if t else col("lim0"), A.is_lt)
+        mms(acc(P(5, 4), [(I128, x) for x in (sub(r12, 0, 16), sub(r12, 16, 32), sub(hm, 0, 16), sub(hm, 16, 32), sw)] + ([(NEG, lge)] if t else []) + [(I128, t1)]))
+        ts(jn, P(5, 4), 6.0, A.is_equal)
+        act(wb(5), ind(LUT, sub(li("kU", 32), 0, 16))); act(wb(8), ind(LUT, sub(li("kU", 32), 16, 32)))
         if t:
-            tt(w(8), ind(a("LUT", 264, 272), li("sp")), w(12), A.is_lt)
-            tt(w(11), a("P5", 0, 256), w(8), A.mult)
-        tt(ind(a("VR", 0, 768), li("vo")), w(11), w(7), A.add)
+            items = acc(P(6, 0, 16), [(LIM, ONES)] + [(Y(0, ROW[k]), b("AD%d" % (k >> 2), (0, 16), k & 3, (0, 16))) for k in range(16)], True, False)
+            mms(items)
+            items = spread(6, 0, sub(r12, 0, 16)); items[-1] = items[-1][:4] + (True,)
+            mms(items)
+            act(w(4), ind(a("VR", 0, 512), aU))
+            tt(w(5), w(4), P(6, 0, 16), A.min)
+        mms(acc(P(6, 16, 32), [(I128, wb(5)), (I128, wb(8))], True, False))
+        mms(spread(6, 16, jn) + [(P(6, 16, 32), I128, IDT, False, True)])
+        act(w(6), P(6, 16, 32), F.Relu, bias=t + 1.0)
+        if t: tt(ind(a("VR", 0, 768), li("vo")), w(5), w(6), A.max)
+        else: cp(ind(a("VR", 0, 768), li("vo")), w(6))
         if t < S - 1:
             for h in range(2):
-                act(a("V2", 512 * h, 512 * h + 512), a("VR", 0, 512), bias=col("vb%d" % h), scale=col("vs%d" % h))
-        up = sm("up", 64); u0, u1, u2, u3 = (sub(up, 16 * k, 16 * k + 16) for k in range(4))
-        if t: tt(u0, sm("cc"), d8k, A.min); tt(u0, u0, kc, A.max)
-        else: tt(u0, cl, sm("cc"), A.is_le); tt(u0, u0, d8k, A.mult); tt(u0, u0, e, A.max); ms(sub(up, 16, 48), 0.0)
-        if t < S - 2:
-            tt(u1, lge, d8k, A.mult); tt(u2, d8k, u1, A.subtract); tt(u1, u1, u0, A.max); tt(u2, u2, u0, A.max)
-        act(sm("t4"), a1, bias=4096.0 + 512 * ((t + 2) & 7))
-        act(u3, jn, scale=-16384.0, bias=16384.0); tt(u3, u3, d8k, A.min); tt(u3, u3, sm("t4"), A.max)
-        cp(li("up%d" % t, 64), up)
-        ts(sub(li("yl", 128), 16 * t, 16 * t + 16), u3, 8192.0, A.min)
+                mul(h in V2_ON_VECTOR, a("V2", 512 * h, 512 * h + 512), a("VR", 0, 512), col("vs%d" % h))
+        up = sm("up", 64); u3, u0, u1, u2 = (sub(up, 16 * k, 16 * k + 16) for k in range(4))
+        tt(ed, ed, tk, A.mult); tt(u0, ed, dW, A.add)
+        nl = 4 if 0 < t < S - 2 else 2
+        if nl == 4: tt(u1, u0, dW, A.min); tt(u2, u0, dW, A.max)
+        act(sm("t4"), mf, bias=LONG + 512.0 * (t + 1))
+        tt(sm("t4"), sm("t4"), jn, A.mult); tt(u3, sm("t4"), dW, A.max)
+        cp(sub(li("up%d" % t, 64), 0, 16 * nl), sub(up, 0, 16 * nl))
+        ts(sub(li("yl", 128), 16 * t, 16 * t + 16), sm("t4"), float(ZERO), A.max)
         if t < S - 1:
-            mms(acc(a("P1", 256, 512), [(ME, wb(10)), (MF, wb(11))]))
-            act(wb(9), a("P1", 256, 512))
-            mms(acc(a("P3", 96, 112), [(BLK, jn)]))
-            act(a("JK", 2176, 2192), a("P3", 96, 112), acc=col("nj"))
-            ts(si(6, 1), col("nj"), 8.0, A.mult, col("A"), A.add); ts(si(6, 1), si(6, 1), 255, A.bitwise_and)
-            ts(col("jl"), si(6, 1), col("lim0"), A.add); act(col("A"), col("jl"), bias=col("nl0"))
+            mms(acc(P(7, 16, 32), [(ME, wb(10)), (MG, wb(11))]))
+            act(wb(9), P(7, 16, 32))
+            mms(acc(P(5, 5), [(BLK, jn)]))
+            act(a("JK", 0, 16), P(5, 5), scale=8.0, acc=col("nj"))
+            ts(si(6, 1), si(6, 1), col("nj"), A.add); ts(si(6, 1), si(6, 1), 255, A.bitwise_and)
+            ts(col("jl"), si(6, 1), col("lim0"), A.add)
 
-    ts(a("G1", 0, 512), a("VR", 0, 512), short, A.add, 2.0 ** 21, A.mult)
-    act(a("P4", 0, 512), a("VR", 0, 512), scale=2.0 ** 21, bias=c_(short, 2.0 ** 21, A.mult))
-    tt(t5(0), a("P4", 0, 512), a("G1", 0, 512), A.subtract)
-    act(a("NB", 0, 512), t5(0))
-    act(a("P5", 0, 512), t5(0))
-    tt(a("NB", 512, 1024), a("P5", 0, 512), a("NB", 0, 512), A.subtract)
+    act(a("NB", 0, 512), a("VR", 0, 512))
+    tt(a("NB", 512, 1024), a("VR", 0, 512), a("NB", 0, 512), A.subtract)
     for f in range(2):
         dma("s", grp("GB", f, 8192), a("NB", 512 * f, 512 * f + 512), 128)
     updates(S - 1)
     dma("s", T.yx[:, 0:4096], a("X", 0, 4096), 1024)
     yl = li("yl", 128)
-    act(a("DD", 0, 1024), ind(XW, sub(yl, 0, 64))); (cp if 4 in LAST_ON_VECTOR else act)(a("DD", 1024, 2048), ind(XW, sub(yl, 64, 128)))
+    for h in range(2):
+        get(4 + h in LAST_ON_VECTOR, a("DD", 1024 * h, 1024 * h + 1024), ind(XW, sub(yl, 64 * h, 64 * h + 64)))
     dma("s", T.yx[:, 4096:6144], a("DD", 0, 2048), 512)
     for c in range(4):
-        o, i = a("G1", 1024 * c, 1024 * c + 1024), ind(a("GB", 0, 8208), a("LB", 768 + 64 * c, 832 + 64 * c))
-        if c in LAST_ON_VECTOR: cp(o, i)
-        else: act(o, i)
-        wsel(a("P0", 64 * c, 64 * c + 64), 3, "G1", 1024 * c, 1024)
-    M0 = MW * S
-    arrival(S, sent)
-    dma("a", T.yz[:], a("MSG", M0, M0 + 256), 64)
-    for h in range(2): tt(a("BXF", 16 * h, 16 * h + 16), a("MSG", M0 + 272, M0 + 288), a("MSG", M0 + 288, M0 + 304), A.add)
+        get(c in LAST_ON_VECTOR, a("G1", 1024 * c, 1024 * c + 1024), ind(a("GB", 0, 8208), a("LB", 768 + 64 * c, 832 + 64 * c)))
+        wsel(P(0, 4 * c, 4 * c + 4), 7, "G1", 1024 * c, 1024)
+    arrival("arr", S, zlands(S), sent[1]); arrival("box", S, blands(S), sent[0])
+    dma("a", T.yz[:], zof(S), 64)
+    for h in range(2): cp(a("BXF", 16 * h, 16 * h + 16), a("BOX", 32 * S, 32 * S + 16))
     flip(sm("b0"))
     dma("a", T.yb[:], sm("b0"), 8)
     ts(nf(0), io5(0, 256), c_(pm, 256.0, A.mult), A.add)
-    ts(nf(1), a("P0", 0, 256), 0.0, A.is_gt, 4095.0, A.mult); tt(nf(1), a("P0", 0, 256), nf(1), A.add)
+    ts(nf(1), P(0, 0, 16), 0.0, A.is_gt, 3840.0, A.mult); tt(nf(1), P(0, 0, 16), nf(1), A.add)
     tt(nf(1), nf(1), nf(0), A.max)
     dma("s", T.yj[:], nf(1), 128)
 
     n = len(ops)
-    hist = {}; turns = {}
+    hist = {}; turns = {}; lastp = {}
     deps = PLAN.get("deps", [])
     for i, o in enumerate(ops if not deps else ()):
         d = {}
         for kind, rs in (("r", o["r"]), ("w", o["w"])):
-            for (nm, lo, hi, pt) in rs:
-                for (j, k2, l2, h2, p2) in hist.get(nm, ()):
-                    if lo < h2 and l2 < hi and pt & p2 and (kind == "w" or k2 == "w"):
+            for (nm, m, pt, lo) in rs:
+                for (j, k2, m2, p2) in hist.get(nm, ()):
+                    if m & m2 and pt & p2 and (kind == "w" or k2 == "w"):
                         d[j] = bool(ops[j]["e"] != o["e"] or o["e"] != "p")
         for kind, rs in (("w", o["w"]), ("r", o["r"])):
-            for (nm, lo, hi, pt) in rs:
+            for (nm, m, pt, lo) in rs:
                 keep = hist.get(nm, [])
-                if kind == "w": keep = [x for x in keep if not (lo <= x[2] and x[3] <= hi and x[4] & ~pt == 0)]
-                hist[nm] = keep + [(i, kind, lo, hi, pt)]
+                if kind == "w": keep = [x for x in keep if x[2] & ~m or x[3] & ~pt]
+                hist[nm] = keep + [(i, kind, m, pt)]
         for nm in set(x[0] for x in o["w"] + o["r"] if SCRATCH[x[0]][0] == "psum"):
             was, now = turns.get(nm, ([], []))
             if now and ops[now[0]]["e"] != o["e"]: was, now = now, []
             for j in was: d[j] = True
             turns[nm] = (was, now + [i])
+            if o["e"] == "p":
+                if nm in lastp: d.setdefault(lastp[nm], False)
+                lastp[nm] = i
         d.pop(i, None)
         deps.append(d)
     pred = [dict(d) for d in deps]
@@ -559,7 +543,7 @@ def rank_program(g, core, T, topo):
         for j in pred[i]: succ[j].append(i)
     prio = [0.0] * n
     for i in range(n - 1, -1, -1):
-        prio[i] = ops[i]["c"] + ops[i].get("early", 0) + max([prio[k] + (ops[i]["lat"] if pred[k][i] else 0) for k in succ[i]] + [ops[i]["lat"] if ops[i]["dma"] else 0])
+        prio[i] = ops[i]["c"] + max([prio[k] + (ops[i]["lat"] if pred[k][i] else 0) for k in succ[i]] + [ops[i]["lat"] if ops[i]["dma"] else 0])
     tail = [ops[i]["lat"] if ops[i]["dma"] else 0 for i in range(n)]
 
     def run(before, after, gap, first, pr, peek):
@@ -581,7 +565,8 @@ def rank_program(g, core, T, topo):
         return seq, fin
 
     if "order" not in PLAN:
-        keys = ["%s%s%d" % (o["e"], o["w"][0][0], o["w"][0][1] % MW if o["w"][0][0] in ("MSG", "OUT") else o["w"][0][1]) if o["w"] else "send" for o in ops]
+        span = {"MSG": MW, "OUT": 256, "BOX": 32, "BOXO": 32}
+        keys = ["%s%s%d" % (o["e"], o["w"][0][0], o["w"][0][3] % span.get(o["w"][0][0], 1 << 20)) if o["w"] else "send" for o in ops]
         keys = [k + ("." if i < marks[1] else "!" if i >= marks[S - 1] else "") for i, k in enumerate(keys)]
         pl = [list(p.items()) for p in pred]; eng = [o["e"] for o in ops]
         sets = [([o["c"] * (kp if o["e"] == "p" else 1) + o.get("g", 0) * kg + o.get("s", 0) * ks for o in ops],
@@ -617,6 +602,7 @@ def rank_program(g, core, T, topo):
             seq = forward([x + trial[k] for x, k in zip(base, keys)])[0]; got = score(seq)
             if got[0] <= best[0]: best = got + (seq,); more = trial
         PLAN["deps"], PLAN["order"], PLAN["span"] = deps, best[2], best[1]
+        PLAN["ops"], PLAN["marks"], PLAN["pred"] = ops, marks, pred
     order = PLAN["order"]
     place = {i: k for k, i in enumerate(order)}
     clock = {}
@@ -648,7 +634,7 @@ def rank_program(g, core, T, topo):
         if o["e"] == "x": continue
         for j in need[i]:
             oj = ops[j]
-            if oj["e"] == "x": queue[o["e"]].wait_ge(T.sem[oj["dma"]], nen)
+            if oj["e"] == "x": queue[o["e"]].wait_ge(T.sem[oj["dma"]], expect[oj["dma"]])
             elif oj["dma"]: queue[o["e"]].wait_ge(T.sem[oj["dma"]], 16)
             else: queue[o["e"]].wait_ge(T.sem[semof[oj["e"]]], val[j])
         for fn in o["f"]: ins = fn()
@@ -661,15 +647,17 @@ def rank_program(g, core, T, topo):
         if v: g.wait_ge(T.sem[semof[q]], v)
     for k in range(ndma[0]):
         g.wait_ge(T.sem["d%d" % k], 16)
-    for t in range(1, S + 1):
-        g.wait_ge(T.sem["arr%d" % t], nen); g.wait_ge(T.sem["box%d" % t], nen)
+    for nm, v in expect.items():
+        g.wait_ge(T.sem[nm], v)
     g.wait_ge(T.sem.sent, nen * 2 * S)
 
 
-BITS_ON_SCALAR = tuple(range(17))
+ACT = 0
 GB_ON_VECTOR = (0, 2, 4)
-FIRST_ON_SCALAR = False
-XE_ON_SCALAR = True
-XF_ON_SCALAR = True
-DIGITS_ON_VECTOR = (1,)
+LOW_ON_VECTOR = tuple(range(16))
+SPREAD_ON_VECTOR = ()
+DIGITS_ON_VECTOR = (1, 3, 5)
+TAKE_ON_VECTOR = False
+OUT_ON_VECTOR = False
+V2_ON_VECTOR = ()
 LAST_ON_VECTOR = (1, 3)

@@ -9,34 +9,35 @@ SPARE, ZERO, LONG = 4096, 4352, 4096
 f32, bf, i32, u16 = "float32", "bfloat16", "int32", "uint16"
 SCRATCH = {
     "X": ("sbuf", [128, XC], bf), "PQ": ("sbuf", [128, 8192], bf), "IOT": ("sbuf", [128, 8192], i32),
-    "GB": ("sbuf", [128, 8208], bf), "DD": ("sbuf", [128, 4096], bf), "G1": ("sbuf", [128, 4096], bf),
-    "E": ("sbuf", [128, 16, 256], bf), "IOS": ("sbuf", [128, 2560], f32), "IO": ("sbuf", [128, 512], f32),
+    "GB": ("sbuf", [128, 8704], bf), "E2": ("sbuf", [128, 1024], bf), "DD": ("sbuf", [128, 4096], bf), "G1": ("sbuf", [128, 4096], bf),
+    "E": ("sbuf", [128, 16, 256], bf), "IOS": ("sbuf", [128, 1024], f32), "IO": ("sbuf", [128, 512], f32),
     "TT": ("sbuf", [128, 1536], f32), "TB": ("sbuf", [128, 1024], bf), "SBI": ("sbuf", [128, 1024], i32), "SBU": ("sbuf", [128, 512], u16),
-    "VR": ("sbuf", [128, 768], f32), "V2": ("sbuf", [128, 1024], bf),
+    "VR": ("sbuf", [128, 1536], f32), "V2": ("sbuf", [128, 1024], bf),
     "MSG": ("sbuf", [128, MW * S + 256], bf), "OUT": ("sbuf", [128, 256 * S], bf),
-    "BOX": ("sbuf", [128, 32 * (S + 1)], u16), "BOXO": ("sbuf", [128, 32 * S], u16),
+    "BOX": ("sbuf", [128, 32 * (S + 1)], u16), "LOOK": ("sbuf", [128, 32 * (S + 2)], u16), "BOXO": ("sbuf", [128, 32 * S], u16),
     "XD": ("sbuf", [128, 16, 16], bf), "T2": ("sbuf", [128, 16, 16], f32), "MN": ("sbuf", [128, 512], f32),
     "W": ("sbuf", [128, 256 * 10], f32), "WI": ("sbuf", [128, 512], i32), "WB": ("sbuf", [128, 256 * 16], bf),
     "SM": ("sbuf", [128, 16 * 72], f32), "SI": ("sbuf", [128, 16 * 8], i32),
     "SH": ("sbuf", [128, 16 * 12], bf), "L": ("sbuf", [128, 16 * 64], u16), "LB": ("sbuf", [128, 256 * 5], u16),
-    "MAT": ("sbuf", [128, 144 * 8 + 128 * 12 + 256 * 4], bf), "SEL": ("sbuf", [128, 128 * 32], bf), "IF": ("sbuf", [128, 128 * 8], f32),
+    "MAT": ("sbuf", [128, 144 * 8 + 128 * 15 + 256 * 4], bf), "SEL": ("sbuf", [128, 128 * 32], bf), "IF": ("sbuf", [128, 128 * 8], f32),
     "T5": ("sbuf", [128, 512 * 3], f32),
-    "NI": ("sbuf", [128, 512], i32), "NF": ("sbuf", [128, 256 * 3], f32), "NB": ("sbuf", [128, 256 * 4], bf),
-    "BXI": ("sbuf", [128, 32], i32), "BXF": ("sbuf", [128, 64], f32), "LI": ("sbuf", [128, 4], i32), "LF": ("sbuf", [128, 4], f32),
-    "E8": ("sbuf", [128, 256], f32), "JK": ("sbuf", [128, 16], bf), "RST": ("sbuf", [128, 256], f32), "QR": ("sbuf", [128, 512], f32),
+    "NI": ("sbuf", [128, 512], i32), "NF": ("sbuf", [128, 256 * 3], f32), "NB": ("sbuf", [128, 256 * 6], bf),
+    "BXI": ("sbuf", [128, 32], i32), "BXF": ("sbuf", [128, 64], f32), "LI": ("sbuf", [128, 4], i32),
+    "JK": ("sbuf", [128, 16], bf), "RST": ("sbuf", [128, 256], f32), "QR": ("sbuf", [128, 512], f32),
 }
 for _b in range(4):
     SCRATCH["AD%d" % _b] = ("sbuf", [128, 16, 4, 16], bf)
 for _b in range(8):
     SCRATCH["P%d" % _b] = ("psum", [128, 32, 16] if _b != 2 else [128, 512], f32)
 ROW = [4 * (k & 3) + (k >> 2) for k in range(16)]
-NDMA = 56
-SEMAPHORES = ["ev", "ea", "ep", "eg", "sent"] + [nm + str(t) for t in range(1, S + 1) for nm in ("arr", "box")] + ["d%d" % k for k in range(NDMA)]
+NDMA = 72
+SEMAPHORES = ["ev", "ea", "ep", "eg", "sent", "box0"] + [nm + str(t) for t in range(1, S + 1) for nm in ("arr", "box")] + ["d%d" % k for k in range(NDMA)]
 SIZE = {f32: 4, bf: 2, i32: 4, u16: 2}
-GATHER, SCATTER, TENSOR, SYNC, WIRE = 1.56, 3.8, 0.5, 60, 2460
+GATHER, SCATTER, TENSOR, SYNC, WIRE = 1.56, 3.8, 0.55, 70, 2800
 ALL = (1 << 128) - 1
-PEEK, SEED, TRIES, MOVES = 130, 1, 2000, (150, 400, 1000, 2500, 6000)
-SETTINGS = ((0, 0, 1, 60, 0.4), (-0.46, -1.6, 1, 40, 0.24), (0.44, 1.7, 1, 80, 0.17), (0, 0, 2, 140, 0.16))
+PEEK, SEED, TRIES, MOVES = 130, 1, 1000, (150, 400, 1000, 2500, 6000)
+SETTINGS = ((0, 0, 1, 70, 0.35, 0, 2800), (-0.46, -1.6, 1.05, 60, 0.3, 0, 2800), (0.44, 1.7, 0.9, 80, 0.15, -40, 2400), (-0.2, -0.6, 1.2, 110, 0.2, 30, 4200))
+PULLS, SLACK = 22000, 20
 PLAN = {}
 MASKS = {}
 
@@ -54,10 +55,10 @@ def rank_program(g, core, T, topo):
     rank = T.rank_of(core)
     if rank is None:
         return
-    nxt = T.cores[(rank + 1) % len(T.cores)]
-    rid, pid, _ = topo.addr(nxt)
-    emask = topo.mask(core, nxt)
-    nen = len(topo.engines(core, nxt))
+    ahead_ = {k: T.cores[(rank + k) % len(T.cores)] for k in (1, 2)}
+    to = {k: topo.addr(c) for k, c in ahead_.items()}
+    emask = topo.mask(core, ahead_[1]) & topo.mask(core, ahead_[2])
+    nen = len(set(topo.engines(core, ahead_[1])) & set(topo.engines(core, ahead_[2])))
     ops = []
     ndma = [0]
     expect = {}
@@ -121,6 +122,7 @@ def rank_program(g, core, T, topo):
         if acc is None: op("a", lambda: g.scalar.activation(ap(o), ap(i), fn, bias=ap(bias), scale=ap(scale)), o, [i, bias, scale], c)
         else: op("a", lambda: g.scalar.activation(ap(o), ap(i), fn, bias=ap(bias), scale=ap(scale), accum_out=ap(acc)), acc, [i, bias, scale], c + 24)
         if acc is not None: ops[-1]["w"] += regs([o])
+        if i[0] != "ind": ops[-1]["fix"] = 1
     def mul(on_v, o, i, s):
         if on_v: ts(o, i, s, A.mult)
         else: act(o, i, scale=s)
@@ -133,25 +135,29 @@ def rank_program(g, core, T, topo):
     def iota(o, pat, base, cm):
         if SCRATCH[o[0]][2] != i32: op("g", lambda: g.iota(ap(o), pat, base, cm, allow_small_or_imprecise_dtypes=True), o, [], 160 + 2 * wid(o))
         else: op("g", lambda: g.iota(ap(o), pat, base, cm), o, [], 160 + 2 * wid(o))
+    def pick(o, i, step, base):
+        op("g", lambda: g.affine_select(ap(o), ap(i), [[0, wid(o) // 16], [step, 16]], A.is_gt, 0.0, base, 0), o, [i], 200 + 2 * wid(o))
     def dma(q, o, i, kb):
         eng = {"s": g.sync, "a": g.scalar}[q]
         op(q, lambda: eng.dma_start(ap(o), ap(i)), o, [i], 60)
         ops[-1]["dma"] = "d%d" % ndma[0]; ops[-1]["lat"] = 2400 + 5 * kb
         ndma[0] += 1
     def arrival(nm, t, lands, after):
-        ops.append({"e": "x", "f": [], "w": regs(lands), "r": [], "dma": nm + str(t), "c": 0, "lat": 0, "after": after})
+        ops.append({"e": "x", "f": [], "w": regs([x for x, _ in lands]), "r": [], "dma": nm + str(t), "c": 0, "lat": 0, "after": after})
         expect[nm + str(t)] = nen * len(lands)
     def send(nm, t, src, lands):
         sem = T.sem[nm + str(t)]
         if len(lands) == 1:
-            op("g", lambda: g.remote_dma(ap(lands[0]), ap(src), sem, T.sem.sent, pid, rid, emask), None, [src], 600)
+            op("g", lambda: g.remote_dma(ap(lands[0][0]), ap(src), sem, T.sem.sent, to[1][1], to[1][0], emask), None, [src], 600)
         else:
-            op("g", lambda: g.remote_dma_fused([RemoteDMATransfer(dst_ids=[DstId(rid=rid, pnc=pid)] * len(lands), dma_engine_mask=emask, remote_sem=sem,
-                                                                  src=ap(src), dsts=[ap(x) for x in lands])], local_sem=T.sem.sent), None, [src], 600)
+            op("g", lambda: g.remote_dma_fused([RemoteDMATransfer(dst_ids=[DstId(rid=to[k][0], pnc=to[k][1]) for _, k in lands], dma_engine_mask=emask, remote_sem=sem,
+                                                                  src=ap(src), dsts=[ap(x) for x, _ in lands])], local_sem=T.sem.sent), None, [src], 600)
         ops[-1]["dma"] = "remote"; ops[-1]["lat"] = WIRE
         return len(ops) - 1
-    def zlands(t): return [a("MSG", MW * t + 256 * h, MW * t + 256 * h + 256) for h in range(2 if t < S else 1)]
-    def blands(t): return [a("BOX", 32 * t, 32 * t + 32)]
+    def zlands(t): return [(a("MSG", MW * t + 256 * h, MW * t + 256 * h + 256), 1) for h in range(2 if t < S else 1)]
+    def blands(t):
+        here, then = a("BOX", 32 * t, 32 * t + (32 if t < S else 16)), a("LOOK", 32 * t + 32, 32 * t + 64)
+        return [(then, 1)] if t == 0 else [(here, 1), (then, 2)] if t < S - 1 else [(here, 1)]
 
     at = {"SM": 0, "L": 0, "SH": 0}
     def slot(buf, name, n):
@@ -173,7 +179,8 @@ def rank_program(g, core, T, topo):
     def MF(k): return a("IF", 128 * k, 128 * k + 128)
     def M2(k): return a("MAT", 2688 + 256 * k, 2944 + 256 * k)
     KC, LUT, IDT, ONES = M2(0), M2(1), M2(2), M2(3)
-    I128, BLK, NEG, HALF, ME, MG, LIM, NIL = MT(4), MT(5), MT(6), MT(7), MT(8), MT(9), MT(10), MT(11)
+    I128, BLK, NEG, HALF, ME, MG, NBLK, NIL = MT(4), MT(5), MT(6), MT(7), MT(8), MT(9), MT(10), MT(11)
+    SA, SE, SF = (a("MAT", 3712 + 128 * k, 3840 + 128 * k) for k in range(3))
     IF, NF, BIG, NBIG = MF(4), MF(5), MF(6), MF(7)
     def LOW(r): return a("SEL", 128 * r, 128 * r + 128)
     def SPREAD(r): return a("SEL", 2048 + 128 * r, 2176 + 128 * r)
@@ -184,8 +191,8 @@ def rank_program(g, core, T, topo):
     def grp(name, f, n): return a(name, 0, n, 1, (f, 128, 16))
     def wsel(out, k, src, lo, n, first=(), start=True, to=range(16)):
         mms(acc(out, list(first) + [(Y(k, to[r]), a(src, lo + r, lo + n, 16)) for r in range(16)], start))
-    TD, TS, TH = a("TT", 0, 512), a("TT", 512, 1024), a("TT", 1024, 1536)
-    TC, IOB = a("TB", 0, 512), a("TB", 512, 1024)
+    TH, TS, TD = a("TT", 0, 512), a("TT", 512, 1024), a("TT", 1024, 1536)
+    IOB, TC = a("TB", 0, 512), a("TB", 512, 1024)
 
     for h in range(2):
         dma("a", a("BXI", 16 * h, 16 * h + 16), T.bx[:], 8)
@@ -195,26 +202,27 @@ def rank_program(g, core, T, topo):
         dma("sa"[k & 1], a("SBI", 512, 1024, 1, (k, 128, 16)), T.sb[ROW[k]:128:16, :], 16)
     dma("s", a("SBI", 0, 512), T.sb[:], 256)
     dma("a", a("NI", 0, 256), T.pe[:], 128)
-    for x in zlands(0): dma("a", x, T.zs[:], 64)
-    dma("a", a("LI", 0, 2, 1, (0, 8)), T.lim[:], 1)
+    for x, _ in zlands(0): dma("a", x, T.zs[:], 64)
+    for k in range(16):
+        dma("s", grp("LI", k, 2), T.lim[:], 1)
     iota(si(0, 1), [[0, 1]], 0, 1)
     iota(io5(0, 512), [[1, 512]], 0, 0)
     iota(a("QR", 0, 256), [[1, 4], [4, 4], [0, 16]], 0, 0)
     iota(a("QR", 256, 512), [[0, 16], [1, 16]], 0, 0)
-    iota(a("E8", 0, 128, 1, (0, 8)), [[1, 128]], 0, -16)
     iota(a("IOS", 0, 1024), [[1, 64], [256, 16]], 0, 0)
     iota(KC, [[1, 16], [16, 4], [64, 4]], 0, 0)
     iota(IOB, [[1, 512]], -256, 0)
     iota(ONES, [[0, 256]], 1, 0)
     iota(NIL, [[0, 128]], 0, 0)
+    iota(wb(1), [[0, 256]], 128, 0)
     iota(sub(wb(12), 0, 16), [[0, 16]], 0, 0)
-    for c in range(8):
-        iota(a("IOT", 1024 * c, 1024 * c + 1024), [[1, 1024]], 1024 * c, 0)
-    for c in range(4):
-        iota(a("X", 4096 + 1152 * c, 5248 + 1152 * c), [[0, 1152]], 0, 0)
-        iota(a("PQ", 4096 + 1024 * c, 5120 + 1024 * c), [[0, 1024]], 0, 0)
-    iota(a("VR", 0, 768), [[0, 768]], 0, 0)
-    iota(a("GB", 8192, 8208), [[0, 16]], 0, 0)
+    for c in range(16):
+        iota(a("IOT", 512 * c, 512 * c + 512), [[1, 512]], 512 * c, 0)
+    for c in range(8, 17):
+        iota(a("X", 512 * c, 512 * c + 512), [[0, 512]], 0, 0)
+        if c < 16: iota(a("PQ", 512 * c, 512 * c + 512), [[0, 512]], 0, 0)
+    iota(col("round"), [[0, 1]], int(ROUND), 0); iota(col("nround"), [[0, 1]], -int(ROUND), 0)
+    iota(a("GB", 0, 512), [[0, 512]], 0, 0)
     pf, pm, p16, par = col("pf"), col("pm"), col("p16"), col("par")
     nc = [0]
     def tmp():
@@ -234,7 +242,7 @@ def rank_program(g, core, T, topo):
     i16 = io5(0, 16)
     ts(YM(0), io5(0, 144), c_(p16, 15.0, A.add), A.is_equal)
     ts(IF, io5(0, 128), pf, A.is_equal)
-    act(I128, IF); act(NEG, IF, scale=-1.0); act(HALF, IF, scale=0.5); act(LIM, IF, scale=-1020.0)
+    act(I128, IF); act(NEG, IF, scale=-1.0); act(HALF, IF, scale=0.5);
     act(NF, IF, scale=-1.0); act(BIG, IF, scale=16384.0); act(NBIG, IF, scale=-16384.0)
     for c in range(2):
         on = c_(par, 16.0 * c, A.is_equal)
@@ -246,11 +254,11 @@ def rank_program(g, core, T, topo):
         tp(a("BXF", 32, 64), a("BXF", 0, 32))
         tt(o, a("BXF", 48, 64), a("BXF", 32, 48), A.subtract); ts(o, o, par1, A.mult); tt(o, o, a("BXF", 32, 48), A.add)
     cp(a("BXF", 0, 32), a("BXI", 0, 32)); flip(sm("b0"))
-    for h in range(2): cp(a("BOX", 16 * h, 16 * h + 16), sm("b0"))
+    cp(a("BOX", 0, 16), sm("b0")); ms(a("BOX", 16, 32), 0)
     cp(TS, a("SBI", 512, 1024))
-    d512, dW, q16 = sm("d512"), sm("dW"), sm("q16")
-    ts(d512, i16, 16.0, A.mult, c_(pm, 512.0, A.add), A.add)
-    act(dW, d512, bias=SPARE - 512.0); act(q16, i16, scale=1.0 / 16)
+    d256, dW, q16 = sm("d256"), sm("dW"), sm("q16")
+    ts(d256, i16, 16.0, A.mult, c_(pm, 256.0, A.add), A.add)
+    act(dW, d256, bias=SPARE - 256.0); act(q16, i16, scale=1.0 / 16)
     iota(sm("row"), [[1, 4], [4, 4]], 0, 0)
     ts(li("reo"), sm("row"), c_(pm, 16.0, A.mult), A.add)
     qk, rk = a("QR", 0, 256), a("QR", 256, 512)
@@ -259,9 +267,9 @@ def rank_program(g, core, T, topo):
     act(RST, rk, F.Relu, scale=-65536.0, bias=65536.0)
     ts(LUT, qk, pm, A.not_equal, -2048.0, A.mult)
     act(IDT, io5(0, 256), scale=2.0 ** -18)
-    ms(a("DD", 0, 2048), 0.0)
-    for o in (a("PQ", 0, 2048), a("PQ", 2048, 4096)):
-        dma("s", o, a("DD", 0, 2048), 512)
+    for c in range(2): act(a("E2", 512 * c, 512 * c + 512), io5(0, 512), scale=0.0)
+    for c in range(4):
+        dma("s", a("PQ", 1024 * c, 1024 * c + 1024), a("E2", 0, 1024), 256)
     ts(a("T5", 0, 128), io5(0, 128), p16, A.subtract, -7.5, A.add)
     act(a("T5", 128, 256), a("T5", 0, 128), F.Abs)
     ts(BLK, a("T5", 128, 256), 8.0, A.is_lt)
@@ -280,16 +288,18 @@ def rank_program(g, core, T, topo):
     r8 = tmp(); op("v", lambda: g.vector.reciprocal(ap(r8), ap(p8)), r8, [p8], 240)
     one = [sub(sm("one"), k, k + 1) for k in range(4)]
     m0 = c_(one[0], 1.0 / 2048, A.mult); m1 = c_(one[1], 1.0 / 2048, A.mult)
-    for k, wt in ((1, c_(pm, 1.0, A.add)), (2, c_(r8, 128.0, A.mult)), (3, m0), (4, m1), (5, c_(one[2], 1.0 / 2048, A.mult, m1, A.add)),
-                  (6, c_(one[3], 1.0 / 2048, A.mult)), (7, c_(c_(one[1], 128.0, A.mult), c_(one[0], 0.125, A.mult), A.add))):
+    for k, wt in ((1, c_(pm, 1.0, A.add, 512.0, A.mult)), (2, c_(r8, 128.0, A.mult)), (3, m0), (4, m1), (5, c_(one[2], 1.0 / 2048, A.mult, m1, A.add)),
+                  (6, c_(one[3], 1.0 / 2048, A.mult)), (7, c_(c_(one[1], 128.0, A.mult, c_(one[2], 1.875, A.mult), A.add), c_(one[0], 0.125, A.mult), A.add))):
         act(YM(k), YM(0), scale=wt)
     act(ME, I128, scale=m0); ts(MG, io5(0, 128), c_(pf, 1.0, A.add), A.is_equal, m0, A.mult)
-    e8 = a("E8", 0, 128, 1, (0, 8)); e9 = a("E8", 128, 256, 1, (0, 8))
-    ts(e9, e8, 0.0, A.is_ge); ts(e8, e8, 16.0, A.is_lt); tt(e8, e8, e9, A.mult)
-    cp(a("LF", 0, 2, 1, (0, 8)), a("LI", 0, 2, 1, (0, 8)))
-    mms(acc(b("P5", 8, (0, 2)), [(e8, a("LF", 0, 2, 1, (0, 8)))]))
+    act(NBLK, BLK, scale=-1.0)
+    pm1 = sub(wb(0), 0, 128); two = sub(wb(0), 128, 256); four = sub(wb(6), 0, 128); mid = sub(wb(6), 128, 256)
+    iota(pm1, [[0, 64], [-2, 2]], 1, 0); tt(pm1, pm1, BLK, A.mult)
+    pick(two, pm1, -1, 2); pick(four, pm1, -1, 4); pick(mid, four, 1, -1)
+    act(SE, two, scale=m1); act(SF, mid, scale=m1); act(SA, four, scale=c_(m0, -1.0, A.mult))
     thr = sm("thr", 32)
-    cp(col("lim0"), b("P5", 8, (0, 1))); ts(col("sl"), b("P5", 8, (1, 2)), 1.0, A.add, 1012.0, A.min)
+    ts(col("n4"), sub(sm("one"), 4, 5), -1.0, A.mult)
+    ts(col("lim0"), a("LI", 0, 1), -1.0, A.add, col("n4"), A.mult); ts(col("sl"), a("LI", 1, 2), 1.0, A.add, 1012.0, A.min)
     ts(sub(thr, 0, 16), i16, 0.0, A.mult, col("sl"), A.add); ms(sub(thr, 16, 32), 1012.0)
     ms(si(6, 1), 0)
     for h in range(2):
@@ -297,31 +307,30 @@ def rank_program(g, core, T, topo):
 
     cp(a("SBU", 0, 512), a("SBI", 0, 512))
     for c in range(4):
-        win = a("IOS", 512 + 512 * c, 1024 + 512 * c) if c else TS
+        win = a("VR", 512 * c - 512, 512 * c) if c else TS
         if c: act(win, TS, bias=-64.0 * c)
         tt(a("G1", 1024 * c, 1024 * c + 1024), ind(win, a("LB", 512 + 64 * c, 576 + 64 * c)), a("IOS", 0, 1024), A.is_equal)
-        wsel(P(0, 4 * c, 4 * c + 4), 1, "G1", 1024 * c, 1024)
+        wsel(P(0, 4 * c, 4 * c + 4), 1, "G1", 1024 * c, 1024, [(I128, sub(nb(1), 64 * c, 64 * c + 64))])
         wsel(P(0, 16 + 4 * c, 20 + 4 * c), 2, "G1", 1024 * c, 1024)
+    iota(a("VR", 0, 768), [[0, 768]], 0, 0)
     kh, sc = P(0, 0, 16), P(0, 16, 32)
-    ts(nb(2), kh, 9.0, A.is_ge, 512.0, A.mult); cp(nb(3), sc)
+    ts(nb(2), kh, 512.0 * 9 - 256, A.is_ge, 512.0, A.mult); act(nb(3), sc)
     for f in range(2, 4):
         dma("s", grp("PQ", f, 4096), nb(f), 64)
-    act(nf(0), kh, scale=512.0, bias=-512.0); tt(nf(0), nf(0), a("NI", 256, 512), A.add)
-    ts(nf(1), kh, 0.0, A.is_equal, 8192.0, A.mult); tt(nf(0), nf(0), nf(1), A.max)
-    cp(lb(3), nf(0))
+    ts(lb(3), kh, 256.0, A.add)
     for c in range(8):
-        get(c in GB_ON_VECTOR, a("GB", 1024 * c, 1024 * c + 1024), ind(a("PQ", 0, 4096), a("SBU", 64 * c, 64 * c + 64)))
-        for bank, k in ((4, 5), (6, 6), (7, 4)):
-            wsel(P(bank, 4 * c, 4 * c + 4), k, "GB", 1024 * c, 1024, to=ROW)
-    act(TD, P(4, 0, 32), bias=256.0)
+        get(c in GB_ON_VECTOR, a("GB", 512 + 1024 * c, 1536 + 1024 * c), ind(a("PQ", 0, 4096), a("SBU", 64 * c, 64 * c + 64)))
+        for bank, k in ((0, 5), (6, 6), (7, 4)):
+            wsel(P(bank, 4 * c, 4 * c + 4), k, "GB", 512 + 1024 * c, 1024, to=ROW)
+    act(TD, P(0, 0, 32), bias=256.0)
     act(TC, P(6, 0, 32))
     tt(t5(1), P(7, 0, 32), IOB, A.is_equal); act(t5(2), t5(1), scale=0.25, bias=LONG + 256.0); tt(TH, P(7, 0, 32), t5(2), A.add)
 
-    def lowest(keys, own, on, out):
+    def lowest(keys, own, on, out, more=()):
         for q in range(16):
             ts(b("E", q, (0, 256 - 16 * q)), sub(keys, 16 * q, 256), own(q), A.is_equal, sub(on, q, q + 1), A.mult)
             if q < 15: mms([(P(3, q + 1, 16), BLK, b("E", q, (16, 256 - 16 * q)), q == 0, q == 14)])
-        mms(acc(out, [(LOW(r), b("E", (0, 16), r)) for r in range(1, 16)], True, False))
+        mms(acc(out, list(more) + [(LOW(r), b("E", (0, 16), r)) for r in range(1, 16)], True, False))
         act(sub(wb(12), 16, 256), P(3, 1, 16))
         wsel(out, 0, "WB", 256 * 12, 256, start=False)
 
@@ -333,72 +342,87 @@ def rank_program(g, core, T, topo):
     def lst(t, k): return sub(li("up%d" % t, 64), 16 * k, 16 * k + 16)
 
     def updates(t):
+        XW = a("X", 0, 5120 + 512 * t)
         if t >= 1: cp(ind(XW, lst(t - 1, 2 if 1 < t < S - 1 else 1)), zof(t - 1))
         if t >= 3: cp(ind(XW, lst(t - 2, 3)), zof(t - 2))
         cp(ind(XW, lst(t, 0)), wb(7))
-        cp(ind(XW, lst(t, 1)), wb(1) if t < S - 1 else zof(t))
-        if t < S - 1: cp(ind(a("PQ", 0, 8192), lst(t, 0)), wb(9))
+        if t < S - 1: tt(ind(XW, lst(t, 1)), zof(t), wb(1), A.add)
+        else: cp(ind(XW, lst(t, 1)), zof(t))
+        if t < S - 1: cp(ind(a("PQ", 0, wid(XW)), lst(t, 0)), wb(5))
 
-    sent = None
+    sent = (send("box", 0, a("BOX", 0, 32), blands(0)), None)
     marks = []
     for t in range(S):
         marks.append(len(ops))
-        z = zof(t); aU = a("BOX", 32 * t, 32 * t + 16); msg = a("BOX", 32 * t + 16, 32 * t + 32)
-        XT = XW if t else a("X", 0, 4096)
+        z = zof(t); box, out = a("BOX", 32 * t, 32 * t + 16), a("BOX", 32 * t + 16, 32 * t + 32)
+        look = a("LOOK", 32 * t, 32 * t + 16) if t else box
+        XT = a("X", 0, 4608 + 512 * t if t else 4096)
+        def by_box(x): return ind(x, look)
         if t:
-            arrival("arr", t, zlands(t), sent[1]); arrival("box", t, blands(t), sent[0])
-            cp(lb(0), ind(TD, aU))
-            act(wb(13), ind(TC, aU)); act(w(1), ind(TS, aU)); act(w(2), ind(TH, aU))
+            arrival("arr", t, zlands(t), sent[1])
+            cp(lb(0), by_box(TD))
+            act(wb(13), by_box(TC)); act(w(1), by_box(TS)); act(w(2), by_box(TH))
         else:
-            act(w(1), ind(TS, aU))
-        mf, thA, ab, base, a3 = sm("mf"), sh("thA"), sh("ab"), sm("base"), sm("a3")
-        cp(mf, msg); ts(thA, msg, 512.0, A.is_lt, 1012.0, A.mult); ts(ab, aU, -256.0, A.add)
-        if t:
-            ts(base, msg, 512.0, A.is_ge, -512.0, A.mult); tt(base, base, mf, A.add)
-            if t == S - 1: ts(sm("t0"), base, 512.0, A.is_ge, -512.0, A.mult); tt(base, base, sm("t0"), A.add)
-        else: base = mf
-        ts(a3, aU, 256.0, A.mult); tt(a3, a3, i16, A.subtract)
-        act(wb(14), ind(IOB, aU))
-        T2 = b("T2", (0, 16), (0, 16)); XD = b("XD", (0, 16), (0, 16))
-        if t:
-            for Q in range(4):
-                for c in (2 * Q, 2 * Q + 1):
-                    get(c in DIGITS_ON_VECTOR, a("G1", 512 * c, 512 * c + 512), ind(a("V2", 0, 1024), a("LB", 32 * c, 32 * c + 32)))
-                wsel(P(0, 4 * Q, 4 * Q + 4), 0, "G1", 1024 * Q, 1024)
-            updates(t - 1)
-            wi = a("WI", 0, 256)
-            if t < S - 1:
-                tt(wi, P(0, 0, 16), wb(13), A.mult)
-            else:
-                tt(w(3), P(0, 0, 16), wb(13), A.mult); ts(wi, w(3), -0.24, A.add)
-            ts(wi, wi, 7, A.arith_shift_right, 7, A.bitwise_and)
-            ts(XD, wi, 8192.0, A.mult)
-            mms([(P(7, 0, 16), IF, w(1), True, False)])
-            mms([(P(7, 0, 16), I128, XD, False, True)])
-            tt(T2, P(7, 0, 16), w(2), A.min)
-        else:
-            act(T2, w(1))
-        mms([(P(1, 0, 16), NIL, KC, True, False)])
-        if t: mms([(P(1, c, 16, 2), MT(2 * c + h), b("XD", (h, 16, 2), (0, 16)), False, False) for c in range(2) for h in range(2)])
-        mms([(P(1, c, 16, 2), MF(2 * c + h), b("T2", (h, 16, 2), (0, 16)), False, c + h == 2) for c in range(2) for h in range(2)])
+            act(w(1), by_box(TS))
+        arrival("box", t, blands(t), sent[0])
+        thA, ab, base, a3 = sh("thA"), sh("ab"), sm("base", 32), sm("a3")
+        ts(thA, out, 0.0, A.is_equal, 1012.0, A.mult); ts(ab, look, -256.0, A.add)
+        cp(sub(base, 0, 16), box)
+        if t < S - 1: ts(sub(base, 16, 32), out, -1.0, A.add, 0.0, A.max)
+        ts(a3, look, 256.0, A.mult); tt(a3, a3, i16, A.subtract)
+        act(wb(14), by_box(IOB))
         cc = w(0)
-        tp(cc, P(1, 0, 16))
+        cuts = PIECES if t else (0, 16)
+        for j, (lo, hi) in enumerate(zip(cuts, cuts[1:])):
+            bw, bx_, bs = BANKS[j & 1]
+            cut = lambda x: sub(x, 16 * lo, 16 * hi)
+            T2 = b("T2", (lo, hi), (0, 16)); XD = b("XD", (lo, hi), (0, 16))
+            if t:
+                for Q in range(lo // 4, hi // 4):
+                    for c in (2 * Q, 2 * Q + 1):
+                        get(c in DIGITS_ON_VECTOR, a("G1", 512 * c, 512 * c + 512), ind(a("V2", 0, 1024), a("LB", 32 * c, 32 * c + 32)))
+                    wsel(P(bw, 4 * Q, 4 * Q + 4), 0, "G1", 1024 * Q, 1024)
+                if j == 0: updates(t - 1)
+                wi = cut(a("WI", 0, 256))
+                if t < S - 1:
+                    tt(wi, P(bw, lo, hi), cut(wb(13)), A.mult)
+                else:
+                    tt(cut(w(3)), P(bw, lo, hi), cut(wb(13)), A.mult); ts(wi, cut(w(3)), -0.24, A.add)
+                ts(wi, wi, 7, A.arith_shift_right, 7, A.bitwise_and)
+                ts(XD, wi, 8192.0, A.mult)
+                mms([(P(bx_, 16 + lo, 16 + hi), IF, cut(w(1)), True, False)])
+                mms([(P(bx_, 16 + lo, 16 + hi), I128, XD, False, True)])
+                tt(T2, P(bx_, 16 + lo, 16 + hi), cut(w(2)), A.min)
+            else:
+                act(T2, w(1))
+            mms([(P(bs, lo, hi), NIL, cut(KC), True, False)])
+            if t: mms([(P(bs, lo + c, hi, 2), MT(2 * c + h), b("XD", (lo + h, hi, 2), (0, 16)), False, False) for c in range(2) for h in range(2)])
+            mms([(P(bs, lo + c, hi, 2), MF(2 * c + h), b("T2", (lo + h, hi, 2), (0, 16)), False, c + h == 2) for c in range(2) for h in range(2)])
+            tp(cut(cc), P(bs, lo, hi))
         cU = lb(1)
         cp(cU, ind(cc, li("reo")))
-        RN = w(9)
-        if t: ts(RN, cc, 1.5 * 2 ** 23, A.add, -1.5 * 2 ** 23, A.add)
-        else: act(RN, cc)
         key, dl = a("P2", 0, 256), a("P2", 256, 512)
-        mms([(dl, IF, RN, True, False), (sub(dl, 0, 255), NF, sub(RN, 1, 256), False, False), (sub(dl, 15, 255, 16), IF, sub(RN, 16, 256, 16), False, True)])
-        mms(acc(key, ([(BIG, cc), (NBIG, RN)] if t else []) + [(I128, KC)], True, False))
-        lowest(wb(14), lambda q: sub(ab, q, q + 1), thA, P(4, 0))
+        mms([(dl, IF, cc, True, False), (sub(dl, 0, 255), NF, sub(cc, 1, 256), False, False), (sub(dl, 15, 255, 16), IF, sub(cc, 16, 256, 16), False, True)])
+        if t and ROUND_ON_VECTOR: ts(w(9), cc, ROUND, A.add, -ROUND, A.add)
+        elif t: act(w(9), cc, bias=col("round")); act(w(9), w(9), bias=col("nround"))
+        mms(acc(key, ([(BIG, cc), (NBIG, w(9))] if t else []) + [(I128, KC)], True, False))
+        lowest(wb(14), lambda q: sub(ab, q, q + 1), thA, P(4, 0), [(SPREAD(0), sub(ONES, 0, 16))] + 3 * [(NEG, thA)])
+        sw, vo = sm("sw"), sm("vo")
+        tt(sw, P(4, 0), d256, A.min); tt(vo, sw, ab, A.max); ts(li("vo"), vo, 256.0, A.add)
+        zz = a("MSG", MW * t, MW * t + 512)
+        on_scalar = list(zip(X_ON_SCALAR[min(t, 1)], (0, 7, 6, 1) if t else (5, 1) * 4))
         for c in range(8):
-            tt(a("DD", 512 * c, 512 * c + 512), ind(XT, sub(cU, 32 * c, 32 * c + 32)), a("MSG", MW * t, MW * t + 512), A.subtract)
-            for k in (2 * c, 2 * c + 1):
-                act(b("AD%d" % (k >> 2), (0, 16), k & 3, (0, 16)), a("DD", 256 * k, 256 * k + 256), F.Abs)
+            dd, src, bank = a("DD", 512 * c, 512 * c + 512), ind(XT, sub(cU, 32 * c, 32 * c + 32)), dict(on_scalar).get(c)
+            if bank is None: tt(dd, src, zz, A.subtract)
+            else: act(dd, src); mms(acc(P(bank, 0, 32), [(I128, dd), (NEG, zz)]))
+            for h in range(2):
+                k = 2 * c + h
+                act(b("AD%d" % (k >> 2), (0, 16), k & 3, (0, 16)), sub(dd, 256 * h, 256 * h + 256) if bank is None else P(bank, 16 * h, 16 * h + 16), F.Abs)
+            if bank is not None and t == 0: act(dd, P(bank, 0, 32))
             if c & 1:
                 Q = c >> 1
                 mms(acc(sub(key, Q, 256, 4), [(Y(0, r), b("AD%d" % Q, (0, 16), (0, 4), r)) for r in range(16)], False, Q == 3))
+        for c, bank in on_scalar if t else (): act(a("DD", 512 * c, 512 * c + 512), P(bank, 0, 32))
         mn = a("MN", 0, 256); m12 = a("MN", 15, 512, 16)
         scan(mn, RST, key, A.add, A.min)
         tt(w(7), mn, key, A.not_equal)
@@ -407,65 +431,64 @@ def rank_program(g, core, T, topo):
         eU, cl = li("eU"), sm("cl")
         cp(eU, e)
         tt(cl, sub(mn, 15, 256, 16), thA, A.is_lt)
-        cp(lb(4), ind(a("IOT", 0, 8192 if t else 4096), eU))
+        cp(lb(4), ind(a("IOT", 0, wid(XT)), eU))
         tt(sub(w(3), 1, 256), sub(key, 1, 256), sub(mn, 0, 255), A.max)
         scan(a("MN", 257, 512), sub(RST, 0, 255), sub(w(3), 1, 256), A.add, A.min)
+        if t: act(wb(15), key, F.Relu, scale=16.0, bias=-16.0 * (4096 + 1020))
         lowest(lb(4), lambda q: sub(w(8), 16 * q + 15, 16 * q + 16), cl, P(4, 1))
         kq = si(2, 32)
         ts(kq, m12, 256.0, A.mult); ts(kq, kq, 255, A.bitwise_and)
         ts(li("dU", 32), kq, 16.0, A.mult, pm, A.add); cp(li("kU", 32), kq)
         tt(sm("gb"), si(3), a3, A.add); ts(li("gb"), sm("gb"), 1.0 / 16, A.mult)
         d1, d2 = wb(2), wb(3)
-        act(wb(10), ind(a("PQ", 0, 8192 if t else 4096), eU))
-        act(d1, ind(a("DD", 0, 4096), sub(li("dU", 32), 0, 16)))
+        act(wb(10), ind(a("PQ", 0, wid(XT)), eU))
+        act(wb(2, 2), ind(a("DD", 0, 4096), li("dU", 32)))
+        act(wb(11), ind(a("GB", 512, 8704), li("gb")))
         act(zof(t, 2), d1, F.Abs)
-        mms(acc(P(7, 0, 16), [(I128, z), (HALF, d1)]))
-        act(wb(4), P(7, 0, 16), bias=191.75)
+        mms(acc(P(1, 16, 32), [(I128, z), (HALF, d1)]))
+        act(wb(4), P(1, 16, 32), bias=191.75)
         if TAKE_ON_VECTOR: ts(zof(t, 3), wb(4), -192.0, A.add)
         else: act(zof(t, 3), wb(4), bias=-192.0)
         less = [(NEG, ab)]
         wsel(P(5, 0), 3, "WB", 256 * 10, 256, less); wsel(P(5, 1), 4, "WB", 256 * 10, 256, less)
-        lge = sh("lge"); dx = sm("dx")
+        nx = sm("nx", 32); dx = sub(nx, 0, 16)
         ts(dx, P(5, 0), 0.0, A.is_equal); tt(dx, P(5, 1), dx, A.mult); tt(dx, P(5, 0), dx, A.add)
-        if t: ts(lge, e, 4096.0, A.is_ge)
-        if t == 0: act(dx, dx, bias=512.0)
-        elif t < S - 1: act(sm("st"), lge, scale=512.0, bias=512.0); tt(dx, dx, sm("st"), A.add)
-        clq, ed, tk = sm("clq"), sm("ed"), sm("tk")
+        if t: ts(sm("st"), e, 4096.0, A.is_ge, 1.0, A.add)
+        clq, ed, tk = sm("clq"), sm("ed"), sm("tk") if t else sub(nx, 16, 32)
         tt(clq, cl, q16, A.add); tt(ed, e, dW, A.subtract)
         tt(tk, cl, P(4, 1), A.is_gt)
-        tt(dx, dx, tk, A.mult); tt(dx, dx, base, A.add)
-        ts(a("BOXO", 32 * t, 32 * t + 16), dx, 511.0, A.min); cp(a("BOXO", 32 * t + 16, 32 * t + 32), dx)
         tt(clq, clq, tk, A.add); ts(li("ix"), clq, 256.0, A.mult, pm, A.add)
+        nw = 32 if t < S - 1 else 16
+        tt(dx, dx, tk, A.mult)
+        if 0 < t < S - 1: tt(sub(nx, 16, 32), sm("st"), tk, A.mult)
+        tt(sub(base, 0, nw), sub(nx, 0, nw), sub(base, 0, nw), A.add); cp(a("BOXO", 32 * t, 32 * t + nw), sub(base, 0, nw))
         get(OUT_ON_VECTOR, a("OUT", 256 * t, 256 * t + 256), ind(a("MSG", MW * t + 256, MW * t + 1024), li("ix")))
-        sent = (send("box", t + 1, a("BOXO", 32 * t, 32 * t + 32), blands(t + 1)), send("arr", t + 1, a("OUT", 256 * t, 256 * t + 256), zlands(t + 1)))
-        act(d2, ind(a("DD", 0, 4096), sub(li("dU", 32), 16, 32)))
-        act(wb(11), ind(a("GB", 0, 8192), li("gb")))
-        wsel(P(5, 2), 4, "WB", 256 * 11, 256, less)
+        sent = (send("box", t + 1, a("BOXO", 32 * t, 32 * t + nw), blands(t + 1)), send("arr", t + 1, a("OUT", 256 * t, 256 * t + 256), zlands(t + 1)))
         mms(acc(P(0, 0, 16), [(I128, d1), (NEG, d2)]))
         act(wb(6), P(0, 0, 16), F.Abs)
-        wsel(P(5, 3), 0, "WB", 256 * 6, 256)
+        mms(acc(P(7, 0, 16), [(SA, wb(14)), (SE, wb(10)), (SF, wb(11))], True, False))
+        mms([(P(7, 0, 16), Y(0, 4), wb(6), False, True)])
+        act(wb(0), P(7, 0, 16), F.Relu, scale=2048.0, bias=col("jl") if t else col("lim0"))
         mms(acc(P(0, 16, 32), [(I128, z), (HALF, d1), (HALF, d2), (HALF, wb(6))]))
         act(wb(7), P(0, 16, 32))
-        if t < S - 1: act(wb(1), z, bias=128.0)
-        sw, vo, jn = sh("sw"), sm("vo"), sh("jn")
-        tt(sw, thA, P(4, 0), A.is_gt); tt(vo, mf, d512, A.subtract); tt(vo, vo, sw, A.mult); tt(vo, vo, d512, A.add); cp(li("vo"), vo)
-        r12, hm, t1 = sh("r12", 32), sh("hm", 32), sh("t1")
+        r12, rb, jn = sh("r12", 32), sh("rb"), sh("jn")
         tt(r12, m12, thr, A.is_lt)
-        ts(hm, P(5, 1, 3), 0.0, A.is_equal)
-        ts(t1, P(5, 3), col("jl") if t else col("lim0"), A.is_lt)
-        mms(acc(P(5, 4), [(I128, x) for x in (sub(r12, 0, 16), sub(r12, 16, 32), sub(hm, 0, 16), sub(hm, 16, 32), sw)] + ([(NEG, lge)] if t else []) + [(I128, t1)]))
-        ts(jn, P(5, 4), 6.0, A.is_equal)
-        act(wb(5), ind(LUT, sub(li("kU", 32), 0, 16))); act(wb(8), ind(LUT, sub(li("kU", 32), 16, 32)))
+        tt(rb, sub(r12, 0, 16), sub(r12, 16, 32), A.mult)
+        if t: tt(rb, rb, sm("st"), A.is_ge)
+        act(wb(8, 2), ind(LUT, li("kU", 32)))
         if t:
-            items = acc(P(6, 0, 16), [(LIM, ONES)] + [(Y(0, ROW[k]), b("AD%d" % (k >> 2), (0, 16), k & 3, (0, 16))) for k in range(16)], True, False)
-            mms(items)
+            tp(b("XD", (0, 16), (0, 16)), wb(15))
+            mms([(P(6, 0, 16), NIL, KC, True, False)] + [(P(6, c, 16, 2), MT(2 * c + h), b("XD", (h, 16, 2), (0, 16)), False, False) for c in range(2) for h in range(2)])
             items = spread(6, 0, sub(r12, 0, 16)); items[-1] = items[-1][:4] + (True,)
             mms(items)
-            act(w(4), ind(a("VR", 0, 512), aU))
+            act(w(4), by_box(a("VR", 0, 512)))
             tt(w(5), w(4), P(6, 0, 16), A.min)
-        mms(acc(P(6, 16, 32), [(I128, wb(5)), (I128, wb(8))], True, False))
-        mms(spread(6, 16, jn) + [(P(6, 16, 32), I128, IDT, False, True)])
+        mms(acc(P(6, 16, 32), [(I128, wb(8)), (I128, wb(9))], True, False))
+        mms(spread(6, 16, rb))
+        mms(acc(P(6, 16, 32), [(NBLK, wb(0)), (I128, IDT)], False))
         act(w(6), P(6, 16, 32), F.Relu, bias=t + 1.0)
+        wsel(P(5, 4), 0, "WB", 0, 256, [(IF, sw), (NEG, rb)])
+        ts(jn, P(5, 4), -989.0, A.is_equal)
         if t: tt(ind(a("VR", 0, 768), li("vo")), w(5), w(6), A.max)
         else: cp(ind(a("VR", 0, 768), li("vo")), w(6))
         if t < S - 1:
@@ -475,22 +498,24 @@ def rank_program(g, core, T, topo):
         tt(ed, ed, tk, A.mult); tt(u0, ed, dW, A.add)
         nl = 4 if 0 < t < S - 2 else 2
         if nl == 4: tt(u1, u0, dW, A.min); tt(u2, u0, dW, A.max)
-        act(sm("t4"), mf, bias=LONG + 512.0 * (t + 1))
+        act(sm("t4"), ab, bias=LONG + 256.0 + 512.0 * (t + 1))
         tt(sm("t4"), sm("t4"), jn, A.mult); tt(u3, sm("t4"), dW, A.max)
         cp(sub(li("up%d" % t, 64), 0, 16 * nl), sub(up, 0, 16 * nl))
         ts(sub(li("yl", 128), 16 * t, 16 * t + 16), sm("t4"), float(ZERO), A.max)
         if t < S - 1:
             mms(acc(P(7, 16, 32), [(ME, wb(10)), (MG, wb(11))]))
-            act(wb(9), P(7, 16, 32))
+            act(wb(5), P(7, 16, 32))
             mms(acc(P(5, 5), [(BLK, jn)]))
             act(a("JK", 0, 16), P(5, 5), scale=8.0, acc=col("nj"))
             ts(si(6, 1), si(6, 1), col("nj"), A.add); ts(si(6, 1), si(6, 1), 255, A.bitwise_and)
-            ts(col("jl"), si(6, 1), col("lim0"), A.add)
+            ts(col("jl"), si(6, 1), col("n4"), A.mult, col("lim0"), A.add)
 
-    act(a("NB", 0, 512), a("VR", 0, 512))
-    tt(a("NB", 512, 1024), a("VR", 0, 512), a("NB", 0, 512), A.subtract)
-    for f in range(2):
-        dma("s", grp("GB", f, 8192), a("NB", 512 * f, 512 * f + 512), 128)
+    for lo in (0, 256):
+        act(a("NB", lo, lo + 256), a("VR", lo, lo + 256))
+        tt(a("NB", 512 + lo, 768 + lo), a("VR", lo, lo + 256), a("NB", lo, lo + 256), A.subtract)
+    act(a("NB", 1024, 1536), a("VR", 0, 512), F.Sign)
+    for f in range(3):
+        dma("s", a("GB", 512, 8704, 1, (f, 128, 16)), a("NB", 512 * f, 512 * f + 512), 128)
     updates(S - 1)
     dma("s", T.yx[:, 0:4096], a("X", 0, 4096), 1024)
     yl = li("yl", 128)
@@ -498,16 +523,15 @@ def rank_program(g, core, T, topo):
         get(4 + h in LAST_ON_VECTOR, a("DD", 1024 * h, 1024 * h + 1024), ind(XW, sub(yl, 64 * h, 64 * h + 64)))
     dma("s", T.yx[:, 4096:6144], a("DD", 0, 2048), 512)
     for c in range(4):
-        get(c in LAST_ON_VECTOR, a("G1", 1024 * c, 1024 * c + 1024), ind(a("GB", 0, 8208), a("LB", 768 + 64 * c, 832 + 64 * c)))
+        get(c in LAST_ON_VECTOR, a("G1", 1024 * c, 1024 * c + 1024), ind(a("GB", 0, 8704), a("LB", 768 + 64 * c, 832 + 64 * c)))
         wsel(P(0, 4 * c, 4 * c + 4), 7, "G1", 1024 * c, 1024)
     arrival("arr", S, zlands(S), sent[1]); arrival("box", S, blands(S), sent[0])
     dma("a", T.yz[:], zof(S), 64)
-    for h in range(2): cp(a("BXF", 16 * h, 16 * h + 16), a("BOX", 32 * S, 32 * S + 16))
+    for h in range(2): cp(a("BXF", 16 * h, 16 * h + 16), blands(S)[0][0])
     flip(sm("b0"))
     dma("a", T.yb[:], sm("b0"), 8)
-    ts(nf(0), io5(0, 256), c_(pm, 256.0, A.mult), A.add)
-    ts(nf(1), P(0, 0, 16), 0.0, A.is_gt, 3840.0, A.mult); tt(nf(1), P(0, 0, 16), nf(1), A.add)
-    tt(nf(1), nf(1), nf(0), A.max)
+    act(nf(0), io5(0, 256), bias=c_(pm, 256.0, A.mult))
+    tt(nf(1), P(0, 0, 16), nf(0), A.max)
     dma("s", T.yj[:], nf(1), 128)
 
     n = len(ops)
@@ -546,7 +570,9 @@ def rank_program(g, core, T, topo):
         prio[i] = ops[i]["c"] + max([prio[k] + (ops[i]["lat"] if pred[k][i] else 0) for k in succ[i]] + [ops[i]["lat"] if ops[i]["dma"] else 0])
     tail = [ops[i]["lat"] if ops[i]["dma"] else 0 for i in range(n)]
 
-    def run(before, after, gap, first, pr, peek):
+    eng = [o["e"] for o in ops]; cost = [o["c"] for o in ops]; NEVER = 1e18
+
+    def run(before, after, first, pr, peek):
         left = [len(p) for p in before]
         ready = list(first); fin = [0.0] * n
         free = {q: 0.0 for q in "vapgsx"}
@@ -554,23 +580,33 @@ def rank_program(g, core, T, topo):
         for i in range(n):
             if not left[i]: pool[ops[i]["e"]].append(i)
         seq = []
-        while len(seq) < n:
-            s0, q = min((max(free[q_], min(ready[i] for i in p)), q_) for q_, p in pool.items() if p)
-            i = max((i for i in pool[q] if ready[i] <= s0 + peek), key=lambda k: (pr[k], -k))
-            pool[q].remove(i); seq.append(i)
-            end = max(free[q], ready[i]) + ops[i]["c"]; free[q] = end; fin[i] = end
-            for k in after[i]:
-                ready[k] = max(ready[k], end + gap(i, k)); left[k] -= 1
-                if not left[k]: pool[ops[k]["e"]].append(k)
+        soon = {q: min([ready[i] for i in p], default=NEVER) for q, p in pool.items()}
+        for _ in range(n):
+            s0 = NEVER
+            for q_, x in soon.items():
+                if x < free[q_]: x = free[q_]
+                if x < s0: s0 = x; q = q_
+            p = pool[q]; s0 += peek; top = -NEVER
+            for k in p:
+                if ready[k] <= s0 and pr[k] > top: top = pr[k]; i = k
+            p.remove(i); seq.append(i)
+            soon[q] = min([ready[k] for k in p], default=NEVER)
+            end = max(free[q], ready[i]) + cost[i]; free[q] = end; fin[i] = end
+            for k, gp in after[i]:
+                if end + gp > ready[k]: ready[k] = end + gp
+                left[k] -= 1
+                if not left[k]:
+                    pool[eng[k]].append(k)
+                    if ready[k] < soon[eng[k]]: soon[eng[k]] = ready[k]
         return seq, fin
 
     if "order" not in PLAN:
-        span = {"MSG": MW, "OUT": 256, "BOX": 32, "BOXO": 32}
+        span = {"MSG": MW, "OUT": 256, "BOX": 32, "BOXO": 32, "LOOK": 32}
         keys = ["%s%s%d" % (o["e"], o["w"][0][0], o["w"][0][3] % span.get(o["w"][0][0], 1 << 20)) if o["w"] else "send" for o in ops]
         keys = [k + ("." if i < marks[1] else "!" if i >= marks[S - 1] else "") for i, k in enumerate(keys)]
-        pl = [list(p.items()) for p in pred]; eng = [o["e"] for o in ops]
-        sets = [([o["c"] * (kp if o["e"] == "p" else 1) + o.get("g", 0) * kg + o.get("s", 0) * ks for o in ops],
-                 [sy if o["lat"] == SYNC else o["lat"] for o in ops], wt) for kg, ks, kp, sy, wt in SETTINGS]
+        pl = [list(p.items()) for p in pred]
+        sets = [([o["c"] * (kp if o["e"] == "p" else 1) + o.get("g", 0) * kg + o.get("s", 0) * ks + o.get("fix", 0) * kf for o in ops],
+                 [sy if o["lat"] == SYNC else wire if o["lat"] == WIRE else o["lat"] for o in ops], wt) for kg, ks, kp, sy, wt, kf, wire in SETTINGS]
 
         def score(seq):
             r = []
@@ -585,9 +621,10 @@ def rank_program(g, core, T, topo):
                     if s_ + tail[i] > mx: mx = s_ + tail[i]
                 r.append(mx)
             return sum(x * y[2] for x, y in zip(r, sets)), r
-        forward = lambda pr: run(pred, succ, lambda i, k: ops[i]["lat"] if pred[k][i] else 0, [0.0] * n, pr, PEEK)
+        ahead = [[(k, ops[i]["lat"] if pred[k][i] else 0) for k in succ[i]] for i in range(n)]
+        forward = lambda pr: run(pred, ahead, [0.0] * n, pr, PEEK)
         seq, fin = forward(prio)
-        base = run(succ, pred, lambda i, k: ops[k]["lat"] if pred[i][k] else 0, tail, fin, PEEK)[1]
+        base = run(succ, [[(k, ops[k]["lat"] if wait else 0) for k, wait in pred[i].items()] for i in range(n)], tail, fin, PEEK)[1]
         rng = np.random.default_rng(SEED)
         more = dict.fromkeys(keys, 0.0)
         seq = forward(base)[0]; best = score(seq) + (seq,)
@@ -601,6 +638,75 @@ def rank_program(g, core, T, topo):
             for k in set(keys[j] for j in near): trial[k] += step
             seq = forward([x + trial[k] for x, k in zip(base, keys)])[0]; got = score(seq)
             if got[0] <= best[0]: best = got + (seq,); more = trial
+        seq = best[2]
+        below = [0] * n; lean = [None] * n
+        for i in range(n):
+            far = 0
+            for j in pred[i]: far |= below[j]
+            lean[i] = [(j, wait) for j, wait in pl[i] if not far >> j & 1 or ops[j]["dma"]]
+            for j in pred[i]: far |= 1 << j
+            below[i] = far
+        stepof = [sum(i >= m for m in marks) for i in range(n)]
+        seen = {}; twin = {}; name = []
+        for i in range(n):
+            k = (keys[i].rstrip(".!"), stepof[i]); seen[k] = seen.get(k, 0) + 1
+            name.append((k[0], seen[k])); twin[name[i], stepof[i]] = i
+        qn = ["vapgsx".index(x) for x in eng]
+        wts = [x[2] for x in sets]
+        lean4 = [[(j,) + tuple(x[1][j] if wait else 0 for x in sets) for j, wait in lean[i]] for i in range(n)]
+        cost4 = [tuple(x[0][i] for x in sets) for i in range(n)]
+
+        def times(seq):
+            f0 = [0.0] * n; f1 = [0.0] * n; f2 = [0.0] * n; f3 = [0.0] * n
+            last = [n - 1] * 6
+            for i in seq:
+                q = qn[i]; p = last[q]; last[q] = i
+                s0 = f0[p]; s1 = f1[p]; s2 = f2[p]; s3 = f3[p]
+                for j, l0, l1, l2, l3 in lean4[i]:
+                    x = f0[j] + l0
+                    if x > s0: s0 = x
+                    x = f1[j] + l1
+                    if x > s1: s1 = x
+                    x = f2[j] + l2
+                    if x > s2: s2 = x
+                    x = f3[j] + l3
+                    if x > s3: s3 = x
+                c = cost4[i]
+                f0[i] = s0 + c[0]; f1[i] = s1 + c[1]; f2[i] = s2 + c[2]; f3[i] = s3 + c[3]
+            fs = (f0, f1, f2, f3); r = [max(f[i] + tail[i] for i in ends) for f in fs]
+            return sum(x * y for x, y in zip(r, wts)), r, fs
+
+        def held_up(seq, fs):
+            before = {}; last = {}
+            for i in seq: before[i] = last.get(qn[i]); last[qn[i]] = i
+            r = []
+            for k, f in enumerate(fs):
+                i = max(ends, key=lambda e: f[e] + tail[e])
+                while i is not None:
+                    s0 = f[i] - cost4[i][k] - 1e-6
+                    up = [x[0] for x in lean4[i] if f[x[0]] + x[1 + k] >= s0]
+                    if up: i = up[0]
+                    elif before[i] is not None and f[before[i]] >= s0: r.append((i, before[i])); i = before[i]
+                    else: i = None
+            return r, before
+        ends = [i for i in range(n) if not succ[i]]
+        now = times(seq); pairs, before = held_up(seq, now[2]); best = (now[0], now[1], seq)
+        for _ in range(PULLS):
+            i, j = pairs[int(rng.integers(len(pairs)))]
+            for _d in range(int(rng.choice((0, 0, 1, 2, 4, 8)))):
+                if before[j] is not None and not below[i] >> before[j] & 1: j = before[j]
+            new = list(seq)
+            for d in range(-S, S + 1) if rng.random() < 0.7 else (0,):
+                x, y = twin.get((name[i], stepof[i] + d)), twin.get((name[j], stepof[j] + d))
+                if x is None or y is None or below[x] >> y & 1: continue
+                lo, hi = new.index(y), new.index(x)
+                if lo < hi:
+                    part = new[lo:hi]; m = below[x]
+                    new[lo:hi + 1] = [k for k in part if m >> k & 1] + [x] + [k for k in part if not m >> k & 1]
+            got = times(new)
+            if got[0] <= now[0] + SLACK * rng.random() * (1 - _ / PULLS):
+                seq, now = new, got; pairs, before = held_up(seq, now[2])
+                if now[0] < best[0]: best = (now[0], now[1], seq)
         PLAN["deps"], PLAN["order"], PLAN["span"] = deps, best[2], best[1]
         PLAN["ops"], PLAN["marks"], PLAN["pred"] = ops, marks, pred
     order = PLAN["order"]
@@ -649,15 +755,20 @@ def rank_program(g, core, T, topo):
         g.wait_ge(T.sem["d%d" % k], 16)
     for nm, v in expect.items():
         g.wait_ge(T.sem[nm], v)
-    g.wait_ge(T.sem.sent, nen * 2 * S)
+    g.wait_ge(T.sem.sent, nen * (2 * S + 1))
 
 
-ACT = 0
-GB_ON_VECTOR = (0, 2, 4)
+ACT = 40
+ROUND = 1.5 * 2 ** 23
+ROUND_ON_VECTOR = False
+PIECES = (0, 8, 16)
+BANKS = ((0, 7, 1), (6, 5, 0))
+X_ON_SCALAR = ((), (0, 1))
+GB_ON_VECTOR = (6, 7)
 LOW_ON_VECTOR = tuple(range(16))
-SPREAD_ON_VECTOR = ()
+SPREAD_ON_VECTOR = tuple(range(16))
 DIGITS_ON_VECTOR = (1, 3, 5)
 TAKE_ON_VECTOR = False
 OUT_ON_VECTOR = False
-V2_ON_VECTOR = ()
+V2_ON_VECTOR = (1,)
 LAST_ON_VECTOR = (1, 3)

import numpy as np
from concourse.bass import DstId, RemoteDMATransfer
from concourse.mybir import AluOpType as A, ActivationFunctionType as F

S = 8
MW = 1024
XC = 8704
SPARE, ZERO, LONG = 4096, 4352, 4096
f32, bf, i32, u16 = "float32", "bfloat16", "int32", "uint16"
SCRATCH = {
    "X": ("sbuf", [128, XC], bf), "PQ": ("sbuf", [128, 8192], bf), "IOT": ("sbuf", [128, 8192], i32),
    "GB": ("sbuf", [128, 8704], bf), "E2": ("sbuf", [128, 1024], bf), "DD": ("sbuf", [128, 4096], bf), "G1": ("sbuf", [128, 4096], bf),
    "E": ("sbuf", [128, 16, 256], bf), "IOS": ("sbuf", [128, 1024], f32), "IO": ("sbuf", [128, 512], f32),
    "TT": ("sbuf", [128, 1536], f32), "TB": ("sbuf", [128, 1024], bf), "SBI": ("sbuf", [128, 1024], i32), "SBU": ("sbuf", [128, 512], u16),
    "VR": ("sbuf", [128, 1536], f32), "V2": ("sbuf", [128, 1024], bf),
    "MSG": ("sbuf", [128, MW * S + 256], bf), "OUT": ("sbuf", [128, 256 * S], bf),
    "BOX": ("sbuf", [128, 32 * (S + 1)], u16), "LOOK": ("sbuf", [128, 32 * (S + 2)], u16), "BOXO": ("sbuf", [128, 32 * S], u16),
    "XD": ("sbuf", [128, 16, 16], bf), "T2": ("sbuf", [128, 16, 16], f32), "MN": ("sbuf", [128, 512], f32),
    "W": ("sbuf", [128, 256 * 10], f32), "WI": ("sbuf", [128, 512], i32), "WB": ("sbuf", [128, 256 * 16], bf),
    "SM": ("sbuf", [128, 16 * 72], f32), "SI": ("sbuf", [128, 16 * 8], i32),
    "SH": ("sbuf", [128, 16 * 12], bf), "L": ("sbuf", [128, 16 * 64], u16), "LB": ("sbuf", [128, 256 * 5], u16),
    "MAT": ("sbuf", [128, 144 * 8 + 128 * 15 + 256 * 4], bf), "SEL": ("sbuf", [128, 128 * 32], bf), "IF": ("sbuf", [128, 128 * 8], f32),
    "T5": ("sbuf", [128, 512 * 3], f32),
    "NI": ("sbuf", [128, 512], i32), "NF": ("sbuf", [128, 256 * 3], f32), "NB": ("sbuf", [128, 256 * 6], bf),
    "BXI": ("sbuf", [128, 32], i32), "BXF": ("sbuf", [128, 64], f32), "LI": ("sbuf", [128, 4], i32),
    "JK": ("sbuf", [128, 16], bf), "RST": ("sbuf", [128, 256], f32), "QR": ("sbuf", [128, 512], f32),
}
for _b in range(4):
    SCRATCH["AD%d" % _b] = ("sbuf", [128, 16, 4, 16], bf)
for _b in range(8):
    SCRATCH["P%d" % _b] = ("psum", [128, 32, 16] if _b != 2 else [128, 512], f32)
ROW = [4 * (k & 3) + (k >> 2) for k in range(16)]
NDMA = 72
SEMAPHORES = ["ev", "ea", "ep", "eg", "sent", "box0"] + [nm + str(t) for t in range(1, S + 1) for nm in ("arr", "box")] + ["d%d" % k for k in range(NDMA)]
SIZE = {f32: 4, bf: 2, i32: 4, u16: 2}
GATHER, SCATTER, TENSOR, SYNC, WIRE = 1.56, 3.8, 0.55, 70, 2800
ALL = (1 << 128) - 1
PEEK, SEED, TRIES, MOVES = 130, 1, 1000, (150, 400, 1000, 2500, 6000)
SETTINGS = ((0, 0, 1, 70, 0.35, 0, 2800), (-0.46, -1.6, 1.05, 60, 0.3, 0, 2800), (0.44, 1.7, 0.9, 80, 0.15, -40, 2400), (-0.2, -0.6, 1.2, 110, 0.2, 30, 4200))
PULLS, SLACK = 22000, 20
PLAN = {}
MASKS = {}


def cover(x):
    if x[:2] not in MASKS:
        shape = SCRATCH[x[0]][1][1:]
        cols = np.arange(int(np.prod(shape))).reshape(shape)[tuple(i if isinstance(i, int) else slice(*i) for i in x[1])].reshape(-1)
        bits = np.zeros(int(np.prod(shape)), np.uint8); bits[cols] = 1
        MASKS[x[:2]] = (int.from_bytes(np.packbits(bits, bitorder="little").tobytes(), "little"), int(cols.min()), int(cols.size))
    return MASKS[x[:2]]


def rank_program(g, core, T, topo):
    rank = T.rank_of(core)
    if rank is None:
        return
    ahead_ = {k: T.cores[(rank + k) % len(T.cores)] for k in (1, 2)}
    to = {k: topo.addr(c) for k, c in ahead_.items()}
    emask = topo.mask(core, ahead_[1]) & topo.mask(core, ahead_[2])
    nen = len(set(topo.engines(core, ahead_[1])) & set(topo.engines(core, ahead_[2])))
    ops = []
    ndma = [0]
    expect = {}

    def a(name, lo, hi, step=1, ps=None):
        return (name, ((lo, hi, step),), ps)

    def b(name, *idx):
        return (name, tuple(i if isinstance(i, int) else tuple(i) + (1,) * (3 - len(i)) for i in idx), None)

    def P(k, lo, hi=None, step=1):
        return b("P%d" % k, lo, (0, 16)) if hi is None else b("P%d" % k, (lo, hi, step), (0, 16))

    def ind(win, off):
        return ("ind", win, off)

    def ap(x):
        if not isinstance(x, tuple):
            return x
        if x[0] == "ind":
            return ap(x[1]).indirect(ap(x[2]))
        ps = slice(None) if x[2] is None else slice(*x[2])
        return T[x[0]][(ps,) + tuple(i if isinstance(i, int) else slice(i[0], i[1]) if i[2] == 1 else slice(*i) for i in x[1])]

    def regs(xs):
        r = []
        for x in xs:
            if isinstance(x, tuple):
                r += regs([x[1], x[2]]) if x[0] == "ind" else [(x[0], cover(x)[0], ALL if x[2] is None else sum(1 << p for p in range(*x[2])), cover(x)[1])]
        return r

    def wid(x):
        return 16 * wid(x[2]) if x[0] == "ind" else cover(x)[2]

    def op(eng, fn, out, ins, cost):
        if isinstance(out, tuple) and out[0] == "ind":
            w_, r_ = regs([out[1]]), regs(list(ins) + [out[2]])
        else:
            w_, r_ = regs([out]), regs(ins)
        ops.append({"e": eng, "f": [fn], "w": w_, "r": r_, "dma": None, "c": cost, "lat": SYNC})
        if isinstance(out, tuple) and out[0] == "ind": ops[-1]["s"] = wid(out)
        elif ins and isinstance(ins[0], tuple) and ins[0][0] == "ind": ops[-1]["g"] = wid(out)

    def vc(o, i, k=1.0):
        if o[0] == "ind": return 60 + wid(o) * SCATTER
        if i[0] == "ind": return 60 + wid(o) * GATHER
        if SIZE[SCRATCH[o[0]][2]] == 2 and SIZE[SCRATCH[i[0]][2]] == 2: k *= 0.5
        return max(64, wid(o) * k)

    def ps(x): return x[0] != "ind" and SCRATCH[x[0]][0] == "psum"
    def cp(o, i): op("v", lambda: g.vector.tensor_copy(ap(o), ap(i)), o, [i], vc(o, i))
    def tt(o, x, y, f): op("v", lambda: g.vector.tensor_tensor(ap(o), ap(x), ap(y), f), o, [x, y], vc(o, x, 1.0 if ps(x) or ps(y) else 2.0))
    def ts(o, x, s1, f0, s2=None, f1=None):
        if f1 is None: op("v", lambda: g.vector.tensor_scalar(ap(o), ap(x), ap(s1), None, f0), o, [x, s1], vc(o, x))
        else: op("v", lambda: g.vector.tensor_scalar(ap(o), ap(x), ap(s1), ap(s2), f0, f1), o, [x, s1, s2], vc(o, x))
    def scan(o, d0, d1, f0, f1): op("v", lambda: g.vector.tensor_tensor_scan(ap(o), ap(d0), ap(d1), 0.0, f0, f1), o, [d0, d1], vc(o, d1))
    def tp(o, i): op("v", lambda: g.vector.transpose(ap(o), ap(i)), o, [i], vc(o, i))
    def ms(o, c): op("v", lambda: g.vector.memset(ap(o), c), o, [], vc(o, o))
    def act(o, i, fn=F.Identity, bias=0.0, scale=1.0, acc=None):
        c = 78 + wid(o) * GATHER if i[0] == "ind" else max(64, wid(o)) + ACT
        if acc is None: op("a", lambda: g.scalar.activation(ap(o), ap(i), fn, bias=ap(bias), scale=ap(scale)), o, [i, bias, scale], c)
        else: op("a", lambda: g.scalar.activation(ap(o), ap(i), fn, bias=ap(bias), scale=ap(scale), accum_out=ap(acc)), acc, [i, bias, scale], c + 24)
        if acc is not None: ops[-1]["w"] += regs([o])
        if i[0] != "ind": ops[-1]["fix"] = 1
    def mul(on_v, o, i, s):
        if on_v: ts(o, i, s, A.mult)
        else: act(o, i, scale=s)
    def get(on_v, o, i): (cp if on_v else act)(o, i)
    def mms(items):
        fs = [(lambda o, l, r, st, sp: lambda: g.tensor.matmul(ap(o), ap(l), ap(r), st, sp))(*x) for x in items]
        ops.append({"e": "p", "f": fs, "w": list(set(regs([x[0] for x in items]))), "r": list(set(regs([x[1] for x in items] + [x[2] for x in items]))), "dma": None,
                    "c": sum(TENSOR * max(64, wid(x[2])) * (4 if SCRATCH[x[1][0]][2] == f32 else 1) for x in items), "lat": SYNC})
    def acc(o, pairs, start=True, stop=True): return [(o, l, r, start and k == 0, stop and k == len(pairs) - 1) for k, (l, r) in enumerate(pairs)]
    def iota(o, pat, base, cm):
        if SCRATCH[o[0]][2] != i32: op("g", lambda: g.iota(ap(o), pat, base, cm, allow_small_or_imprecise_dtypes=True), o, [], 160 + 2 * wid(o))
        else: op("g", lambda: g.iota(ap(o), pat, base, cm), o, [], 160 + 2 * wid(o))
    def pick(o, i, step, base):
        op("g", lambda: g.affine_select(ap(o), ap(i), [[0, wid(o) // 16], [step, 16]], A.is_gt, 0.0, base, 0), o, [i], 200 + 2 * wid(o))
    def dma(q, o, i, kb):
        eng = {"s": g.sync, "a": g.scalar}[q]
        op(q, lambda: eng.dma_start(ap(o), ap(i)), o, [i], 60)
        ops[-1]["dma"] = "d%d" % ndma[0]; ops[-1]["lat"] = 2400 + 5 * kb
        ndma[0] += 1
    def arrival(nm, t, lands, after):
        ops.append({"e": "x", "f": [], "w": regs([x for x, _ in lands]), "r": [], "dma": nm + str(t), "c": 0, "lat": 0, "after": after})
        expect[nm + str(t)] = nen * len(lands)
    def send(nm, t, src, lands):
        sem = T.sem[nm + str(t)]
        if len(lands) == 1:
            op("g", lambda: g.remote_dma(ap(lands[0][0]), ap(src), sem, T.sem.sent, to[1][1], to[1][0], emask), None, [src], 600)
        else:
            op("g", lambda: g.remote_dma_fused([RemoteDMATransfer(dst_ids=[DstId(rid=to[k][0], pnc=to[k][1]) for _, k in lands], dma_engine_mask=emask, remote_sem=sem,
                                                                  src=ap(src), dsts=[ap(x) for x, _ in lands])], local_sem=T.sem.sent), None, [src], 600)
        ops[-1]["dma"] = "remote"; ops[-1]["lat"] = WIRE
        return len(ops) - 1
    def zlands(t): return [(a("MSG", MW * t + 256 * h, MW * t + 256 * h + 256), 1) for h in range(2 if t < S else 1)]
    def blands(t):
        here, then = a("BOX", 32 * t, 32 * t + (32 if t < S else 16)), a("LOOK", 32 * t + 32, 32 * t + 64)
        return [(then, 1)] if t == 0 else [(here, 1), (then, 2)] if t < S - 1 else [(here, 1)]

    at = {"SM": 0, "L": 0, "SH": 0}
    def slot(buf, name, n):
        if (buf, name) not in at:
            at[(buf, name)] = at[buf]; at[buf] += n
        return a(buf, at[(buf, name)], at[(buf, name)] + n)
    def sm(name, n=16): return slot("SM", name, n)
    def sh(name, n=16): return slot("SH", name, n)
    def col(name): return slot("SM", name, 1)
    def li(name, n=16): return slot("L", name, n)
    def sub(x, lo, hi, step=1): return a(x[0], x[1][0][0] + lo, x[1][0][0] + hi, step)
    def w(k): return a("W", 256 * k, 256 * k + 256)
    def wb(k, n=1): return a("WB", 256 * k, 256 * (k + n))
    def si(k, n=16): return a("SI", 16 * k, 16 * k + n)
    def lb(k): return a("LB", 256 * k, 256 * k + 256)
    def YM(k): return a("MAT", 144 * k, 144 * k + 144)
    def Y(k, r): return a("MAT", 144 * k + 15 - r, 144 * k + 143 - r)
    def MT(k): return a("MAT", 1152 + 128 * k, 1280 + 128 * k)
    def MF(k): return a("IF", 128 * k, 128 * k + 128)
    def M2(k): return a("MAT", 2688 + 256 * k, 2944 + 256 * k)
    KC, LUT, IDT, ONES = M2(0), M2(1), M2(2), M2(3)
    I128, BLK, NEG, HALF, ME, MG, NBLK, NIL = MT(4), MT(5), MT(6), MT(7), MT(8), MT(9), MT(10), MT(11)
    SA, SE, SF = (a("MAT", 3712 + 128 * k, 3840 + 128 * k) for k in range(3))
    IF, NF, BIG, NBIG = MF(4), MF(5), MF(6), MF(7)
    def LOW(r): return a("SEL", 128 * r, 128 * r + 128)
    def SPREAD(r): return a("SEL", 2048 + 128 * r, 2176 + 128 * r)
    def io5(lo, hi): return a("IO", lo, hi)
    def nf(k): return a("NF", 256 * k, 256 * k + 256)
    def nb(k): return a("NB", 256 * k, 256 * k + 256)
    def t5(k): return a("T5", 512 * k, 512 * k + 512)
    def grp(name, f, n): return a(name, 0, n, 1, (f, 128, 16))
    def wsel(out, k, src, lo, n, first=(), start=True, to=range(16)):
        mms(acc(out, list(first) + [(Y(k, to[r]), a(src, lo + r, lo + n, 16)) for r in range(16)], start))
    TH, TS, TD = a("TT", 0, 512), a("TT", 512, 1024), a("TT", 1024, 1536)
    IOB, TC = a("TB", 0, 512), a("TB", 512, 1024)

    for h in range(2):
        dma("a", a("BXI", 16 * h, 16 * h + 16), T.bx[:], 8)
    dma("s", a("X", 0, 4096), T.xs[:], 1024)
    dma("a", a("NI", 256, 512), T.he[:], 128)
    for k in range(16):
        dma("sa"[k & 1], a("SBI", 512, 1024, 1, (k, 128, 16)), T.sb[ROW[k]:128:16, :], 16)
    dma("s", a("SBI", 0, 512), T.sb[:], 256)
    dma("a", a("NI", 0, 256), T.pe[:], 128)
    for x, _ in zlands(0): dma("a", x, T.zs[:], 64)
    for k in range(16):
        dma("s", grp("LI", k, 2), T.lim[:], 1)
    iota(si(0, 1), [[0, 1]], 0, 1)
    iota(io5(0, 512), [[1, 512]], 0, 0)
    iota(a("QR", 0, 256), [[1, 4], [4, 4], [0, 16]], 0, 0)
    iota(a("QR", 256, 512), [[0, 16], [1, 16]], 0, 0)
    iota(a("IOS", 0, 1024), [[1, 64], [256, 16]], 0, 0)
    iota(KC, [[1, 16], [16, 4], [64, 4]], 0, 0)
    iota(IOB, [[1, 512]], -256, 0)
    iota(ONES, [[0, 256]], 1, 0)
    iota(NIL, [[0, 128]], 0, 0)
    iota(wb(1), [[0, 256]], 128, 0)
    iota(sub(wb(12), 0, 16), [[0, 16]], 0, 0)
    for c in range(16):
        iota(a("IOT", 512 * c, 512 * c + 512), [[1, 512]], 512 * c, 0)
    for c in range(8, 17):
        iota(a("X", 512 * c, 512 * c + 512), [[0, 512]], 0, 0)
        if c < 16: iota(a("PQ", 512 * c, 512 * c + 512), [[0, 512]], 0, 0)
    iota(col("round"), [[0, 1]], int(ROUND), 0); iota(col("nround"), [[0, 1]], -int(ROUND), 0)
    iota(a("GB", 0, 512), [[0, 512]], 0, 0)
    pf, pm, p16, par = col("pf"), col("pm"), col("p16"), col("par")
    nc = [0]
    def tmp():
        nc[0] += 1
        return col("tmp%d" % nc[0])
    def bit(m):
        nc[0] += 1
        x = a("SI", 16 + nc[0] % 16, 17 + nc[0] % 16)
        ts(x, si(0, 1), m, A.bitwise_and)
        return x
    def c_(x, s1, f0, s2=None, f1=None):
        o = tmp(); ts(o, x, s1, f0, s2, f1); return o
    cp(pf, si(0, 1))
    for o, m in ((pm, 15), (par, 16)):
        cp(o, bit(m))
    tt(p16, pf, pm, A.subtract)
    i16 = io5(0, 16)
    ts(YM(0), io5(0, 144), c_(p16, 15.0, A.add), A.is_equal)
    ts(IF, io5(0, 128), pf, A.is_equal)
    act(I128, IF); act(NEG, IF, scale=-1.0); act(HALF, IF, scale=0.5);
    act(NF, IF, scale=-1.0); act(BIG, IF, scale=16384.0); act(NBIG, IF, scale=-16384.0)
    for c in range(2):
        on = c_(par, 16.0 * c, A.is_equal)
        for h in range(2):
            ts(MF(2 * c + h), io5(0, 128), c_(pf, 16.0 * (h - c), A.add), A.is_equal, on, A.mult)
            act(MT(2 * c + h), MF(2 * c + h), scale=1.0 / 16)
    par1 = c_(par, 1.0 / 16, A.mult)
    def flip(o):
        tp(a("BXF", 32, 64), a("BXF", 0, 32))
        tt(o, a("BXF", 48, 64), a("BXF", 32, 48), A.subtract); ts(o, o, par1, A.mult); tt(o, o, a("BXF", 32, 48), A.add)
    cp(a("BXF", 0, 32), a("BXI", 0, 32)); flip(sm("b0"))
    cp(a("BOX", 0, 16), sm("b0")); ms(a("BOX", 16, 32), 0)
    cp(TS, a("SBI", 512, 1024))
    d256, dW, q16 = sm("d256"), sm("dW"), sm("q16")
    ts(d256, i16, 16.0, A.mult, c_(pm, 256.0, A.add), A.add)
    act(dW, d256, bias=SPARE - 256.0); act(q16, i16, scale=1.0 / 16)
    iota(sm("row"), [[1, 4], [4, 4]], 0, 0)
    ts(li("reo"), sm("row"), c_(pm, 16.0, A.mult), A.add)
    qk, rk = a("QR", 0, 256), a("QR", 256, 512)
    act(KC, KC, scale=1.0 / 256)
    RST = a("RST", 0, 256)
    act(RST, rk, F.Relu, scale=-65536.0, bias=65536.0)
    ts(LUT, qk, pm, A.not_equal, -2048.0, A.mult)
    act(IDT, io5(0, 256), scale=2.0 ** -18)
    for c in range(2): act(a("E2", 512 * c, 512 * c + 512), io5(0, 512), scale=0.0)
    for c in range(4):
        dma("s", a("PQ", 1024 * c, 1024 * c + 1024), a("E2", 0, 1024), 256)
    ts(a("T5", 0, 128), io5(0, 128), p16, A.subtract, -7.5, A.add)
    act(a("T5", 128, 256), a("T5", 0, 128), F.Abs)
    ts(BLK, a("T5", 128, 256), 8.0, A.is_lt)
    ts(sm("low"), i16, pm, A.is_gt, 2.0, A.mult); ts(sm("one"), i16, pm, A.is_equal, 2048.0, A.mult)
    for r in range(16):
        mul(r in LOW_ON_VECTOR, LOW(r), Y(0, r), sub(sm("low"), r, r + 1))
        mul(r in SPREAD_ON_VECTOR, SPREAD(r), BLK, sub(sm("one"), r, r + 1))
    cp(lb(2), a("NI", 256, 512))
    ts(a("NB", 0, 512), a("NI", 0, 512), -256.0, A.add)
    for f in range(2):
        dma("s", grp("PQ", f, 4096), nb(f), 64)
    p8 = None
    for k in range(3):
        x = c_(c_(bit(1 << k), 0.0, A.is_gt, 8.0 ** (1 << k) - 1.0, A.mult), 1.0, A.add)
        p8 = x if p8 is None else c_(x, p8, A.mult)
    r8 = tmp(); op("v", lambda: g.vector.reciprocal(ap(r8), ap(p8)), r8, [p8], 240)
    one = [sub(sm("one"), k, k + 1) for k in range(4)]
    m0 = c_(one[0], 1.0 / 2048, A.mult); m1 = c_(one[1], 1.0 / 2048, A.mult)
    for k, wt in ((1, c_(pm, 1.0, A.add, 512.0, A.mult)), (2, c_(r8, 128.0, A.mult)), (3, m0), (4, m1), (5, c_(one[2], 1.0 / 2048, A.mult, m1, A.add)),
                  (6, c_(one[3], 1.0 / 2048, A.mult)), (7, c_(c_(one[1], 128.0, A.mult, c_(one[2], 1.875, A.mult), A.add), c_(one[0], 0.125, A.mult), A.add))):
        act(YM(k), YM(0), scale=wt)
    act(ME, I128, scale=m0); ts(MG, io5(0, 128), c_(pf, 1.0, A.add), A.is_equal, m0, A.mult)
    act(NBLK, BLK, scale=-1.0)
    pm1 = sub(wb(0), 0, 128); two = sub(wb(0), 128, 256); four = sub(wb(6), 0, 128); mid = sub(wb(6), 128, 256)
    iota(pm1, [[0, 64], [-2, 2]], 1, 0); tt(pm1, pm1, BLK, A.mult)
    pick(two, pm1, -1, 2); pick(four, pm1, -1, 4); pick(mid, four, 1, -1)
    act(SE, two, scale=m1); act(SF, mid, scale=m1); act(SA, four, scale=c_(m0, -1.0, A.mult))
    thr = sm("thr", 32)
    ts(col("n4"), sub(sm("one"), 4, 5), -1.0, A.mult)
    ts(col("lim0"), a("LI", 0, 1), -1.0, A.add, col("n4"), A.mult); ts(col("sl"), a("LI", 1, 2), 1.0, A.add, 1012.0, A.min)
    ts(sub(thr, 0, 16), i16, 0.0, A.mult, col("sl"), A.add); ms(sub(thr, 16, 32), 1012.0)
    ms(si(6, 1), 0)
    for h in range(2):
        ts(col("vs%d" % h), pm, 8.0, A.is_ge if h else A.is_lt, p8, A.mult)

    cp(a("SBU", 0, 512), a("SBI", 0, 512))
    for c in range(4):
        win = a("VR", 512 * c - 512, 512 * c) if c else TS
        if c: act(win, TS, bias=-64.0 * c)
        tt(a("G1", 1024 * c, 1024 * c + 1024), ind(win, a("LB", 512 + 64 * c, 576 + 64 * c)), a("IOS", 0, 1024), A.is_equal)
        wsel(P(0, 4 * c, 4 * c + 4), 1, "G1", 1024 * c, 1024, [(I128, sub(nb(1), 64 * c, 64 * c + 64))])
        wsel(P(0, 16 + 4 * c, 20 + 4 * c), 2, "G1", 1024 * c, 1024)
    iota(a("VR", 0, 768), [[0, 768]], 0, 0)
    kh, sc = P(0, 0, 16), P(0, 16, 32)
    ts(nb(2), kh, 512.0 * 9 - 256, A.is_ge, 512.0, A.mult); act(nb(3), sc)
    for f in range(2, 4):
        dma("s", grp("PQ", f, 4096), nb(f), 64)
    ts(lb(3), kh, 256.0, A.add)
    for c in range(8):
        get(c in GB_ON_VECTOR, a("GB", 512 + 1024 * c, 1536 + 1024 * c), ind(a("PQ", 0, 4096), a("SBU", 64 * c, 64 * c + 64)))
        for bank, k in ((0, 5), (6, 6), (7, 4)):
            wsel(P(bank, 4 * c, 4 * c + 4), k, "GB", 512 + 1024 * c, 1024, to=ROW)
    act(TD, P(0, 0, 32), bias=256.0)
    act(TC, P(6, 0, 32))
    tt(t5(1), P(7, 0, 32), IOB, A.is_equal); act(t5(2), t5(1), scale=0.25, bias=LONG + 256.0); tt(TH, P(7, 0, 32), t5(2), A.add)

    def lowest(keys, own, on, out, more=()):
        for q in range(16):
            ts(b("E", q, (0, 256 - 16 * q)), sub(keys, 16 * q, 256), own(q), A.is_equal, sub(on, q, q + 1), A.mult)
            if q < 15: mms([(P(3, q + 1, 16), BLK, b("E", q, (16, 256 - 16 * q)), q == 0, q == 14)])
        mms(acc(out, list(more) + [(LOW(r), b("E", (0, 16), r)) for r in range(1, 16)], True, False))
        act(sub(wb(12), 16, 256), P(3, 1, 16))
        wsel(out, 0, "WB", 256 * 12, 256, start=False)

    def spread(bank, lo, x):
        return [(b("P%d" % bank, (lo, lo + 16), r), SPREAD(r), x, False, False) for r in range(16)]

    XW = a("X", 0, XC)
    def zof(u, h=0): return a("MSG", MW * u + 256 * h, MW * u + 256 * h + 256)
    def lst(t, k): return sub(li("up%d" % t, 64), 16 * k, 16 * k + 16)

    def updates(t):
        XW = a("X", 0, 5120 + 512 * t)
        if t >= 1: cp(ind(XW, lst(t - 1, 2 if 1 < t < S - 1 else 1)), zof(t - 1))
        if t >= 3: cp(ind(XW, lst(t - 2, 3)), zof(t - 2))
        cp(ind(XW, lst(t, 0)), wb(7))
        if t < S - 1: tt(ind(XW, lst(t, 1)), zof(t), wb(1), A.add)
        else: cp(ind(XW, lst(t, 1)), zof(t))
        if t < S - 1: cp(ind(a("PQ", 0, wid(XW)), lst(t, 0)), wb(5))

    sent = (send("box", 0, a("BOX", 0, 32), blands(0)), None)
    marks = []
    for t in range(S):
        marks.append(len(ops))
        z = zof(t); box, out = a("BOX", 32 * t, 32 * t + 16), a("BOX", 32 * t + 16, 32 * t + 32)
        look = a("LOOK", 32 * t, 32 * t + 16) if t else box
        XT = a("X", 0, 4608 + 512 * t if t else 4096)
        def by_box(x): return ind(x, look)
        if t:
            arrival("arr", t, zlands(t), sent[1])
            cp(lb(0), by_box(TD))
            act(wb(13), by_box(TC)); act(w(1), by_box(TS)); act(w(2), by_box(TH))
        else:
            act(w(1), by_box(TS))
        arrival("box", t, blands(t), sent[0])
        thA, ab, base, a3 = sh("thA"), sh("ab"), sm("base", 32), sm("a3")
        ts(thA, out, 0.0, A.is_equal, 1012.0, A.mult); ts(ab, look, -256.0, A.add)
        cp(sub(base, 0, 16), box)
        if t < S - 1: ts(sub(base, 16, 32), out, -1.0, A.add, 0.0, A.max)
        ts(a3, look, 256.0, A.mult); tt(a3, a3, i16, A.subtract)
        act(wb(14), by_box(IOB))
        cc = w(0)
        cuts = PIECES if t else (0, 16)
        for j, (lo, hi) in enumerate(zip(cuts, cuts[1:])):
            bw, bx_, bs = BANKS[j & 1]
            cut = lambda x: sub(x, 16 * lo, 16 * hi)
            T2 = b("T2", (lo, hi), (0, 16)); XD = b("XD", (lo, hi), (0, 16))
            if t:
                for Q in range(lo // 4, hi // 4):
                    for c in (2 * Q, 2 * Q + 1):
                        get(c in DIGITS_ON_VECTOR, a("G1", 512 * c, 512 * c + 512), ind(a("V2", 0, 1024), a("LB", 32 * c, 32 * c + 32)))
                    wsel(P(bw, 4 * Q, 4 * Q + 4), 0, "G1", 1024 * Q, 1024)
                if j == 0: updates(t - 1)
                wi = cut(a("WI", 0, 256))
                if t < S - 1:
                    tt(wi, P(bw, lo, hi), cut(wb(13)), A.mult)
                else:
                    tt(cut(w(3)), P(bw, lo, hi), cut(wb(13)), A.mult); ts(wi, cut(w(3)), -0.24, A.add)
                ts(wi, wi, 7, A.arith_shift_right, 7, A.bitwise_and)
                ts(XD, wi, 8192.0, A.mult)
                mms([(P(bx_, 16 + lo, 16 + hi), IF, cut(w(1)), True, False)])
                mms([(P(bx_, 16 + lo, 16 + hi), I128, XD, False, True)])
                tt(T2, P(bx_, 16 + lo, 16 + hi), cut(w(2)), A.min)
            else:
                act(T2, w(1))
            mms([(P(bs, lo, hi), NIL, cut(KC), True, False)])
            if t: mms([(P(bs, lo + c, hi, 2), MT(2 * c + h), b("XD", (lo + h, hi, 2), (0, 16)), False, False) for c in range(2) for h in range(2)])
            mms([(P(bs, lo + c, hi, 2), MF(2 * c + h), b("T2", (lo + h, hi, 2), (0, 16)), False, c + h == 2) for c in range(2) for h in range(2)])
            tp(cut(cc), P(bs, lo, hi))
        cU = lb(1)
        cp(cU, ind(cc, li("reo")))
        key, dl = a("P2", 0, 256), a("P2", 256, 512)
        mms([(dl, IF, cc, True, False), (sub(dl, 0, 255), NF, sub(cc, 1, 256), False, False), (sub(dl, 15, 255, 16), IF, sub(cc, 16, 256, 16), False, True)])
        if t and ROUND_ON_VECTOR: ts(w(9), cc, ROUND, A.add, -ROUND, A.add)
        elif t: act(w(9), cc, bias=col("round")); act(w(9), w(9), bias=col("nround"))
        mms(acc(key, ([(BIG, cc), (NBIG, w(9))] if t else []) + [(I128, KC)], True, False))
        lowest(wb(14), lambda q: sub(ab, q, q + 1), thA, P(4, 0), [(SPREAD(0), sub(ONES, 0, 16))] + 3 * [(NEG, thA)])
        sw, vo = sm("sw"), sm("vo")
        tt(sw, P(4, 0), d256, A.min); tt(vo, sw, ab, A.max); ts(li("vo"), vo, 256.0, A.add)
        zz = a("MSG", MW * t, MW * t + 512)
        on_scalar = list(zip(X_ON_SCALAR[min(t, 1)], (0, 7, 6, 1) if t else (5, 1) * 4))
        for c in range(8):
            dd, src, bank = a("DD", 512 * c, 512 * c + 512), ind(XT, sub(cU, 32 * c, 32 * c + 32)), dict(on_scalar).get(c)
            if bank is None: tt(dd, src, zz, A.subtract)
            else: act(dd, src); mms(acc(P(bank, 0, 32), [(I128, dd), (NEG, zz)]))
            for h in range(2):
                k = 2 * c + h
                act(b("AD%d" % (k >> 2), (0, 16), k & 3, (0, 16)), sub(dd, 256 * h, 256 * h + 256) if bank is None else P(bank, 16 * h, 16 * h + 16), F.Abs)
            if bank is not None and t == 0: act(dd, P(bank, 0, 32))
            if c & 1:
                Q = c >> 1
                mms(acc(sub(key, Q, 256, 4), [(Y(0, r), b("AD%d" % Q, (0, 16), (0, 4), r)) for r in range(16)], False, Q == 3))
        for c, bank in on_scalar if t else (): act(a("DD", 512 * c, 512 * c + 512), P(bank, 0, 32))
        mn = a("MN", 0, 256); m12 = a("MN", 15, 512, 16)
        scan(mn, RST, key, A.add, A.min)
        tt(w(7), mn, key, A.not_equal)
        scan(w(8), w(7), dl, A.mult, A.add)
        e = sub(w(8), 15, 256, 16)
        eU, cl = li("eU"), sm("cl")
        cp(eU, e)
        tt(cl, sub(mn, 15, 256, 16), thA, A.is_lt)
        cp(lb(4), ind(a("IOT", 0, wid(XT)), eU))
        tt(sub(w(3), 1, 256), sub(key, 1, 256), sub(mn, 0, 255), A.max)
        scan(a("MN", 257, 512), sub(RST, 0, 255), sub(w(3), 1, 256), A.add, A.min)
        if t: act(wb(15), key, F.Relu, scale=16.0, bias=-16.0 * (4096 + 1020))
        lowest(lb(4), lambda q: sub(w(8), 16 * q + 15, 16 * q + 16), cl, P(4, 1))
        kq = si(2, 32)
        ts(kq, m12, 256.0, A.mult); ts(kq, kq, 255, A.bitwise_and)
        ts(li("dU", 32), kq, 16.0, A.mult, pm, A.add); cp(li("kU", 32), kq)
        tt(sm("gb"), si(3), a3, A.add); ts(li("gb"), sm("gb"), 1.0 / 16, A.mult)
        d1, d2 = wb(2), wb(3)
        act(wb(10), ind(a("PQ", 0, wid(XT)), eU))
        act(wb(2, 2), ind(a("DD", 0, 4096), li("dU", 32)))
        act(wb(11), ind(a("GB", 512, 8704), li("gb")))
        act(zof(t, 2), d1, F.Abs)
        mms(acc(P(1, 16, 32), [(I128, z), (HALF, d1)]))
        act(wb(4), P(1, 16, 32), bias=191.75)
        if TAKE_ON_VECTOR: ts(zof(t, 3), wb(4), -192.0, A.add)
        else: act(zof(t, 3), wb(4), bias=-192.0)
        less = [(NEG, ab)]
        wsel(P(5, 0), 3, "WB", 256 * 10, 256, less); wsel(P(5, 1), 4, "WB", 256 * 10, 256, less)
        nx = sm("nx", 32); dx = sub(nx, 0, 16)
        ts(dx, P(5, 0), 0.0, A.is_equal); tt(dx, P(5, 1), dx, A.mult); tt(dx, P(5, 0), dx, A.add)
        if t: ts(sm("st"), e, 4096.0, A.is_ge, 1.0, A.add)
        clq, ed, tk = sm("clq"), sm("ed"), sm("tk") if t else sub(nx, 16, 32)
        tt(clq, cl, q16, A.add); tt(ed, e, dW, A.subtract)
        tt(tk, cl, P(4, 1), A.is_gt)
        tt(clq, clq, tk, A.add); ts(li("ix"), clq, 256.0, A.mult, pm, A.add)
        nw = 32 if t < S - 1 else 16
        tt(dx, dx, tk, A.mult)
        if 0 < t < S - 1: tt(sub(nx, 16, 32), sm("st"), tk, A.mult)
        tt(sub(base, 0, nw), sub(nx, 0, nw), sub(base, 0, nw), A.add); cp(a("BOXO", 32 * t, 32 * t + nw), sub(base, 0, nw))
        get(OUT_ON_VECTOR, a("OUT", 256 * t, 256 * t + 256), ind(a("MSG", MW * t + 256, MW * t + 1024), li("ix")))
        sent = (send("box", t + 1, a("BOXO", 32 * t, 32 * t + nw), blands(t + 1)), send("arr", t + 1, a("OUT", 256 * t, 256 * t + 256), zlands(t + 1)))
        mms(acc(P(0, 0, 16), [(I128, d1), (NEG, d2)]))
        act(wb(6), P(0, 0, 16), F.Abs)
        mms(acc(P(7, 0, 16), [(SA, wb(14)), (SE, wb(10)), (SF, wb(11))], True, False))
        mms([(P(7, 0, 16), Y(0, 4), wb(6), False, True)])
        act(wb(0), P(7, 0, 16), F.Relu, scale=2048.0, bias=col("jl") if t else col("lim0"))
        mms(acc(P(0, 16, 32), [(I128, z), (HALF, d1), (HALF, d2), (HALF, wb(6))]))
        act(wb(7), P(0, 16, 32))
        r12, rb, jn = sh("r12", 32), sh("rb"), sh("jn")
        tt(r12, m12, thr, A.is_lt)
        tt(rb, sub(r12, 0, 16), sub(r12, 16, 32), A.mult)
        if t: tt(rb, rb, sm("st"), A.is_ge)
        act(wb(8, 2), ind(LUT, li("kU", 32)))
        if t:
            tp(b("XD", (0, 16), (0, 16)), wb(15))
            mms([(P(6, 0, 16), NIL, KC, True, False)] + [(P(6, c, 16, 2), MT(2 * c + h), b("XD", (h, 16, 2), (0, 16)), False, False) for c in range(2) for h in range(2)])
            items = spread(6, 0, sub(r12, 0, 16)); items[-1] = items[-1][:4] + (True,)
            mms(items)
            act(w(4), by_box(a("VR", 0, 512)))
            tt(w(5), w(4), P(6, 0, 16), A.min)
        mms(acc(P(6, 16, 32), [(I128, wb(8)), (I128, wb(9))], True, False))
        mms(spread(6, 16, rb))
        mms(acc(P(6, 16, 32), [(NBLK, wb(0)), (I128, IDT)], False))
        act(w(6), P(6, 16, 32), F.Relu, bias=t + 1.0)
        wsel(P(5, 4), 0, "WB", 0, 256, [(IF, sw), (NEG, rb)])
        ts(jn, P(5, 4), -989.0, A.is_equal)
        if t: tt(ind(a("VR", 0, 768), li("vo")), w(5), w(6), A.max)
        else: cp(ind(a("VR", 0, 768), li("vo")), w(6))
        if t < S - 1:
            for h in range(2):
                mul(h in V2_ON_VECTOR, a("V2", 512 * h, 512 * h + 512), a("VR", 0, 512), col("vs%d" % h))
        up = sm("up", 64); u3, u0, u1, u2 = (sub(up, 16 * k, 16 * k + 16) for k in range(4))
        tt(ed, ed, tk, A.mult); tt(u0, ed, dW, A.add)
        nl = 4 if 0 < t < S - 2 else 2
        if nl == 4: tt(u1, u0, dW, A.min); tt(u2, u0, dW, A.max)
        act(sm("t4"), ab, bias=LONG + 256.0 + 512.0 * (t + 1))
        tt(sm("t4"), sm("t4"), jn, A.mult); tt(u3, sm("t4"), dW, A.max)
        cp(sub(li("up%d" % t, 64), 0, 16 * nl), sub(up, 0, 16 * nl))
        ts(sub(li("yl", 128), 16 * t, 16 * t + 16), sm("t4"), float(ZERO), A.max)
        if t < S - 1:
            mms(acc(P(7, 16, 32), [(ME, wb(10)), (MG, wb(11))]))
            act(wb(5), P(7, 16, 32))
            mms(acc(P(5, 5), [(BLK, jn)]))
            act(a("JK", 0, 16), P(5, 5), scale=8.0, acc=col("nj"))
            ts(si(6, 1), si(6, 1), col("nj"), A.add); ts(si(6, 1), si(6, 1), 255, A.bitwise_and)
            ts(col("jl"), si(6, 1), col("n4"), A.mult, col("lim0"), A.add)

    for lo in (0, 256):
        act(a("NB", lo, lo + 256), a("VR", lo, lo + 256))
        tt(a("NB", 512 + lo, 768 + lo), a("VR", lo, lo + 256), a("NB", lo, lo + 256), A.subtract)
    act(a("NB", 1024, 1536), a("VR", 0, 512), F.Sign)
    for f in range(3):
        dma("s", a("GB", 512, 8704, 1, (f, 128, 16)), a("NB", 512 * f, 512 * f + 512), 128)
    updates(S - 1)
    dma("s", T.yx[:, 0:4096], a("X", 0, 4096), 1024)
    yl = li("yl", 128)
    for h in range(2):
        get(4 + h in LAST_ON_VECTOR, a("DD", 1024 * h, 1024 * h + 1024), ind(XW, sub(yl, 64 * h, 64 * h + 64)))
    dma("s", T.yx[:, 4096:6144], a("DD", 0, 2048), 512)
    for c in range(4):
        get(c in LAST_ON_VECTOR, a("G1", 1024 * c, 1024 * c + 1024), ind(a("GB", 0, 8704), a("LB", 768 + 64 * c, 832 + 64 * c)))
        wsel(P(0, 4 * c, 4 * c + 4), 7, "G1", 1024 * c, 1024)
    arrival("arr", S, zlands(S), sent[1]); arrival("box", S, blands(S), sent[0])
    dma("a", T.yz[:], zof(S), 64)
    for h in range(2): cp(a("BXF", 16 * h, 16 * h + 16), blands(S)[0][0])
    flip(sm("b0"))
    dma("a", T.yb[:], sm("b0"), 8)
    act(nf(0), io5(0, 256), bias=c_(pm, 256.0, A.mult))
    tt(nf(1), P(0, 0, 16), nf(0), A.max)
    dma("s", T.yj[:], nf(1), 128)

    n = len(ops)
    hist = {}; turns = {}; lastp = {}
    deps = PLAN.get("deps", [])
    for i, o in enumerate(ops if not deps else ()):
        d = {}
        for kind, rs in (("r", o["r"]), ("w", o["w"])):
            for (nm, m, pt, lo) in rs:
                for (j, k2, m2, p2) in hist.get(nm, ()):
                    if m & m2 and pt & p2 and (kind == "w" or k2 == "w"):
                        d[j] = bool(ops[j]["e"] != o["e"] or o["e"] != "p")
        for kind, rs in (("w", o["w"]), ("r", o["r"])):
            for (nm, m, pt, lo) in rs:
                keep = hist.get(nm, [])
                if kind == "w": keep = [x for x in keep if x[2] & ~m or x[3] & ~pt]
                hist[nm] = keep + [(i, kind, m, pt)]
        for nm in set(x[0] for x in o["w"] + o["r"] if SCRATCH[x[0]][0] == "psum"):
            was, now = turns.get(nm, ([], []))
            if now and ops[now[0]]["e"] != o["e"]: was, now = now, []
            for j in was: d[j] = True
            turns[nm] = (was, now + [i])
            if o["e"] == "p":
                if nm in lastp: d.setdefault(lastp[nm], False)
                lastp[nm] = i
        d.pop(i, None)
        deps.append(d)
    pred = [dict(d) for d in deps]
    for i, o in enumerate(ops):
        if o["e"] == "x": pred[i][o["after"]] = True
    succ = [[] for _ in range(n)]
    for i in range(n):
        for j in pred[i]: succ[j].append(i)
    prio = [0.0] * n
    for i in range(n - 1, -1, -1):
        prio[i] = ops[i]["c"] + max([prio[k] + (ops[i]["lat"] if pred[k][i] else 0) for k in succ[i]] + [ops[i]["lat"] if ops[i]["dma"] else 0])
    tail = [ops[i]["lat"] if ops[i]["dma"] else 0 for i in range(n)]

    eng = [o["e"] for o in ops]; cost = [o["c"] for o in ops]; NEVER = 1e18

    def run(before, after, first, pr, peek):
        left = [len(p) for p in before]
        ready = list(first); fin = [0.0] * n
        free = {q: 0.0 for q in "vapgsx"}
        pool = {q: [] for q in "vapgsx"}
        for i in range(n):
            if not left[i]: pool[ops[i]["e"]].append(i)
        seq = []
        soon = {q: min([ready[i] for i in p], default=NEVER) for q, p in pool.items()}
        for _ in range(n):
            s0 = NEVER
            for q_, x in soon.items():
                if x < free[q_]: x = free[q_]
                if x < s0: s0 = x; q = q_
            p = pool[q]; s0 += peek; top = -NEVER
            for k in p:
                if ready[k] <= s0 and pr[k] > top: top = pr[k]; i = k
            p.remove(i); seq.append(i)
            soon[q] = min([ready[k] for k in p], default=NEVER)
            end = max(free[q], ready[i]) + cost[i]; free[q] = end; fin[i] = end
            for k, gp in after[i]:
                if end + gp > ready[k]: ready[k] = end + gp
                left[k] -= 1
                if not left[k]:
                    pool[eng[k]].append(k)
                    if ready[k] < soon[eng[k]]: soon[eng[k]] = ready[k]
        return seq, fin

    if "order" not in PLAN:
        span = {"MSG": MW, "OUT": 256, "BOX": 32, "BOXO": 32, "LOOK": 32}
        keys = ["%s%s%d" % (o["e"], o["w"][0][0], o["w"][0][3] % span.get(o["w"][0][0], 1 << 20)) if o["w"] else "send" for o in ops]
        keys = [k + ("." if i < marks[1] else "!" if i >= marks[S - 1] else "") for i, k in enumerate(keys)]
        pl = [list(p.items()) for p in pred]
        sets = [([o["c"] * (kp if o["e"] == "p" else 1) + o.get("g", 0) * kg + o.get("s", 0) * ks + o.get("fix", 0) * kf for o in ops],
                 [sy if o["lat"] == SYNC else wire if o["lat"] == WIRE else o["lat"] for o in ops], wt) for kg, ks, kp, sy, wt, kf, wire in SETTINGS]

        def score(seq):
            r = []
            for c, lat, wt in sets:
                fin = [0.0] * n; free = dict.fromkeys("vapgsx", 0.0); mx = 0.0
                for i in seq:
                    s_ = free[eng[i]]
                    for j, wait in pl[i]:
                        x = fin[j] + lat[j] if wait else fin[j]
                        if x > s_: s_ = x
                    s_ += c[i]; fin[i] = s_; free[eng[i]] = s_
                    if s_ + tail[i] > mx: mx = s_ + tail[i]
                r.append(mx)
            return sum(x * y[2] for x, y in zip(r, sets)), r
        ahead = [[(k, ops[i]["lat"] if pred[k][i] else 0) for k in succ[i]] for i in range(n)]
        forward = lambda pr: run(pred, ahead, [0.0] * n, pr, PEEK)
        seq, fin = forward(prio)
        base = run(succ, [[(k, ops[k]["lat"] if wait else 0) for k, wait in pred[i].items()] for i in range(n)], tail, fin, PEEK)[1]
        rng = np.random.default_rng(SEED)
        more = dict.fromkeys(keys, 0.0)
        seq = forward(base)[0]; best = score(seq) + (seq,)
        for _ in range(TRIES):
            i = int(rng.integers(n)); depth = int(rng.choice((0, 1, 2, 3, 5, 9))); step = float(rng.choice(MOVES)) * (1 if rng.random() < 0.5 else -1)
            near = {i}; edge = {i}
            for _d in range(depth):
                edge = set(j for k in edge for j in (pred[k] if step > 0 else succ[k]) if abs(j - i) < 200) - near
                near |= edge
            trial = dict(more)
            for k in set(keys[j] for j in near): trial[k] += step
            seq = forward([x + trial[k] for x, k in zip(base, keys)])[0]; got = score(seq)
            if got[0] <= best[0]: best = got + (seq,); more = trial
        seq = best[2]
        below = [0] * n; lean = [None] * n
        for i in range(n):
            far = 0
            for j in pred[i]: far |= below[j]
            lean[i] = [(j, wait) for j, wait in pl[i] if not far >> j & 1 or ops[j]["dma"]]
            for j in pred[i]: far |= 1 << j
            below[i] = far
        stepof = [sum(i >= m for m in marks) for i in range(n)]
        seen = {}; twin = {}; name = []
        for i in range(n):
            k = (keys[i].rstrip(".!"), stepof[i]); seen[k] = seen.get(k, 0) + 1
            name.append((k[0], seen[k])); twin[name[i], stepof[i]] = i
        qn = ["vapgsx".index(x) for x in eng]
        wts = [x[2] for x in sets]
        lean4 = [[(j,) + tuple(x[1][j] if wait else 0 for x in sets) for j, wait in lean[i]] for i in range(n)]
        cost4 = [tuple(x[0][i] for x in sets) for i in range(n)]

        def times(seq):
            f0 = [0.0] * n; f1 = [0.0] * n; f2 = [0.0] * n; f3 = [0.0] * n
            last = [n - 1] * 6
            for i in seq:
                q = qn[i]; p = last[q]; last[q] = i
                s0 = f0[p]; s1 = f1[p]; s2 = f2[p]; s3 = f3[p]
                for j, l0, l1, l2, l3 in lean4[i]:
                    x = f0[j] + l0
                    if x > s0: s0 = x
                    x = f1[j] + l1
                    if x > s1: s1 = x
                    x = f2[j] + l2
                    if x > s2: s2 = x
                    x = f3[j] + l3
                    if x > s3: s3 = x
                c = cost4[i]
                f0[i] = s0 + c[0]; f1[i] = s1 + c[1]; f2[i] = s2 + c[2]; f3[i] = s3 + c[3]
            fs = (f0, f1, f2, f3); r = [max(f[i] + tail[i] for i in ends) for f in fs]
            return sum(x * y for x, y in zip(r, wts)), r, fs

        def held_up(seq, fs):
            before = {}; last = {}
            for i in seq: before[i] = last.get(qn[i]); last[qn[i]] = i
            r = []
            for k, f in enumerate(fs):
                i = max(ends, key=lambda e: f[e] + tail[e])
                while i is not None:
                    s0 = f[i] - cost4[i][k] - 1e-6
                    up = [x[0] for x in lean4[i] if f[x[0]] + x[1 + k] >= s0]
                    if up: i = up[0]
                    elif before[i] is not None and f[before[i]] >= s0: r.append((i, before[i])); i = before[i]
                    else: i = None
            return r, before
        ends = [i for i in range(n) if not succ[i]]
        now = times(seq); pairs, before = held_up(seq, now[2]); best = (now[0], now[1], seq)
        for _ in range(PULLS):
            i, j = pairs[int(rng.integers(len(pairs)))]
            for _d in range(int(rng.choice((0, 0, 1, 2, 4, 8)))):
                if before[j] is not None and not below[i] >> before[j] & 1: j = before[j]
            new = list(seq)
            for d in range(-S, S + 1) if rng.random() < 0.7 else (0,):
                x, y = twin.get((name[i], stepof[i] + d)), twin.get((name[j], stepof[j] + d))
                if x is None or y is None or below[x] >> y & 1: continue
                lo, hi = new.index(y), new.index(x)
                if lo < hi:
                    part = new[lo:hi]; m = below[x]
                    new[lo:hi + 1] = [k for k in part if m >> k & 1] + [x] + [k for k in part if not m >> k & 1]
            got = times(new)
            if got[0] <= now[0] + SLACK * rng.random() * (1 - _ / PULLS):
                seq, now = new, got; pairs, before = held_up(seq, now[2])
                if now[0] < best[0]: best = (now[0], now[1], seq)
        PLAN["deps"], PLAN["order"], PLAN["span"] = deps, best[2], best[1]
        PLAN["ops"], PLAN["marks"], PLAN["pred"] = ops, marks, pred
    order = PLAN["order"]
    place = {i: k for k, i in enumerate(order)}
    clock = {}
    know = {q: ({}, set()) for q in "vapgsx"}
    need = {}
    marked = set()
    for i in order:
        o = ops[i]; kq, kd = know[o["e"]]; need[i] = []
        for j in sorted((j for j in deps[i] if deps[i][j]), key=lambda k: -place[k]):
            oj = ops[j]
            if oj["dma"]:
                if j in kd or oj["dma"] == "remote": continue
            elif kq.get(oj["e"], -1) >= place[j]: continue
            need[i].append(j); marked.add(j)
            cq, cd = clock[j]
            for q, v in cq.items():
                if kq.get(q, -1) < v: kq[q] = v
            kd |= cd
        cq = dict(kq); cd = set(kd)
        if o["dma"]: cd.add(i)
        else: cq[o["e"]] = place[i]
        clock[i] = (cq, cd)
    semof = {"v": "ev", "a": "ea", "p": "ep", "g": "eg"}
    queue = {"v": g.vector, "a": g.scalar, "p": g.tensor, "g": g, "s": g.sync}
    cnt = {q: 0 for q in semof}
    val = {}
    for i in order:
        o = ops[i]
        if o["e"] == "x": continue
        for j in need[i]:
            oj = ops[j]
            if oj["e"] == "x": queue[o["e"]].wait_ge(T.sem[oj["dma"]], expect[oj["dma"]])
            elif oj["dma"]: queue[o["e"]].wait_ge(T.sem[oj["dma"]], 16)
            else: queue[o["e"]].wait_ge(T.sem[semof[oj["e"]]], val[j])
        for fn in o["f"]: ins = fn()
        if o["dma"] == "remote": continue
        if o["dma"]: ins.then_inc(T.sem[o["dma"]], 16)
        elif i in marked:
            cnt[o["e"]] += 1; val[i] = cnt[o["e"]]
            ins.then_inc(T.sem[semof[o["e"]]], 1)
    for q, v in cnt.items():
        if v: g.wait_ge(T.sem[semof[q]], v)
    for k in range(ndma[0]):
        g.wait_ge(T.sem["d%d" % k], 16)
    for nm, v in expect.items():
        g.wait_ge(T.sem[nm], v)
    g.wait_ge(T.sem.sent, nen * (2 * S + 1))


ACT = 40
ROUND = 1.5 * 2 ** 23
ROUND_ON_VECTOR = False
PIECES = (0, 8, 16)
BANKS = ((0, 7, 1), (6, 5, 0))
X_ON_SCALAR = ((), (0, 1))
GB_ON_VECTOR = (6, 7)
LOW_ON_VECTOR = tuple(range(16))
SPREAD_ON_VECTOR = tuple(range(16))
DIGITS_ON_VECTOR = (1, 3, 5)
TAKE_ON_VECTOR = False
OUT_ON_VECTOR = False
V2_ON_VECTOR = (1,)
LAST_ON_VECTOR = (1, 3)
